import numpy as np
import ml_dtypes


def mxq(x, axis, fmt="e4m3"):
    dtype, down = {"e4m3": (ml_dtypes.float8_e4m3fn, 7), "e5m2": (ml_dtypes.float8_e5m2, 14)}[fmt]
    v = np.moveaxis(np.asarray(x, np.float32).astype(ml_dtypes.bfloat16).astype(np.float64), axis, -1)
    blocks = v.reshape(v.shape[:-1] + (-1, 32))
    amax = np.abs(blocks).max(-1, keepdims=True)
    byte = np.maximum(np.where(amax > 0, np.frexp(amax)[1] - 1 + 127, 0) - down, 1)
    scale = np.exp2(byte - 127.0)
    codes = (blocks / scale).astype(np.float32).astype(dtype).astype(np.float64)
    return np.moveaxis((codes * scale).reshape(v.shape), -1, axis)


WIDE = False


def mx_kscale(k):
    if not WIDE:
        return np.ones(k)
    levels = np.array([10, -10, 5, -5, 0])
    if k % 512:
        return np.exp2(np.random.permutation(np.resize(levels, k // 32))).repeat(32)
    a = np.empty((k // 512, 16))
    for p in range(k // 512):
        a[p, :8] = np.random.permutation(np.resize(levels, 8))
        for g in range(8):
            far = levels[np.abs(levels - a[p, g]) >= 10]
            a[p, g + 8] = far[np.random.randint(len(far))]
    return np.exp2(a.ravel()).repeat(32)


def f64(x):
    return np.asarray(x).astype(np.float64)


def striped(idx):
    return np.tile(idx.reshape(-1, 16).T, (8, 1)).astype(np.uint16)


def unstriped(offs):
    return offs[:16].T.reshape(-1).astype(np.int64)


E2M1 = np.array([0.0, 0.5, 1.0, 1.5, 2.0, 3.0, 4.0, 6.0, -0.0, -0.5, -1.0, -1.5, -2.0, -3.0, -4.0, -6.0])


def pack_weight(w, fmt):
    k, n = w.shape
    w = f64(np.asarray(w, np.float32).astype(ml_dtypes.bfloat16)).reshape(k // 32, 32, n)
    amax = np.abs(w).max(1)
    if fmt == "e4m3":
        byte = np.frexp(amax)[1] - 1 + 127 - 7
    else:
        mant, ex = np.frexp(amax / 6.0)
        byte = np.where(mant > 0.5, ex, ex - 1) + 127
    byte = np.clip(np.where(amax > 0, byte, 1), 1, 254)
    scaled = (w * np.exp2(127.0 - byte)[:, None, :]).reshape(k, n).astype(np.float32)
    by_word = np.ascontiguousarray(scaled.reshape(k // 512, 128, 4, n).transpose(0, 1, 3, 2))
    if fmt == "e4m3":
        words = by_word.astype(ml_dtypes.float8_e4m3fn).view(np.uint8)
    else:
        c = by_word.astype(ml_dtypes.float4_e2m1fn).view(np.uint8) & 0xF
        words = (c[..., 0::2] | (c[..., 1::2] << 4)).reshape(k // 512, 128, 2 * n)
    return np.ascontiguousarray(words), np.ascontiguousarray(byte.astype(np.uint8).reshape(k // 512, 16, n))


def unpack_weight(words, scales, fmt):
    g, _, n = scales.shape
    words = np.ascontiguousarray(words).reshape(g, 128, n, -1)
    if fmt == "e4m3":
        vals = words.view(ml_dtypes.float8_e4m3fn).astype(np.float64)
    else:
        nib = np.empty((g, 128, n, 4), np.uint8)
        nib[..., 0::2] = words & 0xF
        nib[..., 1::2] = words >> 4
        vals = E2M1[nib]
    vals = vals * np.repeat(np.exp2(scales.astype(np.float64) - 127.0), 8, axis=1)[..., None]
    return vals.transpose(0, 1, 3, 2).reshape(g * 512, n)


def gelu(v):
    return 0.5 * v * (1.0 + np.tanh(np.sqrt(2.0 / np.pi) * (v + 0.044715 * v**3)))


def bf(x):
    return np.asarray(x, np.float32).astype(ml_dtypes.bfloat16)


def planes(Y):
    n, m = Y.shape
    b = f64(bf(Y)).reshape(n // 32, 32, m)
    amax = np.abs(b).max(1)
    byte = np.clip(np.where(amax > 0, np.frexp(amax)[1] - 1 + 127 - 7, 1), 1, 254)
    codes = (b * np.exp2(127.0 - byte)[:, None, :]).reshape(n, m).astype(np.float32).astype(ml_dtypes.float8_e4m3fn).view(np.uint8)
    words = codes.reshape(n // 512, 128, 4, m).transpose(0, 1, 3, 2)
    return np.ascontiguousarray(words), np.ascontiguousarray(byte.astype(np.uint8).reshape(n // 512, 16, m))


K, K2, T, S, T2, H, N = 1024, 512, 2048, 1024, 2048, 512, 512


def setup_inputs():
    n = np.random.standard_normal
    s = mx_kscale(K)[:, None]
    s2 = mx_kscale(K2)[:, None]
    u = mx_kscale(H)[:, None]
    tab_words, tab_scales = pack_weight(n((K, T)) * s, "e4m3")
    tab2_words, tab2_scales = pack_weight(n((K2, T)) * s2, "e4m3")
    w1_words, w1_scales = pack_weight(n((K, H)) / np.sqrt(K) / s * u.T, "e2m1")
    w4_words, w4_scales = pack_weight(n((H, N)) / np.sqrt(H) * np.exp(0.8 * n(N)) / u, "e4m3")
    perm = np.random.permutation(T2)
    return {
        "tab_words": tab_words, "tab_scales": tab_scales,
        "tab2_words": tab2_words, "tab2_scales": tab2_scales,
        "offs": striped(np.random.permutation(T)[:S]),
        "offs2": striped(np.random.permutation(T)[:S]),
        "offs3": striped(perm[:S]), "offs4": striped(perm[S:]),
        "w1_words": w1_words, "w1_scales": w1_scales,
        "w2": (n((K, H)) / np.sqrt(K) / s).astype(np.float32),
        "w3": (n((K2, H)) / np.sqrt(K2) / s2 * u.T).astype(np.float32),
        "w4_words": w4_words, "w4_scales": w4_scales,
        "level": np.random.uniform(0.3, 1.0, H).astype(np.float32),
        "prev": (n((H, S)) * u).astype(np.float32),
        "wg1": np.exp(0.3 * n((128, S))).astype(np.float32),
        "wg2": np.exp(0.3 * n((128, S))).astype(np.float32),
    }


def reference(tab_words, tab_scales, tab2_words, tab2_scales, offs, offs2, offs3, offs4, w1_words, w1_scales, w2, w3, w4_words, w4_scales, level, prev, wg1, wg2):
    v = unpack_weight(tab_words, tab_scales, "e4m3")[:, unstriped(offs)]
    v2 = unpack_weight(tab2_words, tab2_scales, "e4m3")[:, unstriped(offs2)]
    a = unpack_weight(w1_words, w1_scales, "e2m1").T @ v
    b = mxq(f64(w2), 0, "e4m3").T @ v
    q = b * b
    h1 = a * (q / (q + f64(level)[:, None]))
    h2 = (mxq(f64(w3), 0, "e4m3").T @ v2) + f64(prev)
    page = np.zeros((H, T2))
    page[:, unstriped(offs3)] = np.tile(f64(wg1), (H // 128, 1)) * h1
    page[:, unstriped(offs4)] = np.tile(f64(wg2), (H // 128, 1)) * h2
    z = np.maximum(page, 0.0)
    y = unpack_weight(w4_words, w4_scales, "e4m3").T @ mxq(z, 0, "e4m3")
    words, scales = planes(y)
    return y, words, scales

@@ -1,0 +1,288 @@
+from contextlib import ExitStack
+
+import concourse.mybir as mybir
+
+K, K2, T, S, T2, H, N = 1024, 512, 2048, 1024, 2048, 512, 512
+FLOPS = 2 * S * H * (2 * K + K2) + 2 * T2 * H * N
+
+F32 = mybir.dt.float32
+BF16 = mybir.dt.bfloat16
+I32 = mybir.dt.int32
+U32 = mybir.dt.uint32
+U16 = mybir.dt.uint16
+U8 = mybir.dt.uint8
+FP8X4 = mybir.dt.float8_e4m3fn_x4
+FP4X4 = mybir.dt.float4_e2m1fn_x4
+ALU = mybir.AluOpType
+ACT = mybir.ActivationFunctionType
+
+P = 128
+PACK = 4
+BANK = 512
+TINY = 2.0 ** -63
+CHUNKS = (256, 512, 512, 512, 256)
+
+
+def tile_list_woven_tile_denoise_kernel(
+    tc, tab_words, tab_scales, tab2_words, tab2_scales, offs, offs2, offs3, offs4,
+    w1_words, w1_scales, w2, w3, w4_words, w4_scales, level, prev, wg1, wg2,
+    out_0, out_1, out_2,
+):
+    nc = tc.nc
+    with ExitStack() as ctx:
+        lists = ctx.enter_context(tc.tile_pool(name="lists", bufs=1))
+        keep = ctx.enter_context(tc.tile_pool(name="keep", bufs=1))
+        psum = ctx.enter_context(tc.psum_pool(name="psum", bufs=1))
+
+        def tile(name, shape, dtype, tag=None):
+            return keep.tile(shape, dtype, name=name, tag=tag or name, align_bytes=64)
+
+        def bank(name, index):
+            return psum.tile([P, BANK], F32, name=name, tag="bank%d" % index)
+
+        def load_list(name, source):
+            held = lists.tile([P, S // 16], U16, name=name)
+            nc.sync.dma_start(held[:], source)
+            return held
+
+        def load_words(name, source, tag=None):
+            held = tile(name, [P, source.shape[1]], I32, tag)
+            nc.sync.dma_start(held[:], source.rearrange("p c i -> p (c i)").bitcast(I32))
+            return held
+
+        def zeroed_plane(name, width):
+            plane = tile(name, [P, width], U8)
+            nc.gpsimd.memset(plane[:].bitcast(I32), 0)
+            return plane
+
+        def gather(name, window, offsets, dtype):
+            picked = tile(name, [P, S], dtype)
+            nc.vector.tensor_copy(picked[:], window.indirect(offsets[:]))
+            return picked
+
+        def load_weight(name, rows, tag):
+            raw = tile(name, [P, PACK, H], F32, tag)
+            nc.sync.dma_start(raw[:], rows.rearrange("(p i) c -> p i c", i=PACK))
+            return raw
+
+        def quantise_weight(name, raw, tag):
+            woven = tile(name + "_bf", [P, H * PACK], BF16, tag)
+            nc.scalar.copy(
+                woven[:].rearrange("p (t m i) -> p m t i", t=PACK, i=PACK),
+                raw[:].rearrange("p i (m t) -> p m t i", t=PACK),
+            )
+            codes = tile(name + "_codes", [P, H], U32)
+            scales = tile(name + "_scales", [P, H], U8)
+            nc.vector.quantize_mx(out=codes[:].bitcast(FP8X4), scales=scales[:], in_=woven[:])
+            return codes, scales
+
+        def load_gain(name, source, tag):
+            held = tile(name, [P, PACK, S], F32, tag)
+            rows = source.rearrange("(m t) j -> m t j", t=PACK)
+            for q in (0, 2, 1, 3):
+                nc.gpsimd.dma_start(held[32 * q : 32 * q + 32, :, :], rows)
+            return held
+
+        tab2_plane = zeroed_plane("tab2_plane", T)
+        tab_plane = zeroed_plane("tab_plane", T)
+        w1_plane = zeroed_plane("w1_plane", 2 * H)
+        w4_plane = zeroed_plane("w4_plane", N)
+        v_scales_1 = zeroed_plane("v_scales_1", S)
+
+        list2 = load_list("list2", offs2)
+        tab2_w = load_words("tab2_w", tab2_words[0], "slot3")
+        for q in range(4):
+            nc.scalar.dma_start(tab2_plane[32 * q : 32 * q + 4, :].bitcast(I32),
+                                tab2_scales[0, 4 * q : 4 * q + 4, :].bitcast(I32))
+        w3_raw = load_weight("w3_raw", w3, "slot0")
+        list1 = load_list("list1", offs)
+        tab_w = [load_words("tab_w%d" % a, tab_words[a]) for a in range(2)]
+        for q in range(4):
+            nc.scalar.dma_start(tab_plane[32 * q : 32 * q + 8, :].bitcast(I32),
+                                tab_scales[:, 4 * q : 4 * q + 4, :].bitcast(I32))
+        list4 = load_list("list4", offs4)
+        list3 = load_list("list3", offs3)
+        prev_rows = prev.rearrange("(p t) j -> p t j", t=PACK)
+        h2 = [tile("h2_%d" % t, [P, S], F32) for t in range(PACK)]
+        nc.sync.dma_start(h2[0][:], prev_rows[:, 0, :])
+        w2_raw = [load_weight("w2_raw%d" % a, w2[512 * a : 512 * (a + 1), :], "slot%d" % (1 + a)) for a in range(2)]
+        level_t = tile("level_t", [P, PACK], F32)
+        nc.scalar.dma_start(level_t[:], level.rearrange("(p t) -> p t", t=PACK))
+        nc.sync.dma_start(h2[1][:], prev_rows[:, 1, :])
+        w1_raw = tile("w1_raw", [P, 2, 2 * H], U8)
+        nc.sync.dma_start(w1_raw[:].bitcast(I32), w1_words.rearrange("a p c -> p a c").bitcast(I32))
+        for q in range(4):
+            nc.sync.dma_start(
+                w1_plane[32 * q : 32 * q + 4, :].rearrange("p (a c) -> p a c", a=2).bitcast(I32),
+                w1_scales[:, 4 * q : 4 * q + 4, :].rearrange("a r c -> r a c").bitcast(I32))
+        nc.sync.dma_start(h2[2][:], prev_rows[:, 2, :])
+        nc.sync.dma_start(h2[3][:], prev_rows[:, 3, :])
+        w4_raw = load_words("w4_raw", w4_words[0])
+        for q in range(4):
+            nc.sync.dma_start(w4_plane[32 * q : 32 * q + 4, :].bitcast(I32),
+                              w4_scales[0, 4 * q : 4 * q + 4, :].bitcast(I32))
+
+        v2_words = gather("v2_words", tab2_w[:].bitcast(U32), list2, U32)
+        v2_scales = gather("v2_scales", tab2_plane[:], list2, U8)
+        gain2 = load_gain("gain2", wg2, "slot3")
+        w3_codes, w3_scales = quantise_weight("w3", w3_raw, "woven0")
+        v_words = [gather("v_words%d" % a, tab_w[a][:].bitcast(U32), list1, U32) for a in range(2)]
+        v_scales = gather("v_scales", tab_plane[:], list1, U8)
+        nc.sync.dma_start(v_scales_1[0:112, :].bitcast(I32), v_scales[4:116, :].bitcast(I32))
+
+        neg_log_level = tile("neg_log_level", [P, PACK], F32)
+        log_level = tile("log_level", [P, PACK], F32)
+        nc.scalar.activation(log_level[:], level_t[:], ACT.Ln)
+        nc.scalar.mul(neg_log_level[:], log_level[:], -1.0)
+
+        page = [tile("page%d" % t, [P, T2], F32) for t in range(PACK)]
+        halves = [slice(BANK * u, BANK * (u + 1)) for u in range(S // BANK)]
+
+        def second_stream(t):
+            rows = slice(P * t, P * (t + 1))
+            for u, cols in enumerate(halves):
+                acc = bank("c_%d_%d" % (t, u), (2 * t + u) % 4)
+                nc.tensor.matmul_mx(out=acc[:], lhsT=w3_codes[:, rows].bitcast(FP8X4), lhsT_scale=w3_scales[:, rows],
+                                    rhs=v2_words[:, cols].bitcast(FP8X4), rhs_scale=v2_scales[:, cols],
+                                    start=True, stop=True)
+                nc.vector.tensor_tensor(h2[t][:, cols], acc[:], h2[t][:, cols], ALU.add)
+
+        def place_second(t):
+            nc.vector.tensor_tensor(page[t][:].indirect(list4[:]), h2[t][:], gain2[:, t, :], ALU.mult)
+
+        second_stream(0)
+        second_stream(1)
+        place_second(0)
+
+        w2_q = [quantise_weight("w2_%d" % a, w2_raw[a], "woven%d" % (1 + a)) for a in range(2)]
+        gain1 = load_gain("gain1", wg1, "slot1")
+
+        h1 = [tile("h1_%d" % t, [P, S], F32) for t in range(PACK)]
+        for t in range(PACK):
+            rows = slice(P * t, P * (t + 1))
+            for u, cols in enumerate(halves):
+                acc = bank("b_%d_%d" % (t, u), 4 + (2 * t + u) % 4)
+                for a in range(2):
+                    nc.tensor.matmul_mx(out=acc[:], lhsT=w2_q[a][0][:, rows].bitcast(FP8X4), lhsT_scale=w2_q[a][1][:, rows],
+                                        rhs=v_words[a][:, cols].bitcast(FP8X4), rhs_scale=v_scales[4 * a : P, cols],
+                                        start=(a == 0), stop=(a == 1))
+                nc.scalar.activation(h1[t][:, cols], acc[:], ACT.Abs)
+            nc.scalar.activation(h1[t][:], h1[t][:], ACT.Ln, bias=TINY)
+        for t in range(PACK):
+            nc.scalar.activation(h1[t][:], h1[t][:], ACT.Sigmoid, bias=neg_log_level[:, t : t + 1], scale=2.0)
+
+        second_stream(2)
+        place_second(1)
+
+        w1_dealt = tile("w1_dealt", [P, 2, 2 * H], U8)
+        nc.vector.tensor_copy(
+            w1_dealt[:].rearrange("p a (t m b) -> p a t m b", t=PACK, b=2),
+            w1_raw[:].rearrange("p a (m t b) -> p a t m b", t=PACK, b=2))
+        w1_dealt_scales = tile("w1_dealt_scales", [P, 2 * H], U8)
+        nc.vector.tensor_copy(
+            w1_dealt_scales[:].rearrange("p (a t m) -> p a t m", a=2, t=PACK),
+            w1_plane[:].rearrange("p (a m t) -> p a t m", a=2, t=PACK))
+        w4_dealt = tile("w4_dealt", [P, N], I32)
+        nc.vector.tensor_copy(
+            w4_dealt[:].rearrange("p (t m) -> p t m", t=PACK),
+            w4_raw[:].rearrange("p (m t) -> p t m", t=PACK))
+        w4_dealt_scales = tile("w4_dealt_scales", [P, N], U8)
+        nc.vector.tensor_copy(
+            w4_dealt_scales[:].rearrange("p (t m) -> p t m", t=PACK),
+            w4_plane[:].rearrange("p (m t) -> p t m", t=PACK))
+
+        second_stream(3)
+        place_second(2)
+
+        z_woven = tile("z_woven", [P, T2, PACK], BF16)
+
+        def first_stream(t):
+            for u, cols in enumerate(halves):
+                acc = bank("a_%d_%d" % (t, u), (2 * t + u) % 4)
+                for a in range(2):
+                    nc.tensor.matmul_mx(
+                        out=acc[:], lhsT=w1_dealt[:, a, 2 * P * t : 2 * P * (t + 1)].bitcast(FP4X4),
+                        lhsT_scale=w1_dealt_scales[:, H * a + P * t : H * a + P * (t + 1)],
+                        rhs=v_words[a][:, cols].bitcast(FP8X4),
+                        rhs_scale=(v_scales, v_scales_1)[a][:, cols],
+                        start=(a == 0), stop=(a == 1))
+                nc.vector.tensor_tensor(h1[t][:, cols], acc[:], h1[t][:, cols], ALU.mult)
+
+        def place_first(t):
+            nc.vector.tensor_tensor(page[t][:].indirect(list3[:]), h1[t][:], gain1[:, t, :], ALU.mult)
+
+        first_stream(0)
+        place_second(3)
+        for t in range(PACK - 1):
+            first_stream(t + 1)
+            place_first(t)
+            if t < PACK - 2:
+                nc.scalar.activation(z_woven[:, :, t], page[t][:], ACT.Relu)
+            else:
+                nc.scalar.activation(z_woven[:, :, t : t + 2], page[t][:].unsqueeze(2).to_broadcast([P, T2, 2]), ACT.Relu)
+        place_first(PACK - 1)
+
+        z_codes = tile("z_codes", [P, T2], U32)
+        z_scales = tile("z_scales", [P, T2], U8)
+        y_codes = tile("y_codes", [P, T2], I32)
+        y_scales = tile("y_scales", [P, T2], U8)
+        out_rows = out_0.rearrange("(p t) m -> p t m", t=PACK)
+        out_words = out_1[0].rearrange("p m i -> p (m i)").bitcast(I32)
+        starts = [sum(CHUNKS[:c]) for c in range(len(CHUNKS))]
+        y_tiles = {}
+
+        def make_z(c):
+            cols = slice(starts[c], starts[c] + CHUNKS[c])
+            if c == len(CHUNKS) - 2:
+                nc.scalar.activation(z_woven[:, cols, PACK - 1], page[PACK - 1][:, cols], ACT.Relu)
+            else:
+                nc.vector.tensor_scalar_max(z_woven[:, cols, PACK - 1], page[PACK - 1][:, cols], 0.0)
+
+        def quantise_z(c):
+            cols = slice(starts[c], starts[c] + CHUNKS[c])
+            nc.vector.quantize_mx(out=z_codes[:, cols].bitcast(FP8X4), scales=z_scales[:, cols],
+                                  in_=z_woven[:, cols, :].rearrange("p m t -> p (m t)"))
+
+        def multiply(c):
+            width = CHUNKS[c]
+            cols = slice(starts[c], starts[c] + width)
+            y = tile("y%d" % c, [P, PACK, width], F32, "slot%d" % ((c + 1) % 4))
+            for t in range(PACK):
+                rows = slice(P * t, P * (t + 1))
+                acc = bank("y_%d_%d" % (c, t), (4 * c + t) % 8)
+                nc.tensor.matmul_mx(out=acc[:, :width], lhsT=w4_dealt[:, rows].bitcast(FP8X4), lhsT_scale=w4_dealt_scales[:, rows],
+                                    rhs=z_codes[:, cols].bitcast(FP8X4), rhs_scale=z_scales[:, cols],
+                                    start=True, stop=True)
+                nc.scalar.copy(y[:, t, :], acc[:, :width])
+            nc.sync.dma_start(out_rows[:, :, cols], y[:])
+            y_tiles[c] = y
+
+        def weave_y(c):
+            width = CHUNKS[c]
+            woven = tile("y_woven%d" % c, [P, width * PACK], BF16, "woven%d" % (c % 3))
+            nc.vector.tensor_copy(
+                woven[:].rearrange("p (m i t) -> p m t i", i=4, t=PACK),
+                y_tiles[c][:].rearrange("p t (m i) -> p m t i", i=4))
+            return woven
+
+        def quantise_y(c, woven):
+            cols = slice(starts[c], starts[c] + CHUNKS[c])
+            nc.vector.quantize_mx(out=y_codes[:, cols].bitcast(FP8X4), scales=y_scales[:, cols], in_=woven[:])
+            nc.sync.dma_start(out_words[:, cols], y_codes[:, cols])
+
+        count = len(CHUNKS)
+        make_z(count - 2)
+        make_z(0)
+        woven = {}
+        for c in range(count + 2):
+            if c + 1 < count and c + 1 != count - 2:
+                make_z(c + 1)
+            if c < count:
+                quantise_z(c)
+                multiply(c)
+            if 1 <= c <= count:
+                woven[c - 1] = weave_y(c - 1)
+            if c >= 2:
+                quantise_y(c - 2, woven[c - 2])
+        for q in range(4):
+            nc.sync.dma_start(out_2[0, 4 * q : 4 * q + 4, :].bitcast(I32), y_scales[32 * q : 32 * q + 4, :].bitcast(I32))

@@ -55,8 +55,8 @@ def tile_list_woven_tile_denoise_kernel(
             nc.gpsimd.memset(plane[:].bitcast(I32), 0)
             return plane
 
-        def gather(name, window, offsets, dtype):
-            picked = tile(name, [P, S], dtype)
+        def gather(name, window, offsets, dtype, tag=None):
+            picked = tile(name, [P, S], dtype, tag)
             nc.vector.tensor_copy(picked[:], window.indirect(offsets[:]))
             return picked
 
@@ -65,23 +65,23 @@ def tile_list_woven_tile_denoise_kernel(
             nc.sync.dma_start(raw[:], rows.rearrange("(p i) c -> p i c", i=PACK))
             return raw
 
-        def quantise_weight(name, raw, tag):
+        def quantise_weight(name, raw, tag, codes_tag=None):
             woven = tile(name + "_bf", [P, H * PACK], BF16, tag)
             nc.scalar.copy(
                 woven[:].rearrange("p (t m i) -> p m t i", t=PACK, i=PACK),
                 raw[:].rearrange("p i (m t) -> p m t i", t=PACK),
             )
-            codes = tile(name + "_codes", [P, H], U32)
+            codes = tile(name + "_codes", [P, H], U32, codes_tag)
             scales = tile(name + "_scales", [P, H], U8)
             nc.vector.quantize_mx(out=codes[:].bitcast(FP8X4), scales=scales[:], in_=woven[:])
             return codes, scales
 
-        def load_gain(name, source, tag):
-            held = tile(name, [P, PACK, S], F32, tag)
-            rows = source.rearrange("(m t) j -> m t j", t=PACK)
+        def load_gain(name, source, first, last):
+            held = tile(name, [P, last - first, S], F32)
+            rows = source.rearrange("(m t) j -> m t j", t=PACK)[:, first:last, :]
             for q in (0, 2, 1, 3):
-                nc.gpsimd.dma_start(held[32 * q : 32 * q + 32, :, :], rows)
-            return held
+                nc.sync.dma_start(held[32 * q : 32 * q + 32, :, :], rows)
+            return [held[:, t, :] for t in range(last - first)]
 
         tab2_plane = zeroed_plane("tab2_plane", T)
         tab_plane = zeroed_plane("tab_plane", T)
@@ -90,25 +90,27 @@ def tile_list_woven_tile_denoise_kernel(
         v_scales_1 = zeroed_plane("v_scales_1", S)
 
         list2 = load_list("list2", offs2)
-        tab2_w = load_words("tab2_w", tab2_words[0], "slot3")
+        tab2_w = load_words("tab2_w", tab2_words[0])
         for q in range(4):
             nc.scalar.dma_start(tab2_plane[32 * q : 32 * q + 4, :].bitcast(I32),
                                 tab2_scales[0, 4 * q : 4 * q + 4, :].bitcast(I32))
+        level_t = tile("level_t", [P, PACK], F32)
+        nc.scalar.dma_start(level_t[:], level.rearrange("(p t) -> p t", t=PACK))
         w3_raw = load_weight("w3_raw", w3, "slot0")
-        list1 = load_list("list1", offs)
-        tab_w = [load_words("tab_w%d" % a, tab_words[a]) for a in range(2)]
-        for q in range(4):
-            nc.scalar.dma_start(tab_plane[32 * q : 32 * q + 8, :].bitcast(I32),
-                                tab_scales[:, 4 * q : 4 * q + 4, :].bitcast(I32))
-        list4 = load_list("list4", offs4)
-        list3 = load_list("list3", offs3)
         prev_rows = prev.rearrange("(p t) j -> p t j", t=PACK)
         h2 = [tile("h2_%d" % t, [P, S], F32) for t in range(PACK)]
         nc.sync.dma_start(h2[0][:], prev_rows[:, 0, :])
-        w2_raw = [load_weight("w2_raw%d" % a, w2[512 * a : 512 * (a + 1), :], "slot%d" % (1 + a)) for a in range(2)]
-        level_t = tile("level_t", [P, PACK], F32)
-        nc.scalar.dma_start(level_t[:], level.rearrange("(p t) -> p t", t=PACK))
+        list4 = load_list("list4", offs4)
+        gain2 = load_gain("gain2_0", wg2, 0, 1)
         nc.sync.dma_start(h2[1][:], prev_rows[:, 1, :])
+        list1 = load_list("list1", offs)
+        tab_w = [load_words("tab_w%d" % a, tab_words[a]) for a in range(2)]
+        for q in range(4):
+            nc.gpsimd.dma_start(tab_plane[32 * q : 32 * q + 8, :].bitcast(I32),
+                                tab_scales[:, 4 * q : 4 * q + 4, :].bitcast(I32))
+        w2_raw = [load_weight("w2_raw%d" % a, w2[512 * a : 512 * (a + 1), :], "slot%d" % (1 + a)) for a in range(2)]
+        gain2.extend(load_gain("gain2_1", wg2, 1, 4))
+        list3 = load_list("list3", offs3)
         w1_raw = tile("w1_raw", [P, 2, 2 * H], U8)
         nc.sync.dma_start(w1_raw[:].bitcast(I32), w1_words.rearrange("a p c -> p a c").bitcast(I32))
         for q in range(4):
@@ -116,18 +118,39 @@ def tile_list_woven_tile_denoise_kernel(
                 w1_plane[32 * q : 32 * q + 4, :].rearrange("p (a c) -> p a c", a=2).bitcast(I32),
                 w1_scales[:, 4 * q : 4 * q + 4, :].rearrange("a r c -> r a c").bitcast(I32))
         nc.sync.dma_start(h2[2][:], prev_rows[:, 2, :])
-        nc.sync.dma_start(h2[3][:], prev_rows[:, 3, :])
+        gain1 = load_gain("gain1_0", wg1, 0, 2)
         w4_raw = load_words("w4_raw", w4_words[0])
         for q in range(4):
             nc.sync.dma_start(w4_plane[32 * q : 32 * q + 4, :].bitcast(I32),
                               w4_scales[0, 4 * q : 4 * q + 4, :].bitcast(I32))
+        nc.sync.dma_start(h2[3][:], prev_rows[:, 3, :])
+        gain1.extend(load_gain("gain1_1", wg1, 2, 4))
 
         v2_words = gather("v2_words", tab2_w[:].bitcast(U32), list2, U32)
         v2_scales = gather("v2_scales", tab2_plane[:], list2, U8)
-        gain2 = load_gain("gain2", wg2, "slot3")
         w3_codes, w3_scales = quantise_weight("w3", w3_raw, "woven0")
-        v_words = [gather("v_words%d" % a, tab_w[a][:].bitcast(U32), list1, U32) for a in range(2)]
-        v_scales = gather("v_scales", tab_plane[:], list1, U8)
+        page = {}
+        halves = [slice(BANK * u, BANK * (u + 1)) for u in range(S // BANK)]
+
+        def second_stream(t):
+            rows = slice(P * t, P * (t + 1))
+            for u, cols in enumerate(halves):
+                acc = bank("c_%d_%d" % (t, u), (0, 2, 2, 0)[t] + u)
+                nc.tensor.matmul_mx(out=acc[:], lhsT=w3_codes[:, rows].bitcast(FP8X4), lhsT_scale=w3_scales[:, rows],
+                                    rhs=v2_words[:, cols].bitcast(FP8X4), rhs_scale=v2_scales[:, cols],
+                                    start=True, stop=True)
+                nc.vector.tensor_tensor(h2[t][:, cols], acc[:], h2[t][:, cols], ALU.add)
+
+        def place_second(t):
+            page[t] = tile("page%d" % t, [P, T2], F32)
+            nc.vector.tensor_tensor(page[t][:].indirect(list4[:]), h2[t][:], gain2[t], ALU.mult)
+
+
+        second_stream(0)
+        second_stream(1)
+        place_second(0)
+        v_words = [gather("v_words%d" % a, tab_w[a][:].bitcast(U32), list1, U32, ("h2_0", "tab_w0")[a]) for a in range(2)]
+        v_scales = gather("v_scales", tab_plane[:], list1, U8, "tab_w1")
         nc.sync.dma_start(v_scales_1[0:112, :].bitcast(I32), v_scales[4:116, :].bitcast(I32))
 
         neg_log_level = tile("neg_log_level", [P, PACK], F32)
@@ -135,33 +158,13 @@ def tile_list_woven_tile_denoise_kernel(
         nc.scalar.activation(log_level[:], level_t[:], ACT.Ln)
         nc.scalar.mul(neg_log_level[:], log_level[:], -1.0)
 
-        page = [tile("page%d" % t, [P, T2], F32) for t in range(PACK)]
-        halves = [slice(BANK * u, BANK * (u + 1)) for u in range(S // BANK)]
-
-        def second_stream(t):
-            rows = slice(P * t, P * (t + 1))
-            for u, cols in enumerate(halves):
-                acc = bank("c_%d_%d" % (t, u), (2 * t + u) % 4)
-                nc.tensor.matmul_mx(out=acc[:], lhsT=w3_codes[:, rows].bitcast(FP8X4), lhsT_scale=w3_scales[:, rows],
-                                    rhs=v2_words[:, cols].bitcast(FP8X4), rhs_scale=v2_scales[:, cols],
-                                    start=True, stop=True)
-                nc.vector.tensor_tensor(h2[t][:, cols], acc[:], h2[t][:, cols], ALU.add)
-
-        def place_second(t):
-            nc.vector.tensor_tensor(page[t][:].indirect(list4[:]), h2[t][:], gain2[:, t, :], ALU.mult)
-
-        second_stream(0)
-        second_stream(1)
-        place_second(0)
-
-        w2_q = [quantise_weight("w2_%d" % a, w2_raw[a], "woven%d" % (1 + a)) for a in range(2)]
-        gain1 = load_gain("gain1", wg1, "slot1")
+        w2_q = [quantise_weight("w2_%d" % a, w2_raw[a], ("woven1", "page1")[a], ("tab_plane", None)[a]) for a in range(2)]
 
         h1 = [tile("h1_%d" % t, [P, S], F32) for t in range(PACK)]
         for t in range(PACK):
             rows = slice(P * t, P * (t + 1))
             for u, cols in enumerate(halves):
-                acc = bank("b_%d_%d" % (t, u), 4 + (2 * t + u) % 4)
+                acc = bank("b_%d_%d" % (t, u), 2 * t + u)
                 for a in range(2):
                     nc.tensor.matmul_mx(out=acc[:], lhsT=w2_q[a][0][:, rows].bitcast(FP8X4), lhsT_scale=w2_q[a][1][:, rows],
                                         rhs=v_words[a][:, cols].bitcast(FP8X4), rhs_scale=v_scales[4 * a : P, cols],
@@ -171,34 +174,23 @@ def tile_list_woven_tile_denoise_kernel(
         for t in range(PACK):
             nc.scalar.activation(h1[t][:], h1[t][:], ACT.Sigmoid, bias=neg_log_level[:, t : t + 1], scale=2.0)
 
-        second_stream(2)
         place_second(1)
+        second_stream(2)
 
-        w1_dealt = tile("w1_dealt", [P, 2, 2 * H], U8)
+        w1_dealt = tile("w1_dealt", [P, 2, 2 * H], U8, "woven1")
         nc.vector.tensor_copy(
-            w1_dealt[:].rearrange("p a (t m b) -> p a t m b", t=PACK, b=2),
-            w1_raw[:].rearrange("p a (m t b) -> p a t m b", t=PACK, b=2))
-        w1_dealt_scales = tile("w1_dealt_scales", [P, 2 * H], U8)
+            w1_dealt[:].bitcast(U16).rearrange("p a (t m) -> p a t m", t=PACK),
+            w1_raw[:].bitcast(U16).rearrange("p a (m t) -> p a t m", t=PACK))
+        w1_dealt_scales = tile("w1_dealt_scales", [P, 2 * H], U8, "slot2")
         nc.vector.tensor_copy(
             w1_dealt_scales[:].rearrange("p (a t m) -> p a t m", a=2, t=PACK),
             w1_plane[:].rearrange("p (a m t) -> p a t m", a=2, t=PACK))
-        w4_dealt = tile("w4_dealt", [P, N], I32)
-        nc.vector.tensor_copy(
-            w4_dealt[:].rearrange("p (t m) -> p t m", t=PACK),
-            w4_raw[:].rearrange("p (m t) -> p t m", t=PACK))
-        w4_dealt_scales = tile("w4_dealt_scales", [P, N], U8)
-        nc.vector.tensor_copy(
-            w4_dealt_scales[:].rearrange("p (t m) -> p t m", t=PACK),
-            w4_plane[:].rearrange("p (m t) -> p t m", t=PACK))
-
-        second_stream(3)
-        place_second(2)
 
         z_woven = tile("z_woven", [P, T2, PACK], BF16)
 
         def first_stream(t):
             for u, cols in enumerate(halves):
-                acc = bank("a_%d_%d" % (t, u), (2 * t + u) % 4)
+                acc = bank("a_%d_%d" % (t, u), (4, 6, 0, 2)[t] + u)
                 for a in range(2):
                     nc.tensor.matmul_mx(
                         out=acc[:], lhsT=w1_dealt[:, a, 2 * P * t : 2 * P * (t + 1)].bitcast(FP4X4),
@@ -209,17 +201,32 @@ def tile_list_woven_tile_denoise_kernel(
                 nc.vector.tensor_tensor(h1[t][:, cols], acc[:], h1[t][:, cols], ALU.mult)
 
         def place_first(t):
-            nc.vector.tensor_tensor(page[t][:].indirect(list3[:]), h1[t][:], gain1[:, t, :], ALU.mult)
+            nc.vector.tensor_tensor(page[t][:].indirect(list3[:]), h1[t][:], gain1[t], ALU.mult)
 
+        place_second(2)
         first_stream(0)
-        place_second(3)
+        w4_dealt = tile("w4_dealt", [P, N], I32, "h2_1")
+        nc.vector.tensor_copy(
+            w4_dealt[:].rearrange("p (t m) -> p t m", t=PACK),
+            w4_raw[:].rearrange("p (m t) -> p t m", t=PACK))
+        w4_dealt_scales = tile("w4_dealt_scales", [P, N], U8, "h2_2")
+        nc.vector.tensor_copy(
+            w4_dealt_scales[:].rearrange("p (t m) -> p t m", t=PACK),
+            w4_plane[:].rearrange("p (m t) -> p t m", t=PACK))
+
+
         for t in range(PACK - 1):
-            first_stream(t + 1)
+            if t + 1 < PACK - 1:
+                first_stream(t + 1)
+            else:
+                second_stream(PACK - 1)
             place_first(t)
             if t < PACK - 2:
                 nc.scalar.activation(z_woven[:, :, t], page[t][:], ACT.Relu)
             else:
                 nc.scalar.activation(z_woven[:, :, t : t + 2], page[t][:].unsqueeze(2).to_broadcast([P, T2, 2]), ACT.Relu)
+        first_stream(PACK - 1)
+        place_second(PACK - 1)
         place_first(PACK - 1)
 
         z_codes = tile("z_codes", [P, T2], U32)
@@ -233,7 +240,7 @@ def tile_list_woven_tile_denoise_kernel(
 
         def make_z(c):
             cols = slice(starts[c], starts[c] + CHUNKS[c])
-            if c == len(CHUNKS) - 2:
+            if c >= len(CHUNKS) - 2:
                 nc.scalar.activation(z_woven[:, cols, PACK - 1], page[PACK - 1][:, cols], ACT.Relu)
             else:
                 nc.vector.tensor_scalar_max(z_woven[:, cols, PACK - 1], page[PACK - 1][:, cols], 0.0)
@@ -246,7 +253,7 @@ def tile_list_woven_tile_denoise_kernel(
         def multiply(c):
             width = CHUNKS[c]
             cols = slice(starts[c], starts[c] + width)
-            y = tile("y%d" % c, [P, PACK, width], F32, "slot%d" % ((c + 1) % 4))
+            y = tile("y%d" % c, [P, PACK, width], F32, ("gain2_0", "slot0", "slot1", "gain2_1", "gain1_0")[c])
             for t in range(PACK):
                 rows = slice(P * t, P * (t + 1))
                 acc = bank("y_%d_%d" % (c, t), (4 * c + t) % 8)
@@ -259,7 +266,7 @@ def tile_list_woven_tile_denoise_kernel(
 
         def weave_y(c):
             width = CHUNKS[c]
-            woven = tile("y_woven%d" % c, [P, width * PACK], BF16, "woven%d" % (c % 3))
+            woven = tile("y_woven%d" % c, [P, width * PACK], BF16, ("woven0", "h1_0", "h1_1")[c % 3])
             nc.vector.tensor_copy(
                 woven[:].rearrange("p (m i t) -> p m t i", i=4, t=PACK),
                 y_tiles[c][:].rearrange("p t (m i) -> p m t i", i=4))
@@ -272,10 +279,11 @@ def tile_list_woven_tile_denoise_kernel(
 
         count = len(CHUNKS)
         make_z(count - 2)
+        make_z(count - 1)
         make_z(0)
         woven = {}
         for c in range(count + 2):
-            if c + 1 < count and c + 1 != count - 2:
+            if c + 1 < count - 2:
                 make_z(c + 1)
             if c < count:
                 quantise_z(c)
@@ -285,4 +293,4 @@ def tile_list_woven_tile_denoise_kernel(
             if c >= 2:
                 quantise_y(c - 2, woven[c - 2])
         for q in range(4):
-            nc.sync.dma_start(out_2[0, 4 * q : 4 * q + 4, :].bitcast(I32), y_scales[32 * q : 32 * q + 4, :].bitcast(I32))
+            (nc.scalar, nc.sync)[q % 2].dma_start(out_2[0, 4 * q : 4 * q + 4, :].bitcast(I32), y_scales[32 * q : 32 * q + 4, :].bitcast(I32))

@@ -34,8 +34,8 @@ def tile_list_woven_tile_denoise_kernel(
         keep = ctx.enter_context(tc.tile_pool(name="keep", bufs=1))
         psum = ctx.enter_context(tc.psum_pool(name="psum", bufs=1))
 
-        def tile(name, shape, dtype, tag=None):
-            return keep.tile(shape, dtype, name=name, tag=tag or name, align_bytes=64)
+        def tile(name, shape, dtype, after=None):
+            return keep.tile(shape, dtype, name=name, tag=after or name, align_bytes=64)
 
         def bank(name, index):
             return psum.tile([P, BANK], F32, name=name, tag="bank%d" % index)
@@ -45,8 +45,8 @@ def tile_list_woven_tile_denoise_kernel(
             nc.sync.dma_start(held[:], source)
             return held
 
-        def load_words(name, source, tag=None):
-            held = tile(name, [P, source.shape[1]], I32, tag)
+        def load_words(name, source):
+            held = tile(name, [P, source.shape[1]], I32)
             nc.sync.dma_start(held[:], source.rearrange("p c i -> p (c i)").bitcast(I32))
             return held
 
@@ -55,39 +55,44 @@ def tile_list_woven_tile_denoise_kernel(
             nc.gpsimd.memset(plane[:].bitcast(I32), 0)
             return plane
 
-        def gather(name, window, offsets, dtype, tag=None):
-            picked = tile(name, [P, S], dtype, tag)
-            nc.vector.tensor_copy(picked[:], window.indirect(offsets[:]))
-            return picked
-
-        def load_weight(name, rows, tag):
-            raw = tile(name, [P, PACK, H], F32, tag)
+        def load_weight(name, rows):
+            raw = tile(name, [P, PACK, H], F32)
             nc.sync.dma_start(raw[:], rows.rearrange("(p i) c -> p i c", i=PACK))
             return raw
 
-        def quantise_weight(name, raw, tag, codes_tag=None):
-            woven = tile(name + "_bf", [P, H * PACK], BF16, tag)
+        def load_prev(t):
+            held = tile("prev%d" % t, [P, S], F32)
+            nc.sync.dma_start(held[:], prev.rearrange("(p t) j -> p t j", t=PACK)[:, t, :])
+            return held
+
+        def load_gain(name, source, t):
+            held = tile("%s_%d" % (name, t), [P, S], F32)
+            rows = source.rearrange("(m t) j -> m t j", t=PACK)[:, t, :]
+            for q in (0, 2, 1, 3):
+                nc.sync.dma_start(held[32 * q : 32 * q + 32, :], rows)
+            return held
+
+        def gather(name, window, offsets, dtype, after=None):
+            picked = tile(name, [P, S], dtype, after)
+            nc.vector.tensor_copy(picked[:], window.indirect(offsets[:]))
+            return picked
+
+        def quantise_weight(name, raw, woven_name, codes_after=None):
+            woven = tile(name + "_bf", [P, H * PACK], BF16, woven_name)
             nc.scalar.copy(
                 woven[:].rearrange("p (t m i) -> p m t i", t=PACK, i=PACK),
                 raw[:].rearrange("p i (m t) -> p m t i", t=PACK),
             )
-            codes = tile(name + "_codes", [P, H], U32, codes_tag)
+            codes = tile(name + "_codes", [P, H], U32, codes_after)
             scales = tile(name + "_scales", [P, H], U8)
             nc.vector.quantize_mx(out=codes[:].bitcast(FP8X4), scales=scales[:], in_=woven[:])
             return codes, scales
 
-        def load_gain(name, source, first, last):
-            held = tile(name, [P, last - first, S], F32)
-            rows = source.rearrange("(m t) j -> m t j", t=PACK)[:, first:last, :]
-            for q in (0, 2, 1, 3):
-                nc.sync.dma_start(held[32 * q : 32 * q + 32, :, :], rows)
-            return [held[:, t, :] for t in range(last - first)]
-
         tab2_plane = zeroed_plane("tab2_plane", T)
         tab_plane = zeroed_plane("tab_plane", T)
+        v_scales_1 = zeroed_plane("v_scales_1", S)
         w1_plane = zeroed_plane("w1_plane", 2 * H)
         w4_plane = zeroed_plane("w4_plane", N)
-        v_scales_1 = zeroed_plane("v_scales_1", S)
 
         list2 = load_list("list2", offs2)
         tab2_w = load_words("tab2_w", tab2_words[0])
@@ -96,20 +101,19 @@ def tile_list_woven_tile_denoise_kernel(
                                 tab2_scales[0, 4 * q : 4 * q + 4, :].bitcast(I32))
         level_t = tile("level_t", [P, PACK], F32)
         nc.scalar.dma_start(level_t[:], level.rearrange("(p t) -> p t", t=PACK))
-        w3_raw = load_weight("w3_raw", w3, "slot0")
-        prev_rows = prev.rearrange("(p t) j -> p t j", t=PACK)
-        h2 = [tile("h2_%d" % t, [P, S], F32) for t in range(PACK)]
-        nc.sync.dma_start(h2[0][:], prev_rows[:, 0, :])
-        list4 = load_list("list4", offs4)
-        gain2 = load_gain("gain2_0", wg2, 0, 1)
-        nc.sync.dma_start(h2[1][:], prev_rows[:, 1, :])
+        w3_raw = load_weight("w3_raw", w3)
         list1 = load_list("list1", offs)
-        tab_w = [load_words("tab_w%d" % a, tab_words[a]) for a in range(2)]
         for q in range(4):
             nc.gpsimd.dma_start(tab_plane[32 * q : 32 * q + 8, :].bitcast(I32),
                                 tab_scales[:, 4 * q : 4 * q + 4, :].bitcast(I32))
-        w2_raw = [load_weight("w2_raw%d" % a, w2[512 * a : 512 * (a + 1), :], "slot%d" % (1 + a)) for a in range(2)]
-        gain2.extend(load_gain("gain2_1", wg2, 1, 4))
+        tab_w = [load_words("tab_w0", tab_words[0])]
+        earlier = [load_prev(0)]
+        gain2 = [load_gain("gain2", wg2, 0)]
+        tab_w.append(load_words("tab_w1", tab_words[1]))
+        list4 = load_list("list4", offs4)
+        w2_raw = [load_weight("w2_raw%d" % a, w2[512 * a : 512 * (a + 1), :]) for a in range(2)]
+        earlier.append(load_prev(1))
+        gain2.append(load_gain("gain2", wg2, 1))
         list3 = load_list("list3", offs3)
         w1_raw = tile("w1_raw", [P, 2, 2 * H], U8)
         nc.sync.dma_start(w1_raw[:].bitcast(I32), w1_words.rearrange("a p c -> p a c").bitcast(I32))
@@ -117,80 +121,91 @@ def tile_list_woven_tile_denoise_kernel(
             nc.sync.dma_start(
                 w1_plane[32 * q : 32 * q + 4, :].rearrange("p (a c) -> p a c", a=2).bitcast(I32),
                 w1_scales[:, 4 * q : 4 * q + 4, :].rearrange("a r c -> r a c").bitcast(I32))
-        nc.sync.dma_start(h2[2][:], prev_rows[:, 2, :])
-        gain1 = load_gain("gain1_0", wg1, 0, 2)
+        earlier.append(load_prev(2))
+        gain2.append(load_gain("gain2", wg2, 2))
+        gain1 = [load_gain("gain1", wg1, t) for t in range(2)]
+        earlier.append(load_prev(3))
+        gain2.append(load_gain("gain2", wg2, 3))
+        gain1.extend(load_gain("gain1", wg1, t) for t in range(2, 4))
         w4_raw = load_words("w4_raw", w4_words[0])
         for q in range(4):
             nc.sync.dma_start(w4_plane[32 * q : 32 * q + 4, :].bitcast(I32),
                               w4_scales[0, 4 * q : 4 * q + 4, :].bitcast(I32))
-        nc.sync.dma_start(h2[3][:], prev_rows[:, 3, :])
-        gain1.extend(load_gain("gain1_1", wg1, 2, 4))
 
         v2_words = gather("v2_words", tab2_w[:].bitcast(U32), list2, U32)
         v2_scales = gather("v2_scales", tab2_plane[:], list2, U8)
-        w3_codes, w3_scales = quantise_weight("w3", w3_raw, "woven0")
-        page = {}
-        halves = [slice(BANK * u, BANK * (u + 1)) for u in range(S // BANK)]
+        w3_codes, w3_scales = quantise_weight("w3", w3_raw, "w3_bf")
+        v_words = [gather("v_words0", tab_w[0][:].bitcast(U32), list1, U32, "w3_bf")]
+        v_scales = gather("v_scales", tab_plane[:], list1, U8, "tab_w0")
+        v_words.append(gather("v_words1", tab_w[1][:].bitcast(U32), list1, U32, "tab_plane"))
+        nc.gpsimd.dma_start(v_scales_1[0:112, :].bitcast(I32), v_scales[4:116, :].bitcast(I32))
 
-        def second_stream(t):
+        log_level = tile("log_level", [P, PACK], F32)
+        nc.scalar.activation(log_level[:], level_t[:], ACT.Ln)
+        neg_log_level = tile("neg_log_level", [P, PACK], F32)
+        nc.scalar.mul(neg_log_level[:], log_level[:], -1.0)
+
+        halves = [slice(BANK * u, BANK * (u + 1)) for u in range(S // BANK)]
+        page, first, second, staged = {}, {}, {}, {}
+
+        def second_product(t):
             rows = slice(P * t, P * (t + 1))
+            staged[t] = tile("c%d" % t, [P, S], F32, "staged%d" % t)
             for u, cols in enumerate(halves):
-                acc = bank("c_%d_%d" % (t, u), (0, 2, 2, 0)[t] + u)
+                acc = bank("c_%d_%d" % (t, u), 2 * t + u)
                 nc.tensor.matmul_mx(out=acc[:], lhsT=w3_codes[:, rows].bitcast(FP8X4), lhsT_scale=w3_scales[:, rows],
                                     rhs=v2_words[:, cols].bitcast(FP8X4), rhs_scale=v2_scales[:, cols],
                                     start=True, stop=True)
-                nc.vector.tensor_tensor(h2[t][:, cols], acc[:], h2[t][:, cols], ALU.add)
+                nc.scalar.copy(staged[t][:, cols], acc[:])
 
-        def place_second(t):
-            page[t] = tile("page%d" % t, [P, T2], F32)
-            nc.vector.tensor_tensor(page[t][:].indirect(list4[:]), h2[t][:], gain2[t], ALU.mult)
+        def second_values(t, after):
+            second[t] = tile("second%d" % t, [P, S], F32, after)
+            nc.gpsimd.tensor_tensor(second[t][:], staged[t][:], earlier[t][:], ALU.add)
+            nc.gpsimd.tensor_tensor(second[t][:], second[t][:], gain2[t][:], ALU.mult)
 
+        def place_second(t, after):
+            page[t] = tile("page%d" % t, [P, T2], F32, after)
+            nc.vector.tensor_copy(page[t][:].indirect(list4[:]), second[t][:])
 
-        second_stream(0)
-        second_stream(1)
-        place_second(0)
-        v_words = [gather("v_words%d" % a, tab_w[a][:].bitcast(U32), list1, U32, ("h2_0", "tab_w0")[a]) for a in range(2)]
-        v_scales = gather("v_scales", tab_plane[:], list1, U8, "tab_w1")
-        nc.sync.dma_start(v_scales_1[0:112, :].bitcast(I32), v_scales[4:116, :].bitcast(I32))
-
-        neg_log_level = tile("neg_log_level", [P, PACK], F32)
-        log_level = tile("log_level", [P, PACK], F32)
-        nc.scalar.activation(log_level[:], level_t[:], ACT.Ln)
-        nc.scalar.mul(neg_log_level[:], log_level[:], -1.0)
-
-        w2_q = [quantise_weight("w2_%d" % a, w2_raw[a], ("woven1", "page1")[a], ("tab_plane", None)[a]) for a in range(2)]
-
-        h1 = [tile("h1_%d" % t, [P, S], F32) for t in range(PACK)]
         for t in range(PACK):
-            rows = slice(P * t, P * (t + 1))
-            for u, cols in enumerate(halves):
-                acc = bank("b_%d_%d" % (t, u), 2 * t + u)
-                for a in range(2):
-                    nc.tensor.matmul_mx(out=acc[:], lhsT=w2_q[a][0][:, rows].bitcast(FP8X4), lhsT_scale=w2_q[a][1][:, rows],
-                                        rhs=v_words[a][:, cols].bitcast(FP8X4), rhs_scale=v_scales[4 * a : P, cols],
-                                        start=(a == 0), stop=(a == 1))
-                nc.scalar.activation(h1[t][:, cols], acc[:], ACT.Abs)
-            nc.scalar.activation(h1[t][:], h1[t][:], ACT.Ln, bias=TINY)
-        for t in range(PACK):
-            nc.scalar.activation(h1[t][:], h1[t][:], ACT.Sigmoid, bias=neg_log_level[:, t : t + 1], scale=2.0)
+            second_product(t)
+        second_values(0, None)
+        place_second(0, None)
 
-        place_second(1)
-        second_stream(2)
+        w2_q = [quantise_weight("w2_%d" % a, w2_raw[a], "w2_%d_bf" % a, ("second0", None)[a]) for a in range(2)]
+        second_values(1, "gain2_0")
+        place_second(1, "w2_1_bf")
 
-        w1_dealt = tile("w1_dealt", [P, 2, 2 * H], U8, "woven1")
+        w1_dealt = tile("w1_dealt", [P, 2, 2 * H], U8, "w2_0_bf")
         nc.vector.tensor_copy(
             w1_dealt[:].bitcast(U16).rearrange("p a (t m) -> p a t m", t=PACK),
             w1_raw[:].bitcast(U16).rearrange("p a (m t) -> p a t m", t=PACK))
-        w1_dealt_scales = tile("w1_dealt_scales", [P, 2 * H], U8, "slot2")
+        w1_dealt_scales = tile("w1_dealt_scales", [P, 2 * H], U8, "w2_raw1")
         nc.vector.tensor_copy(
             w1_dealt_scales[:].rearrange("p (a t m) -> p a t m", a=2, t=PACK),
             w1_plane[:].rearrange("p (a m t) -> p a t m", a=2, t=PACK))
 
-        z_woven = tile("z_woven", [P, T2, PACK], BF16)
+        logs = [tile("logs%d" % pair, [P, 2 * S], F32) for pair in range(2)]
+        shrink = [logs[t // 2][:, S * (t % 2) : S * (t % 2 + 1)] for t in range(PACK)]
 
-        def first_stream(t):
+        def shrinkage(pair):
+            for t in (2 * pair, 2 * pair + 1):
+                rows = slice(P * t, P * (t + 1))
+                for u, cols in enumerate(halves):
+                    acc = bank("b_%d_%d" % (t, u), 2 * t + u)
+                    for a in range(2):
+                        nc.tensor.matmul_mx(out=acc[:], lhsT=w2_q[a][0][:, rows].bitcast(FP8X4), lhsT_scale=w2_q[a][1][:, rows],
+                                            rhs=v_words[a][:, cols].bitcast(FP8X4), rhs_scale=v_scales[4 * a : P, cols],
+                                            start=(a == 0), stop=(a == 1))
+                    nc.scalar.activation(shrink[t][:, cols], acc[:], ACT.Abs)
+            nc.scalar.activation(logs[pair][:], logs[pair][:], ACT.Ln, bias=TINY)
+            for t in (2 * pair, 2 * pair + 1):
+                nc.scalar.activation(shrink[t], shrink[t], ACT.Sigmoid, bias=neg_log_level[:, t : t + 1], scale=2.0)
+
+        def first_values(t):
+            first[t] = tile("first%d" % t, [P, S], F32, "staged%d" % t if t < 3 else None)
             for u, cols in enumerate(halves):
-                acc = bank("a_%d_%d" % (t, u), (4, 6, 0, 2)[t] + u)
+                acc = bank("a_%d_%d" % (t, u), 2 * t + u)
                 for a in range(2):
                     nc.tensor.matmul_mx(
                         out=acc[:], lhsT=w1_dealt[:, a, 2 * P * t : 2 * P * (t + 1)].bitcast(FP4X4),
@@ -198,36 +213,42 @@ def tile_list_woven_tile_denoise_kernel(
                         rhs=v_words[a][:, cols].bitcast(FP8X4),
                         rhs_scale=(v_scales, v_scales_1)[a][:, cols],
                         start=(a == 0), stop=(a == 1))
-                nc.vector.tensor_tensor(h1[t][:, cols], acc[:], h1[t][:, cols], ALU.mult)
+                nc.scalar.copy(first[t][:, cols], acc[:])
+            nc.gpsimd.tensor_tensor(first[t][:], first[t][:], gain1[t][:], ALU.mult)
+            nc.gpsimd.tensor_tensor(first[t][:], first[t][:], shrink[t], ALU.mult)
 
         def place_first(t):
-            nc.vector.tensor_tensor(page[t][:].indirect(list3[:]), h1[t][:], gain1[t], ALU.mult)
+            nc.vector.tensor_copy(page[t][:].indirect(list3[:]), first[t][:])
 
-        place_second(2)
-        first_stream(0)
-        w4_dealt = tile("w4_dealt", [P, N], I32, "h2_1")
+        shrinkage(0)
+        second_values(2, "gain2_1")
+        place_second(2, None)
+        first_values(0)
+        first_values(1)
+        shrinkage(1)
+        first_values(2)
+        second_values(3, "gain1_1")
+        first_values(3)
+
+        z_woven = tile("z_woven", [P, T2, PACK], BF16)
+
+        for t in range(2):
+            place_first(t)
+            nc.scalar.activation(z_woven[:, :, t], page[t][:], ACT.Relu)
+        place_first(2)
+        nc.scalar.activation(z_woven[:, :, 2:4], page[2][:].unsqueeze(2).to_broadcast([P, T2, 2]), ACT.Relu)
+
+        w4_dealt = tile("w4_dealt", [P, N], I32, "staged0")
         nc.vector.tensor_copy(
             w4_dealt[:].rearrange("p (t m) -> p t m", t=PACK),
             w4_raw[:].rearrange("p (m t) -> p t m", t=PACK))
-        w4_dealt_scales = tile("w4_dealt_scales", [P, N], U8, "h2_2")
+        w4_dealt_scales = tile("w4_dealt_scales", [P, N], U8, "staged1")
         nc.vector.tensor_copy(
             w4_dealt_scales[:].rearrange("p (t m) -> p t m", t=PACK),
             w4_plane[:].rearrange("p (m t) -> p t m", t=PACK))
 
-
-        for t in range(PACK - 1):
-            if t + 1 < PACK - 1:
-                first_stream(t + 1)
-            else:
-                second_stream(PACK - 1)
-            place_first(t)
-            if t < PACK - 2:
-                nc.scalar.activation(z_woven[:, :, t], page[t][:], ACT.Relu)
-            else:
-                nc.scalar.activation(z_woven[:, :, t : t + 2], page[t][:].unsqueeze(2).to_broadcast([P, T2, 2]), ACT.Relu)
-        first_stream(PACK - 1)
-        place_second(PACK - 1)
-        place_first(PACK - 1)
+        place_second(3, "staged2")
+        place_first(3)
 
         z_codes = tile("z_codes", [P, T2], U32)
         z_scales = tile("z_scales", [P, T2], U8)
@@ -253,7 +274,7 @@ def tile_list_woven_tile_denoise_kernel(
         def multiply(c):
             width = CHUNKS[c]
             cols = slice(starts[c], starts[c] + width)
-            y = tile("y%d" % c, [P, PACK, width], F32, ("gain2_0", "slot0", "slot1", "gain2_1", "gain1_0")[c])
+            y = tile("y%d" % c, [P, PACK, width], F32, ("gain1_0", "w3_raw", "w2_raw0", "logs0", "gain1_2")[c])
             for t in range(PACK):
                 rows = slice(P * t, P * (t + 1))
                 acc = bank("y_%d_%d" % (c, t), (4 * c + t) % 8)
@@ -266,7 +287,7 @@ def tile_list_woven_tile_denoise_kernel(
 
         def weave_y(c):
             width = CHUNKS[c]
-            woven = tile("y_woven%d" % c, [P, width * PACK], BF16, ("woven0", "h1_0", "h1_1")[c % 3])
+            woven = tile("y_woven%d" % c, [P, width * PACK], BF16, "prev%d" % (c % 3))
             nc.vector.tensor_copy(
                 woven[:].rearrange("p (m i t) -> p m t i", i=4, t=PACK),
                 y_tiles[c][:].rearrange("p t (m i) -> p m t i", i=4))

@@ -77,15 +77,17 @@ def tile_list_woven_tile_denoise_kernel(
             nc.vector.tensor_copy(picked[:], window.indirect(offsets[:]))
             return picked
 
-        def quantise_weight(name, raw, woven_name, codes_after=None):
-            woven = tile(name + "_bf", [P, H * PACK], BF16, woven_name)
-            nc.scalar.copy(
-                woven[:].rearrange("p (t m i) -> p m t i", t=PACK, i=PACK),
-                raw[:].rearrange("p i (m t) -> p m t i", t=PACK),
-            )
-            codes = tile(name + "_codes", [P, H], U32, codes_after)
-            scales = tile(name + "_scales", [P, H], U8)
-            nc.vector.quantize_mx(out=codes[:].bitcast(FP8X4), scales=scales[:], in_=woven[:])
+        def quantise_weight(name, passes, codes_after=None):
+            woven = tile(name + "_bf", [P, len(passes), H * PACK], BF16)
+            for a, raw in enumerate(passes):
+                nc.scalar.copy(
+                    woven[:, a, :].rearrange("p (t m i) -> p m t i", t=PACK, i=PACK),
+                    raw[:].rearrange("p i (m t) -> p m t i", t=PACK),
+                )
+            codes = tile(name + "_codes", [P, len(passes) * H], U32, codes_after)
+            scales = tile(name + "_scales", [P, len(passes) * H], U8)
+            nc.vector.quantize_mx(out=codes[:].bitcast(FP8X4), scales=scales[:],
+                                  in_=woven[:].rearrange("p a c -> p (a c)"))
             return codes, scales
 
         tab2_plane = zeroed_plane("tab2_plane", T)
@@ -112,15 +114,24 @@ def tile_list_woven_tile_denoise_kernel(
         tab_w.append(load_words("tab_w1", tab_words[1]))
         list4 = load_list("list4", offs4)
         w2_raw = [load_weight("w2_raw%d" % a, w2[512 * a : 512 * (a + 1), :]) for a in range(2)]
-        earlier.append(load_prev(1))
-        gain2.append(load_gain("gain2", wg2, 1))
-        list3 = load_list("list3", offs3)
+
+        v2_words = gather("v2_words", tab2_w[:].bitcast(U32), list2, U32)
+        v2_scales = gather("v2_scales", tab2_plane[:], list2, U8)
+        w3_codes, w3_scales = quantise_weight("w3", [w3_raw])
+        v_words = [gather("v_words0", tab_w[0][:].bitcast(U32), list1, U32, "w3_bf")]
+        v_scales = gather("v_scales", tab_plane[:], list1, U8, "tab_w0")
+        v_words.append(gather("v_words1", tab_w[1][:].bitcast(U32), list1, U32, "tab_plane"))
+        nc.sync.dma_start(v_scales_1[0:112, :].bitcast(I32), v_scales[4:116, :].bitcast(I32))
+
         w1_raw = tile("w1_raw", [P, 2, 2 * H], U8)
         nc.sync.dma_start(w1_raw[:].bitcast(I32), w1_words.rearrange("a p c -> p a c").bitcast(I32))
         for q in range(4):
             nc.sync.dma_start(
                 w1_plane[32 * q : 32 * q + 4, :].rearrange("p (a c) -> p a c", a=2).bitcast(I32),
                 w1_scales[:, 4 * q : 4 * q + 4, :].rearrange("a r c -> r a c").bitcast(I32))
+        earlier.append(load_prev(1))
+        gain2.append(load_gain("gain2", wg2, 1))
+        list3 = load_list("list3", offs3)
         earlier.append(load_prev(2))
         gain2.append(load_gain("gain2", wg2, 2))
         gain1 = [load_gain("gain1", wg1, t) for t in range(2)]
@@ -131,14 +142,6 @@ def tile_list_woven_tile_denoise_kernel(
         for q in range(4):
             nc.sync.dma_start(w4_plane[32 * q : 32 * q + 4, :].bitcast(I32),
                               w4_scales[0, 4 * q : 4 * q + 4, :].bitcast(I32))
-
-        v2_words = gather("v2_words", tab2_w[:].bitcast(U32), list2, U32)
-        v2_scales = gather("v2_scales", tab2_plane[:], list2, U8)
-        w3_codes, w3_scales = quantise_weight("w3", w3_raw, "w3_bf")
-        v_words = [gather("v_words0", tab_w[0][:].bitcast(U32), list1, U32, "w3_bf")]
-        v_scales = gather("v_scales", tab_plane[:], list1, U8, "tab_w0")
-        v_words.append(gather("v_words1", tab_w[1][:].bitcast(U32), list1, U32, "tab_plane"))
-        nc.gpsimd.dma_start(v_scales_1[0:112, :].bitcast(I32), v_scales[4:116, :].bitcast(I32))
 
         log_level = tile("log_level", [P, PACK], F32)
         nc.scalar.activation(log_level[:], level_t[:], ACT.Ln)
@@ -170,42 +173,39 @@ def tile_list_woven_tile_denoise_kernel(
         for t in range(PACK):
             second_product(t)
         second_values(0, None)
-        place_second(0, None)
+        place_second(0, "tab_w1")
 
-        w2_q = [quantise_weight("w2_%d" % a, w2_raw[a], "w2_%d_bf" % a, ("second0", None)[a]) for a in range(2)]
-        second_values(1, "gain2_0")
-        place_second(1, "w2_1_bf")
-
-        w1_dealt = tile("w1_dealt", [P, 2, 2 * H], U8, "w2_0_bf")
-        nc.vector.tensor_copy(
-            w1_dealt[:].bitcast(U16).rearrange("p a (t m) -> p a t m", t=PACK),
-            w1_raw[:].bitcast(U16).rearrange("p a (m t) -> p a t m", t=PACK))
-        w1_dealt_scales = tile("w1_dealt_scales", [P, 2 * H], U8, "w2_raw1")
+        w2_codes, w2_scales = quantise_weight("w2", w2_raw, "second0")
+        w1_dealt_scales = tile("w1_dealt_scales", [P, 2 * H], U8, "w2_bf")
         nc.vector.tensor_copy(
             w1_dealt_scales[:].rearrange("p (a t m) -> p a t m", a=2, t=PACK),
             w1_plane[:].rearrange("p (a m t) -> p a t m", a=2, t=PACK))
+        w1_dealt = tile("w1_dealt", [P, 2, 2 * H], U8, "w1_plane")
+        nc.vector.tensor_copy(
+            w1_dealt[:].bitcast(U16).rearrange("p a (t m) -> p a t m", t=PACK),
+            w1_raw[:].bitcast(U16).rearrange("p a (m t) -> p a t m", t=PACK))
+        second_values(1, "gain2_0")
+        place_second(1, "w1_raw")
 
         logs = [tile("logs%d" % pair, [P, 2 * S], F32) for pair in range(2)]
         shrink = [logs[t // 2][:, S * (t % 2) : S * (t % 2 + 1)] for t in range(PACK)]
 
         def shrinkage(pair):
             for t in (2 * pair, 2 * pair + 1):
-                rows = slice(P * t, P * (t + 1))
                 for u, cols in enumerate(halves):
-                    acc = bank("b_%d_%d" % (t, u), 2 * t + u)
+                    acc = bank("b_%d_%d" % (t, u), 2 * (t % 2) + u)
                     for a in range(2):
-                        nc.tensor.matmul_mx(out=acc[:], lhsT=w2_q[a][0][:, rows].bitcast(FP8X4), lhsT_scale=w2_q[a][1][:, rows],
+                        rows = slice(H * a + P * t, H * a + P * (t + 1))
+                        nc.tensor.matmul_mx(out=acc[:], lhsT=w2_codes[:, rows].bitcast(FP8X4), lhsT_scale=w2_scales[:, rows],
                                             rhs=v_words[a][:, cols].bitcast(FP8X4), rhs_scale=v_scales[4 * a : P, cols],
                                             start=(a == 0), stop=(a == 1))
                     nc.scalar.activation(shrink[t][:, cols], acc[:], ACT.Abs)
             nc.scalar.activation(logs[pair][:], logs[pair][:], ACT.Ln, bias=TINY)
-            for t in (2 * pair, 2 * pair + 1):
-                nc.scalar.activation(shrink[t], shrink[t], ACT.Sigmoid, bias=neg_log_level[:, t : t + 1], scale=2.0)
 
-        def first_values(t):
+        def first_product(t):
             first[t] = tile("first%d" % t, [P, S], F32, "staged%d" % t if t < 3 else None)
             for u, cols in enumerate(halves):
-                acc = bank("a_%d_%d" % (t, u), 2 * t + u)
+                acc = bank("a_%d_%d" % (t, u), 4 + 2 * (t % 2) + u)
                 for a in range(2):
                     nc.tensor.matmul_mx(
                         out=acc[:], lhsT=w1_dealt[:, a, 2 * P * t : 2 * P * (t + 1)].bitcast(FP4X4),
@@ -215,6 +215,9 @@ def tile_list_woven_tile_denoise_kernel(
                         start=(a == 0), stop=(a == 1))
                 nc.scalar.copy(first[t][:, cols], acc[:])
             nc.gpsimd.tensor_tensor(first[t][:], first[t][:], gain1[t][:], ALU.mult)
+
+        def first_values(t):
+            nc.scalar.activation(shrink[t], shrink[t], ACT.Sigmoid, bias=neg_log_level[:, t : t + 1], scale=2.0)
             nc.gpsimd.tensor_tensor(first[t][:], first[t][:], shrink[t], ALU.mult)
 
         def place_first(t):
@@ -223,11 +226,15 @@ def tile_list_woven_tile_denoise_kernel(
         shrinkage(0)
         second_values(2, "gain2_1")
         place_second(2, None)
+        first_product(0)
         first_values(0)
+        first_product(1)
         first_values(1)
         shrinkage(1)
+        first_product(2)
         first_values(2)
-        second_values(3, "gain1_1")
+        second_values(3, "gain1_2")
+        first_product(3)
         first_values(3)
 
         z_woven = tile("z_woven", [P, T2, PACK], BF16)
@@ -238,12 +245,12 @@ def tile_list_woven_tile_denoise_kernel(
         place_first(2)
         nc.scalar.activation(z_woven[:, :, 2:4], page[2][:].unsqueeze(2).to_broadcast([P, T2, 2]), ACT.Relu)
 
-        w4_dealt = tile("w4_dealt", [P, N], I32, "staged0")
-        nc.vector.tensor_copy(
+        w4_dealt = tile("w4_dealt", [P, N], I32, "gain1_3")
+        nc.gpsimd.tensor_copy(
             w4_dealt[:].rearrange("p (t m) -> p t m", t=PACK),
             w4_raw[:].rearrange("p (m t) -> p t m", t=PACK))
-        w4_dealt_scales = tile("w4_dealt_scales", [P, N], U8, "staged1")
-        nc.vector.tensor_copy(
+        w4_dealt_scales = tile("w4_dealt_scales", [P, N], U8, "logs1")
+        nc.gpsimd.tensor_copy(
             w4_dealt_scales[:].rearrange("p (t m) -> p t m", t=PACK),
             w4_plane[:].rearrange("p (m t) -> p t m", t=PACK))
 
@@ -261,7 +268,7 @@ def tile_list_woven_tile_denoise_kernel(
 
         def make_z(c):
             cols = slice(starts[c], starts[c] + CHUNKS[c])
-            if c >= len(CHUNKS) - 2:
+            if c == len(CHUNKS) - 2:
                 nc.scalar.activation(z_woven[:, cols, PACK - 1], page[PACK - 1][:, cols], ACT.Relu)
             else:
                 nc.vector.tensor_scalar_max(z_woven[:, cols, PACK - 1], page[PACK - 1][:, cols], 0.0)
@@ -274,7 +281,7 @@ def tile_list_woven_tile_denoise_kernel(
         def multiply(c):
             width = CHUNKS[c]
             cols = slice(starts[c], starts[c] + width)
-            y = tile("y%d" % c, [P, PACK, width], F32, ("gain1_0", "w3_raw", "w2_raw0", "logs0", "gain1_2")[c])
+            y = tile("y%d" % c, [P, PACK, width], F32, ("gain1_0", "w3_raw", "w2_raw0", "logs0", "gain1_1")[c])
             for t in range(PACK):
                 rows = slice(P * t, P * (t + 1))
                 acc = bank("y_%d_%d" % (c, t), (4 * c + t) % 8)
@@ -288,7 +295,8 @@ def tile_list_woven_tile_denoise_kernel(
         def weave_y(c):
             width = CHUNKS[c]
             woven = tile("y_woven%d" % c, [P, width * PACK], BF16, "prev%d" % (c % 3))
-            nc.vector.tensor_copy(
+            copy = nc.scalar.copy if c == len(CHUNKS) - 1 else nc.vector.tensor_copy
+            copy(
                 woven[:].rearrange("p (m i t) -> p m t i", i=4, t=PACK),
                 y_tiles[c][:].rearrange("p t (m i) -> p m t i", i=4))
             return woven
@@ -300,11 +308,10 @@ def tile_list_woven_tile_denoise_kernel(
 
         count = len(CHUNKS)
         make_z(count - 2)
-        make_z(count - 1)
         make_z(0)
         woven = {}
         for c in range(count + 2):
-            if c + 1 < count - 2:
+            if c + 1 < count and c + 1 != count - 2:
                 make_z(c + 1)
             if c < count:
                 quantise_z(c)

@@ -20,6 +20,7 @@ P = 128
 PACK = 4
 BANK = 512
 TINY = 2.0 ** -63
+SHORT = 256
 CHUNKS = (256, 512, 512, 512, 256)
 
 
@@ -163,8 +164,13 @@ def tile_list_woven_tile_denoise_kernel(
 
         def second_values(t, after):
             second[t] = tile("second%d" % t, [P, S], F32, after)
-            nc.gpsimd.tensor_tensor(second[t][:], staged[t][:], earlier[t][:], ALU.add)
-            nc.gpsimd.tensor_tensor(second[t][:], second[t][:], gain2[t][:], ALU.mult)
+            width = SHORT if t in (1, 2) else S
+            for c in range(0, S, width):
+                cols = slice(c, c + width)
+                nc.gpsimd.tensor_tensor(second[t][:, cols], staged[t][:, cols], earlier[t][:, cols], ALU.add)
+            for c in range(0, S, width):
+                cols = slice(c, c + width)
+                nc.gpsimd.tensor_tensor(second[t][:, cols], second[t][:, cols], gain2[t][:, cols], ALU.mult)
 
         def place_second(t, after):
             page[t] = tile("page%d" % t, [P, T2], F32, after)
@@ -239,9 +245,11 @@ def tile_list_woven_tile_denoise_kernel(
 
         z_woven = tile("z_woven", [P, T2, PACK], BF16)
 
+        z_pair = tile("z_pair", [P, 2, T2], BF16)
         for t in range(2):
             place_first(t)
-            nc.scalar.activation(z_woven[:, :, t], page[t][:], ACT.Relu)
+            nc.scalar.activation(z_pair[:, t, :], page[t][:], ACT.Relu)
+        nc.scalar.copy(z_woven[:, :, 0:2], z_pair[:].rearrange("p t m -> p m t"))
         place_first(2)
         nc.scalar.activation(z_woven[:, :, 2:4], page[2][:].unsqueeze(2).to_broadcast([P, T2, 2]), ACT.Relu)
 
@@ -289,7 +297,8 @@ def tile_list_woven_tile_denoise_kernel(
                                     rhs=z_codes[:, cols].bitcast(FP8X4), rhs_scale=z_scales[:, cols],
                                     start=True, stop=True)
                 nc.scalar.copy(y[:, t, :], acc[:, :width])
-            nc.sync.dma_start(out_rows[:, :, cols], y[:])
+                if t % 2 == 1:
+                    nc.sync.dma_start(out_rows[:, t - 1 : t + 1, cols], y[:, t - 1 : t + 1, :])
             y_tiles[c] = y
 
         def weave_y(c):

@@ -20,7 +20,6 @@ P = 128
 PACK = 4
 BANK = 512
 TINY = 2.0 ** -63
-SHORT = 256
 CHUNKS = (256, 512, 512, 512, 256)
 
 
@@ -35,8 +34,11 @@ def tile_list_woven_tile_denoise_kernel(
         keep = ctx.enter_context(tc.tile_pool(name="keep", bufs=1))
         psum = ctx.enter_context(tc.psum_pool(name="psum", bufs=1))
 
-        def tile(name, shape, dtype, after=None):
-            return keep.tile(shape, dtype, name=name, tag=after or name, align_bytes=64)
+        halves = [slice(BANK * u, BANK * (u + 1)) for u in range(S // BANK)]
+        whole = slice(0, S)
+
+        def tile(name, shape, dtype, on=None):
+            return keep.tile(shape, dtype, name=name, tag=on or name, align_bytes=64)
 
         def bank(name, index):
             return psum.tile([P, BANK], F32, name=name, tag="bank%d" % index)
@@ -61,84 +63,80 @@ def tile_list_woven_tile_denoise_kernel(
             nc.sync.dma_start(raw[:], rows.rearrange("(p i) c -> p i c", i=PACK))
             return raw
 
-        def load_prev(t):
-            held = tile("prev%d" % t, [P, S], F32)
-            nc.sync.dma_start(held[:], prev.rearrange("(p t) j -> p t j", t=PACK)[:, t, :])
-            return held
+        earlier = [tile("prev%d" % t, [P, S], F32) for t in range(PACK)]
+        gain1 = [tile("gain1_%d" % t, [P, S], F32) for t in range(PACK)]
+        gain2 = [tile("gain2_%d" % t, [P, S], F32) for t in range(PACK)]
 
-        def load_gain(name, source, t):
-            held = tile("%s_%d" % (name, t), [P, S], F32)
-            rows = source.rearrange("(m t) j -> m t j", t=PACK)[:, t, :]
+        def load_prev(t, cols):
+            nc.sync.dma_start(earlier[t][:, cols], prev.rearrange("(p t) j -> p t j", t=PACK)[:, t, cols])
+
+        def load_gain(held, source, t, cols):
+            rows = source.rearrange("(m t) j -> m t j", t=PACK)[:, t, cols]
             for q in (0, 2, 1, 3):
-                nc.sync.dma_start(held[32 * q : 32 * q + 32, :], rows)
-            return held
+                nc.sync.dma_start(held[t][32 * q : 32 * q + 32, cols], rows)
 
-        def gather(name, window, offsets, dtype, after=None):
-            picked = tile(name, [P, S], dtype, after)
+        def gather(name, window, offsets, dtype, on=None):
+            picked = tile(name, [P, S], dtype, on)
             nc.vector.tensor_copy(picked[:], window.indirect(offsets[:]))
             return picked
 
-        def quantise_weight(name, passes, codes_after=None):
+        def quantise_weight(name, passes, codes_on=None):
             woven = tile(name + "_bf", [P, len(passes), H * PACK], BF16)
             for a, raw in enumerate(passes):
                 nc.scalar.copy(
                     woven[:, a, :].rearrange("p (t m i) -> p m t i", t=PACK, i=PACK),
                     raw[:].rearrange("p i (m t) -> p m t i", t=PACK),
                 )
-            codes = tile(name + "_codes", [P, len(passes) * H], U32, codes_after)
+            codes = tile(name + "_codes", [P, len(passes) * H], U32, codes_on)
             scales = tile(name + "_scales", [P, len(passes) * H], U8)
             nc.vector.quantize_mx(out=codes[:].bitcast(FP8X4), scales=scales[:],
                                   in_=woven[:].rearrange("p a c -> p (a c)"))
             return codes, scales
 
-        tab2_plane = zeroed_plane("tab2_plane", T)
         tab_plane = zeroed_plane("tab_plane", T)
         v_scales_1 = zeroed_plane("v_scales_1", S)
         w1_plane = zeroed_plane("w1_plane", 2 * H)
         w4_plane = zeroed_plane("w4_plane", N)
 
         list2 = load_list("list2", offs2)
-        tab2_w = load_words("tab2_w", tab2_words[0])
-        for q in range(4):
-            nc.scalar.dma_start(tab2_plane[32 * q : 32 * q + 4, :].bitcast(I32),
-                                tab2_scales[0, 4 * q : 4 * q + 4, :].bitcast(I32))
+        tab2_plane = tile("tab2_plane", [P, T], U8)
+        for q in (0, 2, 1, 3):
+            rows = tab2_scales[0, 4 * q : 4 * q + 4, :].bitcast(I32)
+            nc.sync.dma_start(tab2_plane[32 * q : 32 * q + 32, :].bitcast(I32),
+                              rows.unsqueeze(0).to_broadcast([8, 4, T // 4]))
         level_t = tile("level_t", [P, PACK], F32)
-        nc.scalar.dma_start(level_t[:], level.rearrange("(p t) -> p t", t=PACK))
+        nc.sync.dma_start(level_t[:], level.rearrange("(p t) -> p t", t=PACK))
+        tab2_w = load_words("tab2_w", tab2_words[0])
         w3_raw = load_weight("w3_raw", w3)
         list1 = load_list("list1", offs)
         for q in range(4):
-            nc.gpsimd.dma_start(tab_plane[32 * q : 32 * q + 8, :].bitcast(I32),
-                                tab_scales[:, 4 * q : 4 * q + 4, :].bitcast(I32))
+            nc.sync.dma_start(tab_plane[32 * q : 32 * q + 8, :].bitcast(I32),
+                              tab_scales[:, 4 * q : 4 * q + 4, :].bitcast(I32))
         tab_w = [load_words("tab_w0", tab_words[0])]
-        earlier = [load_prev(0)]
-        gain2 = [load_gain("gain2", wg2, 0)]
+        load_prev(0, halves[0])
         tab_w.append(load_words("tab_w1", tab_words[1]))
-        list4 = load_list("list4", offs4)
-        w2_raw = [load_weight("w2_raw%d" % a, w2[512 * a : 512 * (a + 1), :]) for a in range(2)]
-
-        v2_words = gather("v2_words", tab2_w[:].bitcast(U32), list2, U32)
-        v2_scales = gather("v2_scales", tab2_plane[:], list2, U8)
-        w3_codes, w3_scales = quantise_weight("w3", [w3_raw])
-        v_words = [gather("v_words0", tab_w[0][:].bitcast(U32), list1, U32, "w3_bf")]
-        v_scales = gather("v_scales", tab_plane[:], list1, U8, "tab_w0")
-        v_words.append(gather("v_words1", tab_w[1][:].bitcast(U32), list1, U32, "tab_plane"))
-        nc.sync.dma_start(v_scales_1[0:112, :].bitcast(I32), v_scales[4:116, :].bitcast(I32))
-
+        load_gain(gain2, wg2, 0, halves[0])
         w1_raw = tile("w1_raw", [P, 2, 2 * H], U8)
         nc.sync.dma_start(w1_raw[:].bitcast(I32), w1_words.rearrange("a p c -> p a c").bitcast(I32))
+        list4 = load_list("list4", offs4)
+        load_prev(0, halves[1])
+        load_gain(gain2, wg2, 0, halves[1])
         for q in range(4):
             nc.sync.dma_start(
                 w1_plane[32 * q : 32 * q + 4, :].rearrange("p (a c) -> p a c", a=2).bitcast(I32),
                 w1_scales[:, 4 * q : 4 * q + 4, :].rearrange("a r c -> r a c").bitcast(I32))
-        earlier.append(load_prev(1))
-        gain2.append(load_gain("gain2", wg2, 1))
+        load_prev(1, halves[0])
+        load_gain(gain2, wg2, 1, halves[0])
+        w2_raw = [load_weight("w2_raw%d" % a, w2[512 * a : 512 * (a + 1), :]) for a in range(2)]
+        load_prev(2, whole)
+        load_gain(gain2, wg2, 2, whole)
+        load_prev(1, halves[1])
+        load_gain(gain2, wg2, 1, halves[1])
         list3 = load_list("list3", offs3)
-        earlier.append(load_prev(2))
-        gain2.append(load_gain("gain2", wg2, 2))
-        gain1 = [load_gain("gain1", wg1, t) for t in range(2)]
-        earlier.append(load_prev(3))
-        gain2.append(load_gain("gain2", wg2, 3))
-        gain1.extend(load_gain("gain1", wg1, t) for t in range(2, 4))
+        load_prev(3, whole)
+        load_gain(gain2, wg2, 3, whole)
+        for t in range(PACK):
+            load_gain(gain1, wg1, t, whole)
         w4_raw = load_words("w4_raw", w4_words[0])
         for q in range(4):
             nc.sync.dma_start(w4_plane[32 * q : 32 * q + 4, :].bitcast(I32),
@@ -149,69 +147,65 @@ def tile_list_woven_tile_denoise_kernel(
         neg_log_level = tile("neg_log_level", [P, PACK], F32)
         nc.scalar.mul(neg_log_level[:], log_level[:], -1.0)
 
-        halves = [slice(BANK * u, BANK * (u + 1)) for u in range(S // BANK)]
-        page, first, second, staged = {}, {}, {}, {}
+        v2_scales = gather("v2_scales", tab2_plane[:], list2, U8)
+        v2_words = gather("v2_words", tab2_w[:].bitcast(U32), list2, U32, "tab2_plane")
+        v_scales = gather("v_scales", tab_plane[:], list1, U8)
+        nc.gpsimd.dma_start(v_scales_1[0:112, :].bitcast(I32), v_scales[4:116, :].bitcast(I32))
+        w3_codes, w3_scales = quantise_weight("w3", [w3_raw], "tab_plane")
+        v_words = [gather("v_words0", tab_w[0][:].bitcast(U32), list1, U32, "w3_bf")]
+        v_words.append(gather("v_words1", tab_w[1][:].bitcast(U32), list1, U32))
+        w1_dealt = tile("w1_dealt", [P, 2, 2 * H], U8)
+        nc.vector.tensor_copy(
+            w1_dealt[:].bitcast(U16).rearrange("p a (t m) -> p a t m", t=PACK),
+            w1_raw[:].bitcast(U16).rearrange("p a (m t) -> p a t m", t=PACK))
+
+        page, second, shrink = {}, {}, {}
 
         def second_product(t):
             rows = slice(P * t, P * (t + 1))
-            staged[t] = tile("c%d" % t, [P, S], F32, "staged%d" % t)
+            second[t] = tile("second%d" % t, [P, S], F32)
             for u, cols in enumerate(halves):
                 acc = bank("c_%d_%d" % (t, u), 2 * t + u)
                 nc.tensor.matmul_mx(out=acc[:], lhsT=w3_codes[:, rows].bitcast(FP8X4), lhsT_scale=w3_scales[:, rows],
                                     rhs=v2_words[:, cols].bitcast(FP8X4), rhs_scale=v2_scales[:, cols],
                                     start=True, stop=True)
-                nc.scalar.copy(staged[t][:, cols], acc[:])
+                nc.scalar.copy(second[t][:, cols], acc[:])
 
-        def second_values(t, after):
-            second[t] = tile("second%d" % t, [P, S], F32, after)
-            width = SHORT if t in (1, 2) else S
-            for c in range(0, S, width):
-                cols = slice(c, c + width)
-                nc.gpsimd.tensor_tensor(second[t][:, cols], staged[t][:, cols], earlier[t][:, cols], ALU.add)
-            for c in range(0, S, width):
-                cols = slice(c, c + width)
-                nc.gpsimd.tensor_tensor(second[t][:, cols], second[t][:, cols], gain2[t][:, cols], ALU.mult)
+        def second_values(t, cols, into=None):
+            into = second[t][:, cols] if into is None else into
+            nc.gpsimd.tensor_tensor(into, second[t][:, cols], earlier[t][:, cols], ALU.add)
+            nc.gpsimd.tensor_tensor(into, into, gain2[t][:, cols], ALU.mult)
+            return into
 
-        def place_second(t, after):
-            page[t] = tile("page%d" % t, [P, T2], F32, after)
-            nc.vector.tensor_copy(page[t][:].indirect(list4[:]), second[t][:])
+        def place(t, offsets, cols, values):
+            if t not in page:
+                page[t] = tile("page%d" % t, [P, T2], F32, ("w1_raw", "tab_w0", "w2_bf", "w3_raw")[t])
+            nc.vector.tensor_copy(page[t][:].indirect(offsets[:, cols.start // 16 : cols.stop // 16]), values)
+
 
         for t in range(PACK):
             second_product(t)
-        second_values(0, None)
-        place_second(0, "tab_w1")
+        for cols in halves:
+            place(0, list4, cols, second_values(0, cols))
 
-        w2_codes, w2_scales = quantise_weight("w2", w2_raw, "second0")
-        w1_dealt_scales = tile("w1_dealt_scales", [P, 2 * H], U8, "w2_bf")
-        nc.vector.tensor_copy(
+        w1_dealt_scales = tile("w1_dealt_scales", [P, 2 * H], U8)
+        nc.gpsimd.tensor_copy(
             w1_dealt_scales[:].rearrange("p (a t m) -> p a t m", a=2, t=PACK),
             w1_plane[:].rearrange("p (a m t) -> p a t m", a=2, t=PACK))
-        w1_dealt = tile("w1_dealt", [P, 2, 2 * H], U8, "w1_plane")
-        nc.vector.tensor_copy(
-            w1_dealt[:].bitcast(U16).rearrange("p a (t m) -> p a t m", t=PACK),
-            w1_raw[:].bitcast(U16).rearrange("p a (m t) -> p a t m", t=PACK))
-        second_values(1, "gain2_0")
-        place_second(1, "w1_raw")
 
-        logs = [tile("logs%d" % pair, [P, 2 * S], F32) for pair in range(2)]
-        shrink = [logs[t // 2][:, S * (t % 2) : S * (t % 2 + 1)] for t in range(PACK)]
+        place(1, list4, halves[0], second_values(1, halves[0]))
+        w2_codes, w2_scales = quantise_weight("w2", w2_raw)
+        for cols in halves:
+            place(2, list4, cols, second_values(2, cols))
+        place(1, list4, halves[1], second_values(1, halves[1]))
+        place(3, list4, halves[0], second_values(3, halves[0]))
 
-        def shrinkage(pair):
-            for t in (2 * pair, 2 * pair + 1):
-                for u, cols in enumerate(halves):
-                    acc = bank("b_%d_%d" % (t, u), 2 * (t % 2) + u)
-                    for a in range(2):
-                        rows = slice(H * a + P * t, H * a + P * (t + 1))
-                        nc.tensor.matmul_mx(out=acc[:], lhsT=w2_codes[:, rows].bitcast(FP8X4), lhsT_scale=w2_scales[:, rows],
-                                            rhs=v_words[a][:, cols].bitcast(FP8X4), rhs_scale=v_scales[4 * a : P, cols],
-                                            start=(a == 0), stop=(a == 1))
-                    nc.scalar.activation(shrink[t][:, cols], acc[:], ACT.Abs)
-            nc.scalar.activation(logs[pair][:], logs[pair][:], ACT.Ln, bias=TINY)
+        firsts = tile("firsts", [P, PACK, S], F32, "w2_raw1")
+        first = [firsts[:, t, :] for t in range(PACK)]
 
         def first_product(t):
-            first[t] = tile("first%d" % t, [P, S], F32, "staged%d" % t if t < 3 else None)
             for u, cols in enumerate(halves):
-                acc = bank("a_%d_%d" % (t, u), 4 + 2 * (t % 2) + u)
+                acc = bank("a_%d_%d" % (t, u), 2 * t + u)
                 for a in range(2):
                     nc.tensor.matmul_mx(
                         out=acc[:], lhsT=w1_dealt[:, a, 2 * P * t : 2 * P * (t + 1)].bitcast(FP4X4),
@@ -220,51 +214,59 @@ def tile_list_woven_tile_denoise_kernel(
                         rhs_scale=(v_scales, v_scales_1)[a][:, cols],
                         start=(a == 0), stop=(a == 1))
                 nc.scalar.copy(first[t][:, cols], acc[:])
-            nc.gpsimd.tensor_tensor(first[t][:], first[t][:], gain1[t][:], ALU.mult)
+
+        def log_magnitudes(pair):
+            for t in (2 * pair, 2 * pair + 1):
+                shrink[t] = tile("shrink%d" % t, [P, S], F32)
+                for u, cols in enumerate(halves):
+                    acc = bank("b_%d_%d" % (t, u), 2 * t + u)
+                    for a in range(2):
+                        rows = slice(H * a + P * t, H * a + P * (t + 1))
+                        nc.tensor.matmul_mx(out=acc[:], lhsT=w2_codes[:, rows].bitcast(FP8X4), lhsT_scale=w2_scales[:, rows],
+                                            rhs=v_words[a][:, cols].bitcast(FP8X4), rhs_scale=v_scales[4 * a : P, cols],
+                                            start=(a == 0), stop=(a == 1))
+                    nc.scalar.activation(shrink[t][:, cols], acc[:], ACT.Abs)
+            for t in (2 * pair, 2 * pair + 1):
+                nc.scalar.activation(shrink[t][:], shrink[t][:], ACT.Ln, bias=TINY)
 
         def first_values(t):
-            nc.scalar.activation(shrink[t], shrink[t], ACT.Sigmoid, bias=neg_log_level[:, t : t + 1], scale=2.0)
-            nc.gpsimd.tensor_tensor(first[t][:], first[t][:], shrink[t], ALU.mult)
+            nc.scalar.activation(shrink[t][:], shrink[t][:], ACT.Sigmoid, bias=neg_log_level[:, t : t + 1], scale=2.0)
+            for cols in halves:
+                nc.gpsimd.tensor_tensor(first[t][:, cols], first[t][:, cols], gain1[t][:, cols], ALU.mult)
+            for cols in halves:
+                nc.gpsimd.tensor_tensor(first[t][:, cols], first[t][:, cols], shrink[t][:, cols], ALU.mult)
 
-        def place_first(t):
-            nc.vector.tensor_copy(page[t][:].indirect(list3[:]), first[t][:])
-
-        shrinkage(0)
-        second_values(2, "gain2_1")
-        place_second(2, None)
-        first_product(0)
+        for t in range(PACK):
+            first_product(t)
+        log_magnitudes(0)
         first_values(0)
-        first_product(1)
         first_values(1)
-        shrinkage(1)
-        first_product(2)
+        log_magnitudes(1)
         first_values(2)
-        second_values(3, "gain1_2")
-        first_product(3)
+        late = tile("late", [P, BANK], F32, "shrink2")
+        second_values(3, halves[1], late[:])
         first_values(3)
 
         z_woven = tile("z_woven", [P, T2, PACK], BF16)
-
-        z_pair = tile("z_pair", [P, 2, T2], BF16)
+        z_pair = tile("z_pair", [P, 2, T2], BF16, "tab2_w")
         for t in range(2):
-            place_first(t)
+            place(t, list3, whole, first[t])
             nc.scalar.activation(z_pair[:, t, :], page[t][:], ACT.Relu)
         nc.scalar.copy(z_woven[:, :, 0:2], z_pair[:].rearrange("p t m -> p m t"))
-        place_first(2)
+        place(2, list3, whole, first[2])
         nc.scalar.activation(z_woven[:, :, 2:4], page[2][:].unsqueeze(2).to_broadcast([P, T2, 2]), ACT.Relu)
 
-        w4_dealt = tile("w4_dealt", [P, N], I32, "gain1_3")
+        w4_dealt = tile("w4_dealt", [P, N], I32)
         nc.gpsimd.tensor_copy(
             w4_dealt[:].rearrange("p (t m) -> p t m", t=PACK),
             w4_raw[:].rearrange("p (m t) -> p t m", t=PACK))
-        w4_dealt_scales = tile("w4_dealt_scales", [P, N], U8, "logs1")
+        w4_dealt_scales = tile("w4_dealt_scales", [P, N], U8)
         nc.gpsimd.tensor_copy(
             w4_dealt_scales[:].rearrange("p (t m) -> p t m", t=PACK),
             w4_plane[:].rearrange("p (m t) -> p t m", t=PACK))
 
-        place_second(3, "staged2")
-        place_first(3)
-
+        place(3, list4, halves[1], late[:])
+        place(3, list3, whole, first[3])
         z_codes = tile("z_codes", [P, T2], U32)
         z_scales = tile("z_scales", [P, T2], U8)
         y_codes = tile("y_codes", [P, T2], I32)
@@ -289,7 +291,7 @@ def tile_list_woven_tile_denoise_kernel(
         def multiply(c):
             width = CHUNKS[c]
             cols = slice(starts[c], starts[c] + width)
-            y = tile("y%d" % c, [P, PACK, width], F32, ("gain1_0", "w3_raw", "w2_raw0", "logs0", "gain1_1")[c])
+            y = tile("y%d" % c, [P, PACK, width], F32, ("gain1_0", "w2_raw0", "w2_raw1", "tab_w1", "gain1_1")[c])
             for t in range(PACK):
                 rows = slice(P * t, P * (t + 1))
                 acc = bank("y_%d_%d" % (c, t), (4 * c + t) % 8)
@@ -297,8 +299,10 @@ def tile_list_woven_tile_denoise_kernel(
                                     rhs=z_codes[:, cols].bitcast(FP8X4), rhs_scale=z_scales[:, cols],
                                     start=True, stop=True)
                 nc.scalar.copy(y[:, t, :], acc[:, :width])
-                if t % 2 == 1:
-                    nc.sync.dma_start(out_rows[:, t - 1 : t + 1, cols], y[:, t - 1 : t + 1, :])
+                rows_a_store = PACK if c == len(CHUNKS) - 1 else 2
+                if (t + 1) % rows_a_store == 0:
+                    stored = slice(t + 1 - rows_a_store, t + 1)
+                    nc.sync.dma_start(out_rows[:, stored, cols], y[:, stored, :])
             y_tiles[c] = y
 
         def weave_y(c):
@@ -313,21 +317,28 @@ def tile_list_woven_tile_denoise_kernel(
         def quantise_y(c, woven):
             cols = slice(starts[c], starts[c] + CHUNKS[c])
             nc.vector.quantize_mx(out=y_codes[:, cols].bitcast(FP8X4), scales=y_scales[:, cols], in_=woven[:])
-            nc.sync.dma_start(out_words[:, cols], y_codes[:, cols])
+            if c == len(CHUNKS) - 1:
+                cols = slice(starts[c - 1], T2)
+            if c != len(CHUNKS) - 2:
+                nc.sync.dma_start(out_words[:, cols], y_codes[:, cols])
+
+        def store_scales(cols):
+            for q in range(4):
+                (nc.scalar, nc.sync)[q % 2].dma_start(
+                    out_2[0, 4 * q : 4 * q + 4, cols].bitcast(I32), y_scales[32 * q : 32 * q + 4, cols].bitcast(I32))
 
         count = len(CHUNKS)
         make_z(count - 2)
-        make_z(0)
         woven = {}
         for c in range(count + 2):
-            if c + 1 < count and c + 1 != count - 2:
-                make_z(c + 1)
+            if c < count:
+                if c != count - 2:
+                    make_z(c)
+            if 1 <= c <= count:
+                woven[c - 1] = weave_y(c - 1)
             if c < count:
                 quantise_z(c)
                 multiply(c)
-            if 1 <= c <= count:
-                woven[c - 1] = weave_y(c - 1)
             if c >= 2:
                 quantise_y(c - 2, woven[c - 2])
-        for q in range(4):
-            (nc.scalar, nc.sync)[q % 2].dma_start(out_2[0, 4 * q : 4 * q + 4, :].bitcast(I32), y_scales[32 * q : 32 * q + 4, :].bitcast(I32))
+        store_scales(slice(0, T2))

@@ -80,21 +80,23 @@ def tile_list_woven_tile_denoise_kernel(
             nc.vector.tensor_copy(picked[:], window.indirect(offsets[:]))
             return picked
 
-        def quantise_weight(name, passes, codes_on=None):
+        def quantise_weight(name, passes, codes_on=None, shared=False):
             woven = tile(name + "_bf", [P, len(passes), H * PACK], BF16)
             for a, raw in enumerate(passes):
-                nc.scalar.copy(
-                    woven[:, a, :].rearrange("p (t m i) -> p m t i", t=PACK, i=PACK),
-                    raw[:].rearrange("p i (m t) -> p m t i", t=PACK),
-                )
+                dealt = woven[:, a, :].rearrange("p (t m i) -> p m t i", t=PACK, i=PACK)
+                given = raw[:].rearrange("p i (m t) -> p m t i", t=PACK)
+                if shared:
+                    nc.scalar.copy(dealt[:, :, 0:2], given[:, :, 0:2])
+                    nc.gpsimd.tensor_scalar(dealt[:, :, 2:4], given[:, :, 2:4], 1.0, 0.0, ALU.mult, ALU.add)
+                else:
+                    nc.scalar.copy(dealt, given)
             codes = tile(name + "_codes", [P, len(passes) * H], U32, codes_on)
             scales = tile(name + "_scales", [P, len(passes) * H], U8)
             nc.vector.quantize_mx(out=codes[:].bitcast(FP8X4), scales=scales[:],
                                   in_=woven[:].rearrange("p a c -> p (a c)"))
             return codes, scales
 
-        tab_plane = zeroed_plane("tab_plane", T)
-        v_scales_1 = zeroed_plane("v_scales_1", S)
+        v_scales = zeroed_plane("v_scales", 2 * S)
         w1_plane = zeroed_plane("w1_plane", 2 * H)
         w4_plane = zeroed_plane("w4_plane", N)
 
@@ -107,31 +109,54 @@ def tile_list_woven_tile_denoise_kernel(
         level_t = tile("level_t", [P, PACK], F32)
         nc.sync.dma_start(level_t[:], level.rearrange("(p t) -> p t", t=PACK))
         tab2_w = load_words("tab2_w", tab2_words[0])
-        w3_raw = load_weight("w3_raw", w3)
         list1 = load_list("list1", offs)
-        for q in range(4):
-            nc.sync.dma_start(tab_plane[32 * q : 32 * q + 8, :].bitcast(I32),
-                              tab_scales[:, 4 * q : 4 * q + 4, :].bitcast(I32))
-        tab_w = [load_words("tab_w0", tab_words[0])]
-        load_prev(0, halves[0])
-        tab_w.append(load_words("tab_w1", tab_words[1]))
-        load_gain(gain2, wg2, 0, halves[0])
+        tab_rows = tile("tab_rows", [P, T], U8)
+        nc.sync.dma_start(
+            tab_rows[:].bitcast(I32),
+            tab_scales.rearrange("a q c -> (a q) c").bitcast(I32).unsqueeze(1).to_broadcast([32, 4, T // 4]))
+        w3_raw = load_weight("w3_raw", w3)
         w1_raw = tile("w1_raw", [P, 2, 2 * H], U8)
         nc.sync.dma_start(w1_raw[:].bitcast(I32), w1_words.rearrange("a p c -> p a c").bitcast(I32))
-        list4 = load_list("list4", offs4)
-        load_prev(0, halves[1])
-        load_gain(gain2, wg2, 0, halves[1])
+        tab_w = [load_words("tab_w0", tab_words[0])]
         for q in range(4):
             nc.sync.dma_start(
                 w1_plane[32 * q : 32 * q + 4, :].rearrange("p (a c) -> p a c", a=2).bitcast(I32),
                 w1_scales[:, 4 * q : 4 * q + 4, :].rearrange("a r c -> r a c").bitcast(I32))
-        load_prev(1, halves[0])
-        load_gain(gain2, wg2, 1, halves[0])
-        w2_raw = [load_weight("w2_raw%d" % a, w2[512 * a : 512 * (a + 1), :]) for a in range(2)]
+        load_prev(0, whole)
+        tab_w.append(load_words("tab_w1", tab_words[1]))
+        load_gain(gain2, wg2, 0, whole)
+        list4 = load_list("list4", offs4)
+
+        log_level = tile("log_level", [P, PACK], F32)
+        nc.scalar.activation(log_level[:], level_t[:], ACT.Ln)
+        neg_log_level = tile("neg_log_level", [P, PACK], F32)
+        nc.scalar.mul(neg_log_level[:], log_level[:], -1.0)
+
+        v2_scales = gather("v2_scales", tab2_plane[:], list2, U8)
+        v2_words = gather("v2_words", tab2_w[:].bitcast(U32), list2, U32, "tab2_plane")
+        v_rows = gather("v_rows", tab_rows[:], list1, U8)
+        w3_codes, w3_scales = quantise_weight("w3", [w3_raw], "tab_rows", shared=True)
+        w1_dealt = tile("w1_dealt", [P, 2, 2 * H], U8, "w3_bf")
+        nc.vector.tensor_copy(
+            w1_dealt[:].bitcast(U16).rearrange("p a (t m) -> p a t m", t=PACK),
+            w1_raw[:].bitcast(U16).rearrange("p a (m t) -> p a t m", t=PACK))
+        v_words = [gather("v_words0", tab_w[0][:].bitcast(U32), list1, U32, "w1_raw")]
+        v_words.append(gather("v_words1", tab_w[1][:].bitcast(U32), list1, U32))
+
+        def seat_scales(a):
+            for q in range(4):
+                start = 64 * a + 16 * q
+                nc.sync.dma_start(v_scales[32 * q : 32 * q + 4, S * a : S * (a + 1)].bitcast(I32),
+                                  v_rows[start : start + 16 : 4, :].bitcast(I32))
+
+        load_prev(1, whole)
+        seat_scales(0)
+        load_gain(gain2, wg2, 1, whole)
+        w2_raw = [load_weight("w2_raw0", w2[0:512, :])]
+        seat_scales(1)
+        w2_raw.append(load_weight("w2_raw1", w2[512:1024, :]))
         load_prev(2, whole)
         load_gain(gain2, wg2, 2, whole)
-        load_prev(1, halves[1])
-        load_gain(gain2, wg2, 1, halves[1])
         list3 = load_list("list3", offs3)
         load_prev(3, whole)
         load_gain(gain2, wg2, 3, whole)
@@ -142,22 +167,11 @@ def tile_list_woven_tile_denoise_kernel(
             nc.sync.dma_start(w4_plane[32 * q : 32 * q + 4, :].bitcast(I32),
                               w4_scales[0, 4 * q : 4 * q + 4, :].bitcast(I32))
 
-        log_level = tile("log_level", [P, PACK], F32)
-        nc.scalar.activation(log_level[:], level_t[:], ACT.Ln)
-        neg_log_level = tile("neg_log_level", [P, PACK], F32)
-        nc.scalar.mul(neg_log_level[:], log_level[:], -1.0)
 
-        v2_scales = gather("v2_scales", tab2_plane[:], list2, U8)
-        v2_words = gather("v2_words", tab2_w[:].bitcast(U32), list2, U32, "tab2_plane")
-        v_scales = gather("v_scales", tab_plane[:], list1, U8)
-        nc.gpsimd.dma_start(v_scales_1[0:112, :].bitcast(I32), v_scales[4:116, :].bitcast(I32))
-        w3_codes, w3_scales = quantise_weight("w3", [w3_raw], "tab_plane")
-        v_words = [gather("v_words0", tab_w[0][:].bitcast(U32), list1, U32, "w3_bf")]
-        v_words.append(gather("v_words1", tab_w[1][:].bitcast(U32), list1, U32))
-        w1_dealt = tile("w1_dealt", [P, 2, 2 * H], U8)
-        nc.vector.tensor_copy(
-            w1_dealt[:].bitcast(U16).rearrange("p a (t m) -> p a t m", t=PACK),
-            w1_raw[:].bitcast(U16).rearrange("p a (m t) -> p a t m", t=PACK))
+        w1_dealt_scales = tile("w1_dealt_scales", [P, 2 * H], U8)
+        nc.gpsimd.tensor_copy(
+            w1_dealt_scales[:].rearrange("p (a t m) -> p a t m", a=2, t=PACK),
+            w1_plane[:].rearrange("p (a m t) -> p a t m", a=2, t=PACK))
 
         page, second, shrink = {}, {}, {}
 
@@ -173,13 +187,13 @@ def tile_list_woven_tile_denoise_kernel(
 
         def second_values(t, cols, into=None):
             into = second[t][:, cols] if into is None else into
-            nc.gpsimd.tensor_tensor(into, second[t][:, cols], earlier[t][:, cols], ALU.add)
-            nc.gpsimd.tensor_tensor(into, into, gain2[t][:, cols], ALU.mult)
+            nc.gpsimd.tensor_tensor(second[t][:, cols], second[t][:, cols], earlier[t][:, cols], ALU.add)
+            nc.gpsimd.tensor_tensor(into, second[t][:, cols], gain2[t][:, cols], ALU.mult)
             return into
 
         def place(t, offsets, cols, values):
             if t not in page:
-                page[t] = tile("page%d" % t, [P, T2], F32, ("w1_raw", "tab_w0", "w2_bf", "w3_raw")[t])
+                page[t] = tile("page%d" % t, [P, T2], F32, ("tab_w1", "tab_w0", "w2_bf", "w3_raw")[t])
             nc.vector.tensor_copy(page[t][:].indirect(offsets[:, cols.start // 16 : cols.stop // 16]), values)
 
 
@@ -188,20 +202,17 @@ def tile_list_woven_tile_denoise_kernel(
         for cols in halves:
             place(0, list4, cols, second_values(0, cols))
 
-        w1_dealt_scales = tile("w1_dealt_scales", [P, 2 * H], U8)
-        nc.gpsimd.tensor_copy(
-            w1_dealt_scales[:].rearrange("p (a t m) -> p a t m", a=2, t=PACK),
-            w1_plane[:].rearrange("p (a m t) -> p a t m", a=2, t=PACK))
 
         place(1, list4, halves[0], second_values(1, halves[0]))
         w2_codes, w2_scales = quantise_weight("w2", w2_raw)
+        firsts = tile("firsts", [P, PACK * S + BANK], F32, "w2_raw1")
+        first = [firsts[:, S * t : S * (t + 1)] for t in range(PACK)]
+        place(1, list4, halves[1], second_values(1, halves[1], firsts[:, PACK * S :]))
         for cols in halves:
-            place(2, list4, cols, second_values(2, cols))
-        place(1, list4, halves[1], second_values(1, halves[1]))
+            second_values(2, cols)
+        place(2, list4, whole, second[2][:])
         place(3, list4, halves[0], second_values(3, halves[0]))
 
-        firsts = tile("firsts", [P, PACK, S], F32, "w2_raw1")
-        first = [firsts[:, t, :] for t in range(PACK)]
 
         def first_product(t):
             for u, cols in enumerate(halves):
@@ -211,26 +222,32 @@ def tile_list_woven_tile_denoise_kernel(
                         out=acc[:], lhsT=w1_dealt[:, a, 2 * P * t : 2 * P * (t + 1)].bitcast(FP4X4),
                         lhsT_scale=w1_dealt_scales[:, H * a + P * t : H * a + P * (t + 1)],
                         rhs=v_words[a][:, cols].bitcast(FP8X4),
-                        rhs_scale=(v_scales, v_scales_1)[a][:, cols],
+                        rhs_scale=v_scales[:, S * a + cols.start : S * a + cols.stop],
                         start=(a == 0), stop=(a == 1))
                 nc.scalar.copy(first[t][:, cols], acc[:])
 
         def log_magnitudes(pair):
+            sizes = tile("sizes%d" % pair, [P, 2, S], F32, "sizes")
             for t in (2 * pair, 2 * pair + 1):
-                shrink[t] = tile("shrink%d" % t, [P, S], F32)
                 for u, cols in enumerate(halves):
                     acc = bank("b_%d_%d" % (t, u), 2 * t + u)
                     for a in range(2):
                         rows = slice(H * a + P * t, H * a + P * (t + 1))
                         nc.tensor.matmul_mx(out=acc[:], lhsT=w2_codes[:, rows].bitcast(FP8X4), lhsT_scale=w2_scales[:, rows],
-                                            rhs=v_words[a][:, cols].bitcast(FP8X4), rhs_scale=v_scales[4 * a : P, cols],
+                                            rhs=v_words[a][:, cols].bitcast(FP8X4), rhs_scale=v_scales[:, S * a + cols.start : S * a + cols.stop],
                                             start=(a == 0), stop=(a == 1))
-                    nc.scalar.activation(shrink[t][:, cols], acc[:], ACT.Abs)
-            for t in (2 * pair, 2 * pair + 1):
-                nc.scalar.activation(shrink[t][:], shrink[t][:], ACT.Ln, bias=TINY)
+                    nc.scalar.activation(sizes[:, t % 2, cols], acc[:], ACT.Abs)
+            if pair == 0:
+                logs = tile("logs", [P, 2, S], F32)
+                nc.scalar.activation(logs[:], sizes[:], ACT.Ln, bias=TINY)
+                shrink[0], shrink[1] = logs[:, 0, :], logs[:, 1, :]
+            else:
+                for t in (2, 3):
+                    shrink[t] = tile("shrink%d" % t, [P, S], F32)[:]
+                    nc.scalar.activation(shrink[t], sizes[:, t % 2, :], ACT.Ln, bias=TINY)
 
         def first_values(t):
-            nc.scalar.activation(shrink[t][:], shrink[t][:], ACT.Sigmoid, bias=neg_log_level[:, t : t + 1], scale=2.0)
+            nc.scalar.activation(shrink[t], shrink[t], ACT.Sigmoid, bias=neg_log_level[:, t : t + 1], scale=2.0)
             for cols in halves:
                 nc.gpsimd.tensor_tensor(first[t][:, cols], first[t][:, cols], gain1[t][:, cols], ALU.mult)
             for cols in halves:
@@ -291,7 +308,7 @@ def tile_list_woven_tile_denoise_kernel(
         def multiply(c):
             width = CHUNKS[c]
             cols = slice(starts[c], starts[c] + width)
-            y = tile("y%d" % c, [P, PACK, width], F32, ("gain1_0", "w2_raw0", "w2_raw1", "tab_w1", "gain1_1")[c])
+            y = tile("y%d" % c, [P, PACK, width], F32, ("gain1_0", "w2_raw0", "w2_raw1", "y3", "gain1_1")[c])
             for t in range(PACK):
                 rows = slice(P * t, P * (t + 1))
                 acc = bank("y_%d_%d" % (c, t), (4 * c + t) % 8)

@@ -80,12 +80,12 @@ def tile_list_woven_tile_denoise_kernel(
             nc.vector.tensor_copy(picked[:], window.indirect(offsets[:]))
             return picked
 
-        def quantise_weight(name, passes, codes_on=None, shared=False):
+        def quantise_weight(name, passes, codes_on=None):
             woven = tile(name + "_bf", [P, len(passes), H * PACK], BF16)
             for a, raw in enumerate(passes):
                 dealt = woven[:, a, :].rearrange("p (t m i) -> p m t i", t=PACK, i=PACK)
                 given = raw[:].rearrange("p i (m t) -> p m t i", t=PACK)
-                if shared:
+                if a == len(passes) - 1:
                     nc.scalar.copy(dealt[:, :, 0:2], given[:, :, 0:2])
                     nc.gpsimd.tensor_scalar(dealt[:, :, 2:4], given[:, :, 2:4], 1.0, 0.0, ALU.mult, ALU.add)
                 else:
@@ -106,8 +106,6 @@ def tile_list_woven_tile_denoise_kernel(
             rows = tab2_scales[0, 4 * q : 4 * q + 4, :].bitcast(I32)
             nc.sync.dma_start(tab2_plane[32 * q : 32 * q + 32, :].bitcast(I32),
                               rows.unsqueeze(0).to_broadcast([8, 4, T // 4]))
-        level_t = tile("level_t", [P, PACK], F32)
-        nc.sync.dma_start(level_t[:], level.rearrange("(p t) -> p t", t=PACK))
         tab2_w = load_words("tab2_w", tab2_words[0])
         list1 = load_list("list1", offs)
         tab_rows = tile("tab_rows", [P, T], U8)
@@ -122,9 +120,11 @@ def tile_list_woven_tile_denoise_kernel(
             nc.sync.dma_start(
                 w1_plane[32 * q : 32 * q + 4, :].rearrange("p (a c) -> p a c", a=2).bitcast(I32),
                 w1_scales[:, 4 * q : 4 * q + 4, :].rearrange("a r c -> r a c").bitcast(I32))
-        load_prev(0, whole)
+        load_prev(0, halves[0])
         tab_w.append(load_words("tab_w1", tab_words[1]))
-        load_gain(gain2, wg2, 0, whole)
+        load_gain(gain2, wg2, 0, halves[0])
+        level_t = tile("level_t", [P, PACK], F32)
+        nc.sync.dma_start(level_t[:], level.rearrange("(p t) -> p t", t=PACK))
         list4 = load_list("list4", offs4)
 
         log_level = tile("log_level", [P, PACK], F32)
@@ -135,7 +135,7 @@ def tile_list_woven_tile_denoise_kernel(
         v2_scales = gather("v2_scales", tab2_plane[:], list2, U8)
         v2_words = gather("v2_words", tab2_w[:].bitcast(U32), list2, U32, "tab2_plane")
         v_rows = gather("v_rows", tab_rows[:], list1, U8)
-        w3_codes, w3_scales = quantise_weight("w3", [w3_raw], "tab_rows", shared=True)
+        w3_codes, w3_scales = quantise_weight("w3", [w3_raw], "tab_rows")
         w1_dealt = tile("w1_dealt", [P, 2, 2 * H], U8, "w3_bf")
         nc.vector.tensor_copy(
             w1_dealt[:].bitcast(U16).rearrange("p a (t m) -> p a t m", t=PACK),
@@ -149,12 +149,16 @@ def tile_list_woven_tile_denoise_kernel(
                 nc.sync.dma_start(v_scales[32 * q : 32 * q + 4, S * a : S * (a + 1)].bitcast(I32),
                                   v_rows[start : start + 16 : 4, :].bitcast(I32))
 
-        load_prev(1, whole)
-        seat_scales(0)
-        load_gain(gain2, wg2, 1, whole)
+        load_prev(0, halves[1])
+        load_gain(gain2, wg2, 0, halves[1])
+        load_prev(1, halves[0])
+        load_gain(gain2, wg2, 1, halves[0])
         w2_raw = [load_weight("w2_raw0", w2[0:512, :])]
-        seat_scales(1)
+        seat_scales(0)
         w2_raw.append(load_weight("w2_raw1", w2[512:1024, :]))
+        seat_scales(1)
+        load_prev(1, halves[1])
+        load_gain(gain2, wg2, 1, halves[1])
         load_prev(2, whole)
         load_gain(gain2, wg2, 2, whole)
         list3 = load_list("list3", offs3)
@@ -209,8 +213,7 @@ def tile_list_woven_tile_denoise_kernel(
         first = [firsts[:, S * t : S * (t + 1)] for t in range(PACK)]
         place(1, list4, halves[1], second_values(1, halves[1], firsts[:, PACK * S :]))
         for cols in halves:
-            second_values(2, cols)
-        place(2, list4, whole, second[2][:])
+            place(2, list4, cols, second_values(2, cols))
         place(3, list4, halves[0], second_values(3, halves[0]))
 
 
@@ -334,9 +337,9 @@ def tile_list_woven_tile_denoise_kernel(
         def quantise_y(c, woven):
             cols = slice(starts[c], starts[c] + CHUNKS[c])
             nc.vector.quantize_mx(out=y_codes[:, cols].bitcast(FP8X4), scales=y_scales[:, cols], in_=woven[:])
-            if c == len(CHUNKS) - 1:
-                cols = slice(starts[c - 1], T2)
-            if c != len(CHUNKS) - 2:
+            if c == len(CHUNKS) - 2:
+                cols = slice(starts[c - 1], cols.stop)
+            if c != len(CHUNKS) - 3:
                 nc.sync.dma_start(out_words[:, cols], y_codes[:, cols])
 
         def store_scales(cols):

@@ -20,6 +20,7 @@ P = 128
 PACK = 4
 BANK = 512
 TINY = 2.0 ** -63
+EARLY = 768
 CHUNKS = (256, 512, 512, 512, 256)
 
 
@@ -36,6 +37,7 @@ def tile_list_woven_tile_denoise_kernel(
 
         halves = [slice(BANK * u, BANK * (u + 1)) for u in range(S // BANK)]
         whole = slice(0, S)
+        early_part, late_part = slice(0, EARLY), slice(EARLY, S)
 
         def tile(name, shape, dtype, on=None):
             return keep.tile(shape, dtype, name=name, tag=on or name, align_bytes=64)
@@ -96,17 +98,20 @@ def tile_list_woven_tile_denoise_kernel(
                                   in_=woven[:].rearrange("p a c -> p (a c)"))
             return codes, scales
 
-        v_scales = zeroed_plane("v_scales", 2 * S)
         w1_plane = zeroed_plane("w1_plane", 2 * H)
+        v2_scales = zeroed_plane("v2_scales", S)
+        v_scales = zeroed_plane("v_scales", 2 * S)
         w4_plane = zeroed_plane("w4_plane", N)
 
         list2 = load_list("list2", offs2)
-        tab2_plane = tile("tab2_plane", [P, T], U8)
-        for q in (0, 2, 1, 3):
-            rows = tab2_scales[0, 4 * q : 4 * q + 4, :].bitcast(I32)
-            nc.sync.dma_start(tab2_plane[32 * q : 32 * q + 32, :].bitcast(I32),
-                              rows.unsqueeze(0).to_broadcast([8, 4, T // 4]))
+        tab2_rows = tile("tab2_rows", [P, T], U8)
+        nc.sync.dma_start(tab2_rows[:].bitcast(I32),
+                          tab2_scales[0].bitcast(I32).unsqueeze(1).to_broadcast([16, 8, T // 4]))
         tab2_w = load_words("tab2_w", tab2_words[0])
+        for q in range(4):
+            nc.sync.dma_start(
+                w1_plane[32 * q : 32 * q + 4, :].rearrange("p (a c) -> p a c", a=2).bitcast(I32),
+                w1_scales[:, 4 * q : 4 * q + 4, :].rearrange("a r c -> r a c").bitcast(I32))
         list1 = load_list("list1", offs)
         tab_rows = tile("tab_rows", [P, T], U8)
         nc.sync.dma_start(
@@ -115,11 +120,11 @@ def tile_list_woven_tile_denoise_kernel(
         w3_raw = load_weight("w3_raw", w3)
         w1_raw = tile("w1_raw", [P, 2, 2 * H], U8)
         nc.sync.dma_start(w1_raw[:].bitcast(I32), w1_words.rearrange("a p c -> p a c").bitcast(I32))
-        tab_w = [load_words("tab_w0", tab_words[0])]
+        v2_rows = gather("v2_rows", tab2_rows[:], list2, U8)
         for q in range(4):
-            nc.sync.dma_start(
-                w1_plane[32 * q : 32 * q + 4, :].rearrange("p (a c) -> p a c", a=2).bitcast(I32),
-                w1_scales[:, 4 * q : 4 * q + 4, :].rearrange("a r c -> r a c").bitcast(I32))
+            nc.sync.dma_start(v2_scales[32 * q : 32 * q + 4, :].bitcast(I32),
+                              v2_rows[32 * q : 32 * q + 32 : 8, :].bitcast(I32))
+        tab_w = [load_words("tab_w0", tab_words[0])]
         load_prev(0, halves[0])
         tab_w.append(load_words("tab_w1", tab_words[1]))
         load_gain(gain2, wg2, 0, halves[0])
@@ -132,8 +137,11 @@ def tile_list_woven_tile_denoise_kernel(
         neg_log_level = tile("neg_log_level", [P, PACK], F32)
         nc.scalar.mul(neg_log_level[:], log_level[:], -1.0)
 
-        v2_scales = gather("v2_scales", tab2_plane[:], list2, U8)
-        v2_words = gather("v2_words", tab2_w[:].bitcast(U32), list2, U32, "tab2_plane")
+        w1_dealt_scales = tile("w1_dealt_scales", [P, 2 * H], U8)
+        nc.gpsimd.tensor_copy(
+            w1_dealt_scales[:].rearrange("p (a t m) -> p a t m", a=2, t=PACK),
+            w1_plane[:].rearrange("p (a m t) -> p a t m", a=2, t=PACK))
+        v2_words = gather("v2_words", tab2_w[:].bitcast(U32), list2, U32, "tab2_rows")
         v_rows = gather("v_rows", tab_rows[:], list1, U8)
         w3_codes, w3_scales = quantise_weight("w3", [w3_raw], "tab_rows")
         w1_dealt = tile("w1_dealt", [P, 2, 2 * H], U8, "w3_bf")
@@ -172,11 +180,6 @@ def tile_list_woven_tile_denoise_kernel(
                               w4_scales[0, 4 * q : 4 * q + 4, :].bitcast(I32))
 
 
-        w1_dealt_scales = tile("w1_dealt_scales", [P, 2 * H], U8)
-        nc.gpsimd.tensor_copy(
-            w1_dealt_scales[:].rearrange("p (a t m) -> p a t m", a=2, t=PACK),
-            w1_plane[:].rearrange("p (a m t) -> p a t m", a=2, t=PACK))
-
         page, second, shrink = {}, {}, {}
 
         def second_product(t):
@@ -214,7 +217,7 @@ def tile_list_woven_tile_denoise_kernel(
         place(1, list4, halves[1], second_values(1, halves[1], firsts[:, PACK * S :]))
         for cols in halves:
             place(2, list4, cols, second_values(2, cols))
-        place(3, list4, halves[0], second_values(3, halves[0]))
+        place(3, list4, early_part, second_values(3, early_part))
 
 
         def first_product(t):
@@ -251,10 +254,8 @@ def tile_list_woven_tile_denoise_kernel(
 
         def first_values(t):
             nc.scalar.activation(shrink[t], shrink[t], ACT.Sigmoid, bias=neg_log_level[:, t : t + 1], scale=2.0)
-            for cols in halves:
-                nc.gpsimd.tensor_tensor(first[t][:, cols], first[t][:, cols], gain1[t][:, cols], ALU.mult)
-            for cols in halves:
-                nc.gpsimd.tensor_tensor(first[t][:, cols], first[t][:, cols], shrink[t][:, cols], ALU.mult)
+            nc.gpsimd.tensor_tensor(first[t], first[t], gain1[t][:], ALU.mult)
+            nc.gpsimd.tensor_tensor(first[t], first[t], shrink[t], ALU.mult)
 
         for t in range(PACK):
             first_product(t)
@@ -263,16 +264,14 @@ def tile_list_woven_tile_denoise_kernel(
         first_values(1)
         log_magnitudes(1)
         first_values(2)
-        late = tile("late", [P, BANK], F32, "shrink2")
-        second_values(3, halves[1], late[:])
+        late = tile("late", [P, S - EARLY], F32, "shrink2")
+        second_values(3, late_part, late[:])
         first_values(3)
 
         z_woven = tile("z_woven", [P, T2, PACK], BF16)
-        z_pair = tile("z_pair", [P, 2, T2], BF16, "tab2_w")
         for t in range(2):
             place(t, list3, whole, first[t])
-            nc.scalar.activation(z_pair[:, t, :], page[t][:], ACT.Relu)
-        nc.scalar.copy(z_woven[:, :, 0:2], z_pair[:].rearrange("p t m -> p m t"))
+            nc.scalar.activation(z_woven[:, :, t], page[t][:], ACT.Relu)
         place(2, list3, whole, first[2])
         nc.scalar.activation(z_woven[:, :, 2:4], page[2][:].unsqueeze(2).to_broadcast([P, T2, 2]), ACT.Relu)
 
@@ -285,7 +284,7 @@ def tile_list_woven_tile_denoise_kernel(
             w4_dealt_scales[:].rearrange("p (t m) -> p t m", t=PACK),
             w4_plane[:].rearrange("p (m t) -> p t m", t=PACK))
 
-        place(3, list4, halves[1], late[:])
+        place(3, list4, late_part, late[:])
         place(3, list3, whole, first[3])
         z_codes = tile("z_codes", [P, T2], U32)
         z_scales = tile("z_scales", [P, T2], U8)

@@ -20,7 +20,7 @@ P = 128
 PACK = 4
 BANK = 512
 TINY = 2.0 ** -63
-EARLY = 768
+OVERLAID = {"w3_raw": 0, "w1_dealt": 0, "v_words0": 2048}
 CHUNKS = (256, 512, 512, 512, 256)
 
 
@@ -33,13 +33,15 @@ def tile_list_woven_tile_denoise_kernel(
     with ExitStack() as ctx:
         lists = ctx.enter_context(tc.tile_pool(name="lists", bufs=1))
         keep = ctx.enter_context(tc.tile_pool(name="keep", bufs=1))
+        overlay = ctx.enter_context(tc.tile_pool(name="overlay", bufs=1))
         psum = ctx.enter_context(tc.psum_pool(name="psum", bufs=1))
 
         halves = [slice(BANK * u, BANK * (u + 1)) for u in range(S // BANK)]
         whole = slice(0, S)
-        early_part, late_part = slice(0, EARLY), slice(EARLY, S)
 
         def tile(name, shape, dtype, on=None):
+            if name in OVERLAID:
+                return overlay.tile(shape, dtype, name=name, align_bytes=64, offset=OVERLAID[name])
             return keep.tile(shape, dtype, name=name, tag=on or name, align_bytes=64)
 
         def bank(name, index):
@@ -82,7 +84,7 @@ def tile_list_woven_tile_denoise_kernel(
             nc.vector.tensor_copy(picked[:], window.indirect(offsets[:]))
             return picked
 
-        def quantise_weight(name, passes, codes_on=None):
+        def quantise_weight(name, passes):
             woven = tile(name + "_bf", [P, len(passes), H * PACK], BF16)
             for a, raw in enumerate(passes):
                 dealt = woven[:, a, :].rearrange("p (t m i) -> p m t i", t=PACK, i=PACK)
@@ -92,12 +94,13 @@ def tile_list_woven_tile_denoise_kernel(
                     nc.gpsimd.tensor_scalar(dealt[:, :, 2:4], given[:, :, 2:4], 1.0, 0.0, ALU.mult, ALU.add)
                 else:
                     nc.scalar.copy(dealt, given)
-            codes = tile(name + "_codes", [P, len(passes) * H], U32, codes_on)
+            codes = tile(name + "_codes", [P, len(passes) * H], U32)
             scales = tile(name + "_scales", [P, len(passes) * H], U8)
             nc.vector.quantize_mx(out=codes[:].bitcast(FP8X4), scales=scales[:],
                                   in_=woven[:].rearrange("p a c -> p (a c)"))
             return codes, scales
 
+        tab_rows = zeroed_plane("tab_rows", T)
         w1_plane = zeroed_plane("w1_plane", 2 * H)
         v2_scales = zeroed_plane("v2_scales", S)
         v_scales = zeroed_plane("v_scales", 2 * S)
@@ -113,10 +116,7 @@ def tile_list_woven_tile_denoise_kernel(
                 w1_plane[32 * q : 32 * q + 4, :].rearrange("p (a c) -> p a c", a=2).bitcast(I32),
                 w1_scales[:, 4 * q : 4 * q + 4, :].rearrange("a r c -> r a c").bitcast(I32))
         list1 = load_list("list1", offs)
-        tab_rows = tile("tab_rows", [P, T], U8)
-        nc.sync.dma_start(
-            tab_rows[:].bitcast(I32),
-            tab_scales.rearrange("a q c -> (a q) c").bitcast(I32).unsqueeze(1).to_broadcast([32, 4, T // 4]))
+        nc.sync.dma_start(tab_rows[0:32, :].bitcast(I32), tab_scales.rearrange("a q c -> (a q) c").bitcast(I32))
         w3_raw = load_weight("w3_raw", w3)
         w1_raw = tile("w1_raw", [P, 2, 2 * H], U8)
         nc.sync.dma_start(w1_raw[:].bitcast(I32), w1_words.rearrange("a p c -> p a c").bitcast(I32))
@@ -141,34 +141,33 @@ def tile_list_woven_tile_denoise_kernel(
         nc.gpsimd.tensor_copy(
             w1_dealt_scales[:].rearrange("p (a t m) -> p a t m", a=2, t=PACK),
             w1_plane[:].rearrange("p (a m t) -> p a t m", a=2, t=PACK))
-        v2_words = gather("v2_words", tab2_w[:].bitcast(U32), list2, U32, "tab2_rows")
+        v2_words = gather("v2_words", tab2_w[:].bitcast(U32), list2, U32)
         v_rows = gather("v_rows", tab_rows[:], list1, U8)
-        w3_codes, w3_scales = quantise_weight("w3", [w3_raw], "tab_rows")
-        w1_dealt = tile("w1_dealt", [P, 2, 2 * H], U8, "w3_bf")
+        w3_codes, w3_scales = quantise_weight("w3", [w3_raw])
+        w1_dealt = tile("w1_dealt", [P, 2, 2 * H], U8)
         nc.vector.tensor_copy(
             w1_dealt[:].bitcast(U16).rearrange("p a (t m) -> p a t m", t=PACK),
             w1_raw[:].bitcast(U16).rearrange("p a (m t) -> p a t m", t=PACK))
-        v_words = [gather("v_words0", tab_w[0][:].bitcast(U32), list1, U32, "w1_raw")]
+        v_words = [gather("v_words0", tab_w[0][:].bitcast(U32), list1, U32)]
         v_words.append(gather("v_words1", tab_w[1][:].bitcast(U32), list1, U32))
 
         def seat_scales(a):
             for q in range(4):
-                start = 64 * a + 16 * q
+                start = 16 * a + 4 * q
                 nc.sync.dma_start(v_scales[32 * q : 32 * q + 4, S * a : S * (a + 1)].bitcast(I32),
-                                  v_rows[start : start + 16 : 4, :].bitcast(I32))
+                                  v_rows[start : start + 4, :].bitcast(I32))
 
-        load_prev(0, halves[1])
-        load_gain(gain2, wg2, 0, halves[1])
         load_prev(1, halves[0])
         load_gain(gain2, wg2, 1, halves[0])
+        load_prev(0, halves[1])
+        load_gain(gain2, wg2, 0, halves[1])
         w2_raw = [load_weight("w2_raw0", w2[0:512, :])]
         seat_scales(0)
         w2_raw.append(load_weight("w2_raw1", w2[512:1024, :]))
         seat_scales(1)
-        load_prev(1, halves[1])
-        load_gain(gain2, wg2, 1, halves[1])
-        load_prev(2, whole)
-        load_gain(gain2, wg2, 2, whole)
+        for t, cols in ((2, halves[0]), (1, halves[1]), (2, halves[1])):
+            load_prev(t, cols)
+            load_gain(gain2, wg2, t, cols)
         list3 = load_list("list3", offs3)
         load_prev(3, whole)
         load_gain(gain2, wg2, 3, whole)
@@ -192,32 +191,28 @@ def tile_list_woven_tile_denoise_kernel(
                                     start=True, stop=True)
                 nc.scalar.copy(second[t][:, cols], acc[:])
 
-        def second_values(t, cols, into=None):
-            into = second[t][:, cols] if into is None else into
-            nc.gpsimd.tensor_tensor(second[t][:, cols], second[t][:, cols], earlier[t][:, cols], ALU.add)
-            nc.gpsimd.tensor_tensor(into, second[t][:, cols], gain2[t][:, cols], ALU.mult)
-            return into
+        def second_values(t, cols):
+            values = second[t][:, cols]
+            nc.gpsimd.tensor_tensor(values, values, earlier[t][:, cols], ALU.add)
+            nc.gpsimd.tensor_tensor(values, values, gain2[t][:, cols], ALU.mult)
+            return values
 
         def place(t, offsets, cols, values):
             if t not in page:
-                page[t] = tile("page%d" % t, [P, T2], F32, ("tab_w1", "tab_w0", "w2_bf", "w3_raw")[t])
+                page[t] = tile("page%d" % t, [P, T2], F32, ("tab2_w", "tab_w0", "w2_raw0", "tab_w1")[t])
             nc.vector.tensor_copy(page[t][:].indirect(offsets[:, cols.start // 16 : cols.stop // 16]), values)
 
 
         for t in range(PACK):
             second_product(t)
-        for cols in halves:
-            place(0, list4, cols, second_values(0, cols))
-
-
-        place(1, list4, halves[0], second_values(1, halves[0]))
+        for t, cols in ((0, halves[0]), (1, halves[0]), (0, halves[1])):
+            place(t, list4, cols, second_values(t, cols))
         w2_codes, w2_scales = quantise_weight("w2", w2_raw)
-        firsts = tile("firsts", [P, PACK * S + BANK], F32, "w2_raw1")
+        firsts = tile("firsts", [P, PACK * S], F32, "w2_raw1")
         first = [firsts[:, S * t : S * (t + 1)] for t in range(PACK)]
-        place(1, list4, halves[1], second_values(1, halves[1], firsts[:, PACK * S :]))
-        for cols in halves:
-            place(2, list4, cols, second_values(2, cols))
-        place(3, list4, early_part, second_values(3, early_part))
+        for t, cols in ((2, halves[0]), (1, halves[1]), (2, halves[1])):
+            place(t, list4, cols, second_values(t, cols))
+        place(3, list4, whole, second_values(3, whole))
 
 
         def first_product(t):
@@ -264,8 +259,6 @@ def tile_list_woven_tile_denoise_kernel(
         first_values(1)
         log_magnitudes(1)
         first_values(2)
-        late = tile("late", [P, S - EARLY], F32, "shrink2")
-        second_values(3, late_part, late[:])
         first_values(3)
 
         z_woven = tile("z_woven", [P, T2, PACK], BF16)
@@ -273,7 +266,8 @@ def tile_list_woven_tile_denoise_kernel(
             place(t, list3, whole, first[t])
             nc.scalar.activation(z_woven[:, :, t], page[t][:], ACT.Relu)
         place(2, list3, whole, first[2])
-        nc.scalar.activation(z_woven[:, :, 2:4], page[2][:].unsqueeze(2).to_broadcast([P, T2, 2]), ACT.Relu)
+        for cols in (slice(0, T2 // 2), slice(T2 // 2, T2)):
+            nc.scalar.activation(z_woven[:, cols, 2:4], page[2][:, cols].unsqueeze(2).to_broadcast([P, T2 // 2, 2]), ACT.Relu)
 
         w4_dealt = tile("w4_dealt", [P, N], I32)
         nc.gpsimd.tensor_copy(
@@ -284,7 +278,6 @@ def tile_list_woven_tile_denoise_kernel(
             w4_dealt_scales[:].rearrange("p (t m) -> p t m", t=PACK),
             w4_plane[:].rearrange("p (m t) -> p t m", t=PACK))
 
-        place(3, list4, late_part, late[:])
         place(3, list3, whole, first[3])
         z_codes = tile("z_codes", [P, T2], U32)
         z_scales = tile("z_scales", [P, T2], U8)
@@ -310,7 +303,7 @@ def tile_list_woven_tile_denoise_kernel(
         def multiply(c):
             width = CHUNKS[c]
             cols = slice(starts[c], starts[c] + width)
-            y = tile("y%d" % c, [P, PACK, width], F32, ("gain1_0", "w2_raw0", "w2_raw1", "y3", "gain1_1")[c])
+            y = tile("y%d" % c, [P, PACK, width], F32, ("gain1_0", "w2_bf", "w2_raw1", "y3", "gain1_1")[c])
             for t in range(PACK):
                 rows = slice(P * t, P * (t + 1))
                 acc = bank("y_%d_%d" % (c, t), (4 * c + t) % 8)
@@ -318,7 +311,7 @@ def tile_list_woven_tile_denoise_kernel(
                                     rhs=z_codes[:, cols].bitcast(FP8X4), rhs_scale=z_scales[:, cols],
                                     start=True, stop=True)
                 nc.scalar.copy(y[:, t, :], acc[:, :width])
-                rows_a_store = PACK if c == len(CHUNKS) - 1 else 2
+                rows_a_store = (1, 1, 1, 2, 4)[c]
                 if (t + 1) % rows_a_store == 0:
                     stored = slice(t + 1 - rows_a_store, t + 1)
                     nc.sync.dma_start(out_rows[:, stored, cols], y[:, stored, :])

@@ -20,7 +20,7 @@ P = 128
 PACK = 4
 BANK = 512
 TINY = 2.0 ** -63
-OVERLAID = {"w3_raw": 0, "w1_dealt": 0, "v_words0": 2048}
+OVERLAID = {"w3_raw": 0, "w1_dealt": 0, "v_words0": 2048, "page2": 8192, "w2_bf": 12288, "held": 16384}
 CHUNKS = (256, 512, 512, 512, 256)
 
 
@@ -162,15 +162,16 @@ def tile_list_woven_tile_denoise_kernel(
         load_prev(0, halves[1])
         load_gain(gain2, wg2, 0, halves[1])
         w2_raw = [load_weight("w2_raw0", w2[0:512, :])]
-        seat_scales(0)
+        load_prev(2, halves[0])
+        load_gain(gain2, wg2, 2, halves[0])
         w2_raw.append(load_weight("w2_raw1", w2[512:1024, :]))
+        seat_scales(0)
         seat_scales(1)
-        for t, cols in ((2, halves[0]), (1, halves[1]), (2, halves[1])):
+        after_w2 = ((1, halves[1]), (3, halves[0]), (2, halves[1]), (3, halves[1]))
+        for t, cols in after_w2:
             load_prev(t, cols)
             load_gain(gain2, wg2, t, cols)
         list3 = load_list("list3", offs3)
-        load_prev(3, whole)
-        load_gain(gain2, wg2, 3, whole)
         for t in range(PACK):
             load_gain(gain1, wg1, t, whole)
         w4_raw = load_words("w4_raw", w4_words[0])
@@ -191,9 +192,9 @@ def tile_list_woven_tile_denoise_kernel(
                                     start=True, stop=True)
                 nc.scalar.copy(second[t][:, cols], acc[:])
 
-        def second_values(t, cols):
-            values = second[t][:, cols]
-            nc.gpsimd.tensor_tensor(values, values, earlier[t][:, cols], ALU.add)
+        def second_values(t, cols, values=None):
+            values = second[t][:, cols] if values is None else values
+            nc.gpsimd.tensor_tensor(values, second[t][:, cols], earlier[t][:, cols], ALU.add)
             nc.gpsimd.tensor_tensor(values, values, gain2[t][:, cols], ALU.mult)
             return values
 
@@ -207,12 +208,14 @@ def tile_list_woven_tile_denoise_kernel(
             second_product(t)
         for t, cols in ((0, halves[0]), (1, halves[0]), (0, halves[1])):
             place(t, list4, cols, second_values(t, cols))
+        ready = second_values(2, halves[0])
         w2_codes, w2_scales = quantise_weight("w2", w2_raw)
         firsts = tile("firsts", [P, PACK * S], F32, "w2_raw1")
         first = [firsts[:, S * t : S * (t + 1)] for t in range(PACK)]
-        for t, cols in ((2, halves[0]), (1, halves[1]), (2, halves[1])):
-            place(t, list4, cols, second_values(t, cols))
-        place(3, list4, whole, second_values(3, whole))
+        place(2, list4, halves[0], ready)
+        held = tile("held", [P, 2, BANK], F32)
+        for index, (t, cols) in enumerate(after_w2):
+            place(t, list4, cols, second_values(t, cols, held[:, index, :] if index < 2 else None))
 
 
         def first_product(t):
@@ -303,7 +306,7 @@ def tile_list_woven_tile_denoise_kernel(
         def multiply(c):
             width = CHUNKS[c]
             cols = slice(starts[c], starts[c] + width)
-            y = tile("y%d" % c, [P, PACK, width], F32, ("gain1_0", "w2_bf", "w2_raw1", "y3", "gain1_1")[c])
+            y = tile("y%d" % c, [P, PACK, width], F32, ("gain1_0", "w2_raw0", "w2_raw1", "tab_w0", "gain1_1")[c])
             for t in range(PACK):
                 rows = slice(P * t, P * (t + 1))
                 acc = bank("y_%d_%d" % (c, t), (4 * c + t) % 8)

@@ -20,7 +20,11 @@ P = 128
 PACK = 4
 BANK = 512
 TINY = 2.0 ** -63
-OVERLAID = {"w3_raw": 0, "w1_dealt": 0, "v_words0": 2048, "page2": 8192, "w2_bf": 12288, "held": 16384}
+OVERLAID = {"w3_raw": 0, "v2_words": 0, "v_words0": 4096, "page2": 8192, "w2_raw1": 12288, "firsts": 16384,
+            "y2": 16384, "w2_bf": 32768, "held": 32768, "sizes0": 40960, "sizes1": 40960, "z_woven": 40960,
+            "shrink2": 57344, "w4_dealt_scales": 57344, "rounded1": 58368,
+            "rounded2": 61440, "z_codes": 61440}
+LEAD = 256
 CHUNKS = (256, 512, 512, 512, 256)
 
 
@@ -68,88 +72,103 @@ def tile_list_woven_tile_denoise_kernel(
             return raw
 
         earlier = [tile("prev%d" % t, [P, S], F32) for t in range(PACK)]
-        gain1 = [tile("gain1_%d" % t, [P, S], F32) for t in range(PACK)]
         gain2 = [tile("gain2_%d" % t, [P, S], F32) for t in range(PACK)]
+        gain1 = tile("gain1", [P, PACK, S], F32)
+        lead, rest = slice(0, LEAD), slice(LEAD, S)
+        most, last = slice(0, S - LEAD), slice(S - LEAD, S)
+
+        def load_gain(held, rows):
+            for q in (0, 2, 1, 3):
+                nc.sync.dma_start(held[32 * q : 32 * q + 32], rows)
+
+        def load_gain2(t, cols):
+            load_gain(gain2[t][:, cols], wg2.rearrange("(m t) j -> m t j", t=PACK)[:, t, cols])
 
         def load_prev(t, cols):
             nc.sync.dma_start(earlier[t][:, cols], prev.rearrange("(p t) j -> p t j", t=PACK)[:, t, cols])
 
-        def load_gain(held, source, t, cols):
-            rows = source.rearrange("(m t) j -> m t j", t=PACK)[:, t, cols]
-            for q in (0, 2, 1, 3):
-                nc.sync.dma_start(held[t][32 * q : 32 * q + 32, cols], rows)
+        def load_second(t, cols):
+            load_gain2(t, cols)
+            load_prev(t, cols)
 
-        def gather(name, window, offsets, dtype, on=None):
-            picked = tile(name, [P, S], dtype, on)
-            nc.vector.tensor_copy(picked[:], window.indirect(offsets[:]))
+        def gather(name, window, offsets, dtype, pieces=(whole,)):
+            picked = tile(name, [P, S], dtype)
+            for cols in pieces:
+                nc.vector.tensor_copy(picked[:, cols], window.indirect(offsets[:, cols.start // 16 : cols.stop // 16]))
             return picked
 
-        def quantise_weight(name, passes):
+        def scale_window(name):
+            window = tile(name, [P, T], U8)
+            nc.gpsimd.memset(window[32:64, :].bitcast(I32), 0)
+            nc.gpsimd.memset(window[64:128, :].bitcast(I32), 0)
+            return window
+
+        def round_weight(name, passes):
             woven = tile(name + "_bf", [P, len(passes), H * PACK], BF16)
             for a, raw in enumerate(passes):
                 dealt = woven[:, a, :].rearrange("p (t m i) -> p m t i", t=PACK, i=PACK)
                 given = raw[:].rearrange("p i (m t) -> p m t i", t=PACK)
-                if a == len(passes) - 1:
+                if len(passes) == 1:
                     nc.scalar.copy(dealt[:, :, 0:2], given[:, :, 0:2])
                     nc.gpsimd.tensor_scalar(dealt[:, :, 2:4], given[:, :, 2:4], 1.0, 0.0, ALU.mult, ALU.add)
                 else:
                     nc.scalar.copy(dealt, given)
+            return woven
+
+        def quantise_weight(name, passes):
+            woven = round_weight(name, passes)
             codes = tile(name + "_codes", [P, len(passes) * H], U32)
             scales = tile(name + "_scales", [P, len(passes) * H], U8)
             nc.vector.quantize_mx(out=codes[:].bitcast(FP8X4), scales=scales[:],
                                   in_=woven[:].rearrange("p a c -> p (a c)"))
             return codes, scales
 
-        tab_rows = zeroed_plane("tab_rows", T)
+        tab2_rows = zeroed_plane("tab2_rows", T)
+        tab_rows = scale_window("tab_rows")
         w1_plane = zeroed_plane("w1_plane", 2 * H)
-        v2_scales = zeroed_plane("v2_scales", S)
         v_scales = zeroed_plane("v_scales", 2 * S)
         w4_plane = zeroed_plane("w4_plane", N)
 
+        list1 = load_list("list1", offs)
+        nc.sync.dma_start(tab_rows[0:32, :].bitcast(I32), tab_scales.rearrange("a q c -> (a q) c").bitcast(I32))
         list2 = load_list("list2", offs2)
-        tab2_rows = tile("tab2_rows", [P, T], U8)
-        nc.sync.dma_start(tab2_rows[:].bitcast(I32),
-                          tab2_scales[0].bitcast(I32).unsqueeze(1).to_broadcast([16, 8, T // 4]))
+        for q in (0, 2, 1, 3):
+            nc.sync.dma_start(tab2_rows[32 * q : 32 * q + 4, :].bitcast(I32),
+                              tab2_scales[0, 4 * q : 4 * q + 4, :].bitcast(I32))
+        w3_raw = load_weight("w3_raw", w3)
         tab2_w = load_words("tab2_w", tab2_words[0])
-        for q in range(4):
+        for q in (0, 2, 1, 3):
             nc.sync.dma_start(
                 w1_plane[32 * q : 32 * q + 4, :].rearrange("p (a c) -> p a c", a=2).bitcast(I32),
                 w1_scales[:, 4 * q : 4 * q + 4, :].rearrange("a r c -> r a c").bitcast(I32))
-        list1 = load_list("list1", offs)
-        nc.sync.dma_start(tab_rows[0:32, :].bitcast(I32), tab_scales.rearrange("a q c -> (a q) c").bitcast(I32))
-        w3_raw = load_weight("w3_raw", w3)
-        w1_raw = tile("w1_raw", [P, 2, 2 * H], U8)
-        nc.sync.dma_start(w1_raw[:].bitcast(I32), w1_words.rearrange("a p c -> p a c").bitcast(I32))
-        v2_rows = gather("v2_rows", tab2_rows[:], list2, U8)
-        for q in range(4):
-            nc.sync.dma_start(v2_scales[32 * q : 32 * q + 4, :].bitcast(I32),
-                              v2_rows[32 * q : 32 * q + 32 : 8, :].bitcast(I32))
         tab_w = [load_words("tab_w0", tab_words[0])]
-        load_prev(0, halves[0])
-        tab_w.append(load_words("tab_w1", tab_words[1]))
-        load_gain(gain2, wg2, 0, halves[0])
+        load_prev(0, lead)
+        load_gain2(0, lead)
+        list4 = load_list("list4", offs4)
+        tab_w.append(tile("tab_w1", [P, T], I32))
+        tab_w1_source = tab_words[1].rearrange("p c i -> p (c i)").bitcast(I32)
+        nc.sync.dma_start(tab_w[1][:, : 3 * T // 4], tab_w1_source[:, : 3 * T // 4])
+        load_prev(0, rest)
+        load_gain2(0, rest)
+        nc.sync.dma_start(tab_w[1][:, 3 * T // 4 :], tab_w1_source[:, 3 * T // 4 :])
+        load_second(1, whole)
         level_t = tile("level_t", [P, PACK], F32)
         nc.sync.dma_start(level_t[:], level.rearrange("(p t) -> p t", t=PACK))
-        list4 = load_list("list4", offs4)
 
         log_level = tile("log_level", [P, PACK], F32)
         nc.scalar.activation(log_level[:], level_t[:], ACT.Ln)
         neg_log_level = tile("neg_log_level", [P, PACK], F32)
         nc.scalar.mul(neg_log_level[:], log_level[:], -1.0)
 
-        w1_dealt_scales = tile("w1_dealt_scales", [P, 2 * H], U8)
+        v_rows = gather("v_rows", tab_rows[:], list1, U8)
+        v2_scales = gather("v2_scales", tab2_rows[:], list2, U8)
+        w3_codes, w3_scales = quantise_weight("w3", [w3_raw])
+        w1_dealt_scales = tile("w1_dealt_scales", [P, 2 * H], U8, "w3_bf")
         nc.gpsimd.tensor_copy(
             w1_dealt_scales[:].rearrange("p (a t m) -> p a t m", a=2, t=PACK),
             w1_plane[:].rearrange("p (a m t) -> p a t m", a=2, t=PACK))
-        v2_words = gather("v2_words", tab2_w[:].bitcast(U32), list2, U32)
-        v_rows = gather("v_rows", tab_rows[:], list1, U8)
-        w3_codes, w3_scales = quantise_weight("w3", [w3_raw])
-        w1_dealt = tile("w1_dealt", [P, 2, 2 * H], U8)
-        nc.vector.tensor_copy(
-            w1_dealt[:].bitcast(U16).rearrange("p a (t m) -> p a t m", t=PACK),
-            w1_raw[:].bitcast(U16).rearrange("p a (m t) -> p a t m", t=PACK))
+        v2_words = gather("v2_words", tab2_w[:].bitcast(U32), list2, U32, halves)
         v_words = [gather("v_words0", tab_w[0][:].bitcast(U32), list1, U32)]
-        v_words.append(gather("v_words1", tab_w[1][:].bitcast(U32), list1, U32))
 
         def seat_scales(a):
             for q in range(4):
@@ -157,40 +176,33 @@ def tile_list_woven_tile_denoise_kernel(
                 nc.sync.dma_start(v_scales[32 * q : 32 * q + 4, S * a : S * (a + 1)].bitcast(I32),
                                   v_rows[start : start + 4, :].bitcast(I32))
 
-        load_prev(1, halves[0])
-        load_gain(gain2, wg2, 1, halves[0])
-        load_prev(0, halves[1])
-        load_gain(gain2, wg2, 0, halves[1])
         w2_raw = [load_weight("w2_raw0", w2[0:512, :])]
-        load_prev(2, halves[0])
-        load_gain(gain2, wg2, 2, halves[0])
-        w2_raw.append(load_weight("w2_raw1", w2[512:1024, :]))
         seat_scales(0)
+        w1_raw = tile("w1_raw", [P, 2, 2 * H], U8)
+        nc.sync.dma_start(w1_raw[:].bitcast(I32), w1_words.rearrange("a p c -> p a c").bitcast(I32))
+        load_second(2, whole)
+        w2_raw.append(load_weight("w2_raw1", w2[512:1024, :]))
         seat_scales(1)
-        after_w2 = ((1, halves[1]), (3, halves[0]), (2, halves[1]), (3, halves[1]))
-        for t, cols in after_w2:
-            load_prev(t, cols)
-            load_gain(gain2, wg2, t, cols)
+        load_second(3, whole)
         list3 = load_list("list3", offs3)
-        for t in range(PACK):
-            load_gain(gain1, wg1, t, whole)
         w4_raw = load_words("w4_raw", w4_words[0])
         for q in range(4):
             nc.sync.dma_start(w4_plane[32 * q : 32 * q + 4, :].bitcast(I32),
                               w4_scales[0, 4 * q : 4 * q + 4, :].bitcast(I32))
-
+        load_gain(gain1[:], wg1.rearrange("(m t) j -> m t j", t=PACK))
 
         page, second, shrink = {}, {}, {}
 
-        def second_product(t):
+        def second_product(t, u):
             rows = slice(P * t, P * (t + 1))
-            second[t] = tile("second%d" % t, [P, S], F32)
-            for u, cols in enumerate(halves):
-                acc = bank("c_%d_%d" % (t, u), 2 * t + u)
-                nc.tensor.matmul_mx(out=acc[:], lhsT=w3_codes[:, rows].bitcast(FP8X4), lhsT_scale=w3_scales[:, rows],
-                                    rhs=v2_words[:, cols].bitcast(FP8X4), rhs_scale=v2_scales[:, cols],
-                                    start=True, stop=True)
-                nc.scalar.copy(second[t][:, cols], acc[:])
+            if t not in second:
+                second[t] = tile("second%d" % t, [P, S], F32)
+            acc = bank("c_%d_%d" % (t, u), 2 * t + u)
+            cols = halves[u]
+            nc.tensor.matmul_mx(out=acc[:], lhsT=w3_codes[:, rows].bitcast(FP8X4), lhsT_scale=w3_scales[:, rows],
+                                rhs=v2_words[:, cols].bitcast(FP8X4), rhs_scale=v2_scales[:, cols],
+                                start=True, stop=True)
+            return acc
 
         def second_values(t, cols, values=None):
             values = second[t][:, cols] if values is None else values
@@ -204,19 +216,30 @@ def tile_list_woven_tile_denoise_kernel(
             nc.vector.tensor_copy(page[t][:].indirect(offsets[:, cols.start // 16 : cols.stop // 16]), values)
 
 
+        sums = {(t, u): second_product(t, u) for t in range(PACK) for u in range(2)}
+        nc.scalar.copy(second[0][:, lead], sums[0, 0][:, lead])
         for t in range(PACK):
-            second_product(t)
-        for t, cols in ((0, halves[0]), (1, halves[0]), (0, halves[1])):
-            place(t, list4, cols, second_values(t, cols))
-        ready = second_values(2, halves[0])
+            start = LEAD if t == 0 else 0
+            nc.scalar.copy(second[t][:, start:BANK], sums[t, 0][:, start:BANK])
+            nc.scalar.copy(second[t][:, halves[1]], sums[t, 1][:])
+        place(0, list4, lead, second_values(0, lead))
+        v_words.append(gather("v_words1", tab_w[1][:].bitcast(U32), list1, U32))
+        place(0, list4, rest, second_values(0, rest))
+        place(1, list4, most, second_values(1, most))
+        w1_dealt = tile("w1_dealt", [P, 2, 2 * H], U8)
+        nc.gpsimd.tensor_copy(
+            w1_dealt[:].bitcast(U16).rearrange("p a (t m) -> p a t m", t=PACK),
+            w1_raw[:].bitcast(U16).rearrange("p a (m t) -> p a t m", t=PACK))
+        ready = second_values(2, most)
         w2_codes, w2_scales = quantise_weight("w2", w2_raw)
-        firsts = tile("firsts", [P, PACK * S], F32, "w2_raw1")
+        firsts = tile("firsts", [P, PACK * S], F32)
         first = [firsts[:, S * t : S * (t + 1)] for t in range(PACK)]
-        place(2, list4, halves[0], ready)
-        held = tile("held", [P, 2, BANK], F32)
-        for index, (t, cols) in enumerate(after_w2):
-            place(t, list4, cols, second_values(t, cols, held[:, index, :] if index < 2 else None))
-
+        place(2, list4, most, ready)
+        held = tile("held", [P, LEAD + S], F32)
+        place(1, list4, last, second_values(1, last, held[:, :LEAD]))
+        place(3, list4, whole, second_values(3, whole, held[:, LEAD:]))
+        tail2 = tile("tail2", [P, LEAD], F32, "gain2_3")
+        place(2, list4, last, second_values(2, last, tail2[:]))
 
         def first_product(t):
             for u, cols in enumerate(halves):
@@ -234,7 +257,7 @@ def tile_list_woven_tile_denoise_kernel(
             sizes = tile("sizes%d" % pair, [P, 2, S], F32, "sizes")
             for t in (2 * pair, 2 * pair + 1):
                 for u, cols in enumerate(halves):
-                    acc = bank("b_%d_%d" % (t, u), 2 * t + u)
+                    acc = bank("b_%d_%d" % (t, u), (4 + 2 * t + u) % 8)
                     for a in range(2):
                         rows = slice(H * a + P * t, H * a + P * (t + 1))
                         nc.tensor.matmul_mx(out=acc[:], lhsT=w2_codes[:, rows].bitcast(FP8X4), lhsT_scale=w2_scales[:, rows],
@@ -252,27 +275,18 @@ def tile_list_woven_tile_denoise_kernel(
 
         def first_values(t):
             nc.scalar.activation(shrink[t], shrink[t], ACT.Sigmoid, bias=neg_log_level[:, t : t + 1], scale=2.0)
-            nc.gpsimd.tensor_tensor(first[t], first[t], gain1[t][:], ALU.mult)
-            nc.gpsimd.tensor_tensor(first[t], first[t], shrink[t], ALU.mult)
+            gained = tile("gained%d" % t, [P, S], F32, "gain2_2")
+            nc.gpsimd.tensor_tensor(gained[:], first[t], gain1[:, t, :], ALU.mult)
+            nc.gpsimd.tensor_tensor(first[t], gained[:], shrink[t], ALU.mult)
 
-        for t in range(PACK):
-            first_product(t)
-        log_magnitudes(0)
-        first_values(0)
-        first_values(1)
-        log_magnitudes(1)
-        first_values(2)
-        first_values(3)
+        for pair in range(2):
+            first_product(2 * pair)
+            first_product(2 * pair + 1)
+            log_magnitudes(pair)
+            first_values(2 * pair)
+            first_values(2 * pair + 1)
 
-        z_woven = tile("z_woven", [P, T2, PACK], BF16)
-        for t in range(2):
-            place(t, list3, whole, first[t])
-            nc.scalar.activation(z_woven[:, :, t], page[t][:], ACT.Relu)
-        place(2, list3, whole, first[2])
-        for cols in (slice(0, T2 // 2), slice(T2 // 2, T2)):
-            nc.scalar.activation(z_woven[:, cols, 2:4], page[2][:, cols].unsqueeze(2).to_broadcast([P, T2 // 2, 2]), ACT.Relu)
-
-        w4_dealt = tile("w4_dealt", [P, N], I32)
+        w4_dealt = tile("w4_dealt", [P, N], I32, "logs")
         nc.gpsimd.tensor_copy(
             w4_dealt[:].rearrange("p (t m) -> p t m", t=PACK),
             w4_raw[:].rearrange("p (m t) -> p t m", t=PACK))
@@ -280,6 +294,20 @@ def tile_list_woven_tile_denoise_kernel(
         nc.gpsimd.tensor_copy(
             w4_dealt_scales[:].rearrange("p (t m) -> p t m", t=PACK),
             w4_plane[:].rearrange("p (m t) -> p t m", t=PACK))
+
+        z_woven = tile("z_woven", [P, T2, PACK], BF16)
+        place(0, list3, whole, first[0])
+        nc.scalar.activation(z_woven[:, :, 0], page[0][:], ACT.Relu)
+        left, right = slice(0, T2 // 2), slice(T2 // 2, T2)
+        for t in (1, 2):
+            place(t, list3, whole, first[t])
+            copies = t
+            rounded = tile("rounded%d" % t, [P, T2 // 2], BF16)
+            nc.scalar.activation(rounded[:], page[t][:, right], ACT.Relu)
+            nc.scalar.activation(z_woven[:, left, t : t + copies],
+                                 page[t][:, left].unsqueeze(2).to_broadcast([P, T2 // 2, copies]), ACT.Relu)
+            nc.gpsimd.tensor_scalar(z_woven[:, right, t : t + copies],
+                                    rounded[:].unsqueeze(2).to_broadcast([P, T2 // 2, copies]), 1.0, 0.0, ALU.mult, ALU.add)
 
         place(3, list3, whole, first[3])
         z_codes = tile("z_codes", [P, T2], U32)
@@ -291,9 +319,9 @@ def tile_list_woven_tile_denoise_kernel(
         starts = [sum(CHUNKS[:c]) for c in range(len(CHUNKS))]
         y_tiles = {}
 
-        def make_z(c):
-            cols = slice(starts[c], starts[c] + CHUNKS[c])
-            if c == len(CHUNKS) - 2:
+        def make_z(start, width, on_scalar=False):
+            cols = slice(start, start + width)
+            if on_scalar:
                 nc.scalar.activation(z_woven[:, cols, PACK - 1], page[PACK - 1][:, cols], ACT.Relu)
             else:
                 nc.vector.tensor_scalar_max(z_woven[:, cols, PACK - 1], page[PACK - 1][:, cols], 0.0)
@@ -306,7 +334,7 @@ def tile_list_woven_tile_denoise_kernel(
         def multiply(c):
             width = CHUNKS[c]
             cols = slice(starts[c], starts[c] + width)
-            y = tile("y%d" % c, [P, PACK, width], F32, ("gain1_0", "w2_raw0", "w2_raw1", "tab_w0", "gain1_1")[c])
+            y = tile("y%d" % c, [P, PACK, width], F32, ("gain2_0", "w2_raw0", None, "tab_w0", "gain1")[c])
             for t in range(PACK):
                 rows = slice(P * t, P * (t + 1))
                 acc = bank("y_%d_%d" % (c, t), (4 * c + t) % 8)
@@ -343,17 +371,22 @@ def tile_list_woven_tile_denoise_kernel(
                     out_2[0, 4 * q : 4 * q + 4, cols].bitcast(I32), y_scales[32 * q : 32 * q + 4, cols].bitcast(I32))
 
         count = len(CHUNKS)
-        make_z(count - 2)
+        make_z(0, 256, True)
+        make_z(256, 256, True)
+        make_z(512, 256)
+        make_z(768, 256)
+        later = ((1024, 256), (1280, 512), (1792, 256))
         woven = {}
         for c in range(count + 2):
-            if c < count:
-                if c != count - 2:
-                    make_z(c)
-            if 1 <= c <= count:
-                woven[c - 1] = weave_y(c - 1)
+            if 2 <= c <= count + 1 and c - 2 not in woven:
+                woven[c - 2] = weave_y(c - 2)
             if c < count:
                 quantise_z(c)
                 multiply(c)
             if c >= 2:
                 quantise_y(c - 2, woven[c - 2])
+            if c < len(later):
+                make_z(*later[c])
+            if c == count:
+                woven[count - 1] = weave_y(count - 1)
         store_scales(slice(0, T2))

@@ -20,10 +20,9 @@ P = 128
 PACK = 4
 BANK = 512
 TINY = 2.0 ** -63
-OVERLAID = {"w3_raw": 0, "v2_words": 0, "v_words0": 4096, "page2": 8192, "w2_raw1": 12288, "firsts": 16384,
-            "y2": 16384, "w2_bf": 32768, "held": 32768, "sizes0": 40960, "sizes1": 40960, "z_woven": 40960,
-            "shrink2": 57344, "w4_dealt_scales": 57344, "rounded1": 58368,
-            "rounded2": 61440, "z_codes": 61440}
+OVERLAID = {"w3_raw": 0, "v2_words": 0, "v_words0": 4096, "page2": 8192, "w2_raw1": 12288, "firsts1": 16384,
+            "firsts0": 28672, "y2": 16384, "gain_ahead": 32768, "w2_bf": 34816, "held": 32768,
+            "sizes0": 43008, "sizes1": 43008, "z_woven": 43008}
 LEAD = 256
 CHUNKS = (256, 512, 512, 512, 256)
 
@@ -108,7 +107,7 @@ def tile_list_woven_tile_denoise_kernel(
             for a, raw in enumerate(passes):
                 dealt = woven[:, a, :].rearrange("p (t m i) -> p m t i", t=PACK, i=PACK)
                 given = raw[:].rearrange("p i (m t) -> p m t i", t=PACK)
-                if len(passes) == 1:
+                if a == len(passes) - 1:
                     nc.scalar.copy(dealt[:, :, 0:2], given[:, :, 0:2])
                     nc.gpsimd.tensor_scalar(dealt[:, :, 2:4], given[:, :, 2:4], 1.0, 0.0, ALU.mult, ALU.add)
                 else:
@@ -151,7 +150,8 @@ def tile_list_woven_tile_denoise_kernel(
         load_prev(0, rest)
         load_gain2(0, rest)
         nc.sync.dma_start(tab_w[1][:, 3 * T // 4 :], tab_w1_source[:, 3 * T // 4 :])
-        load_second(1, whole)
+        load_prev(1, whole)
+        load_gain2(1, whole)
         level_t = tile("level_t", [P, PACK], F32)
         nc.sync.dma_start(level_t[:], level.rearrange("(p t) -> p t", t=PACK))
 
@@ -180,15 +180,19 @@ def tile_list_woven_tile_denoise_kernel(
         seat_scales(0)
         w1_raw = tile("w1_raw", [P, 2, 2 * H], U8)
         nc.sync.dma_start(w1_raw[:].bitcast(I32), w1_words.rearrange("a p c -> p a c").bitcast(I32))
-        load_second(2, whole)
         w2_raw.append(load_weight("w2_raw1", w2[512:1024, :]))
         seat_scales(1)
-        load_second(3, whole)
+        load_prev(2, halves[0])
+        gain_ahead = tile("gain_ahead", [P, BANK], F32)
+        load_gain(gain_ahead[:], wg2.rearrange("(m t) j -> m t j", t=PACK)[:, 2, halves[0]])
+        load_second(3, halves[0])
         list3 = load_list("list3", offs3)
         w4_raw = load_words("w4_raw", w4_words[0])
         for q in range(4):
             nc.sync.dma_start(w4_plane[32 * q : 32 * q + 4, :].bitcast(I32),
                               w4_scales[0, 4 * q : 4 * q + 4, :].bitcast(I32))
+        load_second(2, halves[1])
+        load_second(3, halves[1])
         load_gain(gain1[:], wg1.rearrange("(m t) j -> m t j", t=PACK))
 
         page, second, shrink = {}, {}, {}
@@ -225,21 +229,26 @@ def tile_list_woven_tile_denoise_kernel(
         place(0, list4, lead, second_values(0, lead))
         v_words.append(gather("v_words1", tab_w[1][:].bitcast(U32), list1, U32))
         place(0, list4, rest, second_values(0, rest))
-        place(1, list4, most, second_values(1, most))
+        nc.gpsimd.tensor_tensor(second[1][:], second[1][:], earlier[1][:], ALU.add)
+        nc.gpsimd.tensor_tensor(second[1][:, most], second[1][:, most], gain2[1][:, most], ALU.mult)
+        place(1, list4, most, second[1][:, most])
         w1_dealt = tile("w1_dealt", [P, 2, 2 * H], U8)
         nc.gpsimd.tensor_copy(
             w1_dealt[:].bitcast(U16).rearrange("p a (t m) -> p a t m", t=PACK),
             w1_raw[:].bitcast(U16).rearrange("p a (m t) -> p a t m", t=PACK))
-        ready = second_values(2, most)
+        ready = second[2][:, halves[0]]
+        nc.gpsimd.tensor_tensor(ready, ready, earlier[2][:, halves[0]], ALU.add)
+        nc.gpsimd.tensor_tensor(ready, ready, gain_ahead[:], ALU.mult)
         w2_codes, w2_scales = quantise_weight("w2", w2_raw)
-        firsts = tile("firsts", [P, PACK * S], F32)
-        first = [firsts[:, S * t : S * (t + 1)] for t in range(PACK)]
-        place(2, list4, most, ready)
-        held = tile("held", [P, LEAD + S], F32)
-        place(1, list4, last, second_values(1, last, held[:, :LEAD]))
-        place(3, list4, whole, second_values(3, whole, held[:, LEAD:]))
-        tail2 = tile("tail2", [P, LEAD], F32, "gain2_3")
-        place(2, list4, last, second_values(2, last, tail2[:]))
+        later_firsts = tile("firsts1", [P, 3 * S], F32)
+        first = [tile("firsts0", [P, S], F32)[:]] + [later_firsts[:, S * t : S * (t + 1)] for t in range(3)]
+        place(2, list4, halves[0], ready)
+        held = tile("held", [P, LEAD + 3 * BANK], F32)
+        nc.gpsimd.tensor_tensor(held[:, :LEAD], second[1][:, last], gain2[1][:, last], ALU.mult)
+        place(1, list4, last, held[:, :LEAD])
+        for index, (t, cols) in enumerate(((3, halves[0]), (2, halves[1]), (3, halves[1]))):
+            start = LEAD + BANK * index
+            place(t, list4, cols, second_values(t, cols, held[:, start : start + BANK]))
 
         def first_product(t):
             for u, cols in enumerate(halves):
@@ -257,7 +266,7 @@ def tile_list_woven_tile_denoise_kernel(
             sizes = tile("sizes%d" % pair, [P, 2, S], F32, "sizes")
             for t in (2 * pair, 2 * pair + 1):
                 for u, cols in enumerate(halves):
-                    acc = bank("b_%d_%d" % (t, u), (4 + 2 * t + u) % 8)
+                    acc = bank("b_%d_%d" % (t, u), 2 * t + u)
                     for a in range(2):
                         rows = slice(H * a + P * t, H * a + P * (t + 1))
                         nc.tensor.matmul_mx(out=acc[:], lhsT=w2_codes[:, rows].bitcast(FP8X4), lhsT_scale=w2_scales[:, rows],
@@ -275,13 +284,13 @@ def tile_list_woven_tile_denoise_kernel(
 
         def first_values(t):
             nc.scalar.activation(shrink[t], shrink[t], ACT.Sigmoid, bias=neg_log_level[:, t : t + 1], scale=2.0)
-            gained = tile("gained%d" % t, [P, S], F32, "gain2_2")
+            gained = tile("gained%d" % t, [P, S], F32, "gain2_3")
             nc.gpsimd.tensor_tensor(gained[:], first[t], gain1[:, t, :], ALU.mult)
             nc.gpsimd.tensor_tensor(first[t], gained[:], shrink[t], ALU.mult)
 
+        for t in range(PACK):
+            first_product(t)
         for pair in range(2):
-            first_product(2 * pair)
-            first_product(2 * pair + 1)
             log_magnitudes(pair)
             first_values(2 * pair)
             first_values(2 * pair + 1)
@@ -290,24 +299,18 @@ def tile_list_woven_tile_denoise_kernel(
         nc.gpsimd.tensor_copy(
             w4_dealt[:].rearrange("p (t m) -> p t m", t=PACK),
             w4_raw[:].rearrange("p (m t) -> p t m", t=PACK))
-        w4_dealt_scales = tile("w4_dealt_scales", [P, N], U8)
+        w4_dealt_scales = tile("w4_dealt_scales", [P, N], U8, "shrink2")
         nc.gpsimd.tensor_copy(
             w4_dealt_scales[:].rearrange("p (t m) -> p t m", t=PACK),
             w4_plane[:].rearrange("p (m t) -> p t m", t=PACK))
 
         z_woven = tile("z_woven", [P, T2, PACK], BF16)
-        place(0, list3, whole, first[0])
-        nc.scalar.activation(z_woven[:, :, 0], page[0][:], ACT.Relu)
-        left, right = slice(0, T2 // 2), slice(T2 // 2, T2)
-        for t in (1, 2):
+        for t in range(2):
             place(t, list3, whole, first[t])
-            copies = t
-            rounded = tile("rounded%d" % t, [P, T2 // 2], BF16)
-            nc.scalar.activation(rounded[:], page[t][:, right], ACT.Relu)
-            nc.scalar.activation(z_woven[:, left, t : t + copies],
-                                 page[t][:, left].unsqueeze(2).to_broadcast([P, T2 // 2, copies]), ACT.Relu)
-            nc.gpsimd.tensor_scalar(z_woven[:, right, t : t + copies],
-                                    rounded[:].unsqueeze(2).to_broadcast([P, T2 // 2, copies]), 1.0, 0.0, ALU.mult, ALU.add)
+            nc.scalar.activation(z_woven[:, :, t], page[t][:], ACT.Relu)
+        place(2, list3, whole, first[2])
+        for cols in (slice(0, T2 // 2), slice(T2 // 2, T2)):
+            nc.scalar.activation(z_woven[:, cols, 2:4], page[2][:, cols].unsqueeze(2).to_broadcast([P, T2 // 2, 2]), ACT.Relu)
 
         place(3, list3, whole, first[3])
         z_codes = tile("z_codes", [P, T2], U32)
@@ -371,13 +374,13 @@ def tile_list_woven_tile_denoise_kernel(
                     out_2[0, 4 * q : 4 * q + 4, cols].bitcast(I32), y_scales[32 * q : 32 * q + 4, cols].bitcast(I32))
 
         count = len(CHUNKS)
-        make_z(0, 256, True)
-        make_z(256, 256, True)
-        make_z(512, 256)
-        make_z(768, 256)
-        later = ((1024, 256), (1280, 512), (1792, 256))
+        make_z(1792, 256, True)
+        ahead = (((0, 256),), ((256, 128), (384, 384)), ((768, 256), (1024, 256)), ((1280, 512),), ())
         woven = {}
         for c in range(count + 2):
+            if c < count:
+                for piece in ahead[c]:
+                    make_z(*piece)
             if 2 <= c <= count + 1 and c - 2 not in woven:
                 woven[c - 2] = weave_y(c - 2)
             if c < count:
@@ -385,8 +388,6 @@ def tile_list_woven_tile_denoise_kernel(
                 multiply(c)
             if c >= 2:
                 quantise_y(c - 2, woven[c - 2])
-            if c < len(later):
-                make_z(*later[c])
             if c == count:
                 woven[count - 1] = weave_y(count - 1)
         store_scales(slice(0, T2))

@@ -72,7 +72,7 @@ def tile_list_woven_tile_denoise_kernel(
 
         earlier = [tile("prev%d" % t, [P, S], F32) for t in range(PACK)]
         gain2 = [tile("gain2_%d" % t, [P, S], F32) for t in range(PACK)]
-        gain1 = tile("gain1", [P, PACK, S], F32)
+        gain1 = [tile("gain1_%d" % t, [P, S], F32) for t in range(PACK)]
         lead, rest = slice(0, LEAD), slice(LEAD, S)
         most, last = slice(0, S - LEAD), slice(S - LEAD, S)
 
@@ -193,7 +193,8 @@ def tile_list_woven_tile_denoise_kernel(
                               w4_scales[0, 4 * q : 4 * q + 4, :].bitcast(I32))
         load_second(2, halves[1])
         load_second(3, halves[1])
-        load_gain(gain1[:], wg1.rearrange("(m t) j -> m t j", t=PACK))
+        for t in range(PACK):
+            load_gain(gain1[t][:], wg1.rearrange("(m t) j -> m t j", t=PACK)[:, t, :])
 
         page, second, shrink = {}, {}, {}
 
@@ -285,7 +286,7 @@ def tile_list_woven_tile_denoise_kernel(
         def first_values(t):
             nc.scalar.activation(shrink[t], shrink[t], ACT.Sigmoid, bias=neg_log_level[:, t : t + 1], scale=2.0)
             gained = tile("gained%d" % t, [P, S], F32, "gain2_3")
-            nc.gpsimd.tensor_tensor(gained[:], first[t], gain1[:, t, :], ALU.mult)
+            nc.gpsimd.tensor_tensor(gained[:], first[t], gain1[t][:], ALU.mult)
             nc.gpsimd.tensor_tensor(first[t], gained[:], shrink[t], ALU.mult)
 
         for t in range(PACK):
@@ -309,17 +310,18 @@ def tile_list_woven_tile_denoise_kernel(
             place(t, list3, whole, first[t])
             nc.scalar.activation(z_woven[:, :, t], page[t][:], ACT.Relu)
         place(2, list3, whole, first[2])
-        for cols in (slice(0, T2 // 2), slice(T2 // 2, T2)):
-            nc.scalar.activation(z_woven[:, cols, 2:4], page[2][:, cols].unsqueeze(2).to_broadcast([P, T2 // 2, 2]), ACT.Relu)
+        for cols in (slice(0, 1280), slice(1280, T2)):
+            nc.scalar.activation(z_woven[:, cols, 2:4],
+                                 page[2][:, cols].unsqueeze(2).to_broadcast([P, cols.stop - cols.start, 2]), ACT.Relu)
 
         place(3, list3, whole, first[3])
         z_codes = tile("z_codes", [P, T2], U32)
         z_scales = tile("z_scales", [P, T2], U8)
         y_codes = tile("y_codes", [P, T2], I32)
-        y_scales = tile("y_scales", [P, T2], U8)
+        y_scales = tile("y_scales", [P, BANK], U8)
         out_rows = out_0.rearrange("(p t) m -> p t m", t=PACK)
         out_words = out_1[0].rearrange("p m i -> p (m i)").bitcast(I32)
-        starts = [sum(CHUNKS[:c]) for c in range(len(CHUNKS))]
+        starts = (0, 512, 1024, 1536, 256)
         y_tiles = {}
 
         def make_z(start, width, on_scalar=False):
@@ -337,7 +339,7 @@ def tile_list_woven_tile_denoise_kernel(
         def multiply(c):
             width = CHUNKS[c]
             cols = slice(starts[c], starts[c] + width)
-            y = tile("y%d" % c, [P, PACK, width], F32, ("gain2_0", "w2_raw0", None, "tab_w0", "gain1")[c])
+            y = tile("y%d" % c, [P, PACK, width], F32, ("gain2_0", "w2_raw0", None, "tab_w0", "gain1_1")[c])
             for t in range(PACK):
                 rows = slice(P * t, P * (t + 1))
                 acc = bank("y_%d_%d" % (c, t), (4 * c + t) % 8)
@@ -362,20 +364,23 @@ def tile_list_woven_tile_denoise_kernel(
 
         def quantise_y(c, woven):
             cols = slice(starts[c], starts[c] + CHUNKS[c])
-            nc.vector.quantize_mx(out=y_codes[:, cols].bitcast(FP8X4), scales=y_scales[:, cols], in_=woven[:])
+            quarter = cols.start // BANK
+            within = slice(cols.start - BANK * quarter, cols.stop - BANK * quarter)
+            nc.vector.quantize_mx(out=y_codes[:, cols].bitcast(FP8X4), scales=y_scales[4 * quarter :, within], in_=woven[:])
             if c == len(CHUNKS) - 2:
                 cols = slice(starts[c - 1], cols.stop)
             if c != len(CHUNKS) - 3:
                 nc.sync.dma_start(out_words[:, cols], y_codes[:, cols])
 
-        def store_scales(cols):
+        def store_scales():
             for q in range(4):
                 (nc.scalar, nc.sync)[q % 2].dma_start(
-                    out_2[0, 4 * q : 4 * q + 4, cols].bitcast(I32), y_scales[32 * q : 32 * q + 4, cols].bitcast(I32))
+                    out_2[0, 4 * q : 4 * q + 4, :].rearrange("r (j c) -> j r c", j=4).bitcast(I32),
+                    y_scales[32 * q : 32 * q + 16, :].bitcast(I32))
 
         count = len(CHUNKS)
-        make_z(1792, 256, True)
-        ahead = (((0, 256),), ((256, 128), (384, 384)), ((768, 256), (1024, 256)), ((1280, 512),), ())
+        make_z(256, 256, True)
+        ahead = (((0, 256),), ((512, 128), (640, 384)), ((1024, 256), (1280, 256)), ((1536, 512),), ())
         woven = {}
         for c in range(count + 2):
             if c < count:
@@ -390,4 +395,4 @@ def tile_list_woven_tile_denoise_kernel(
                 quantise_y(c - 2, woven[c - 2])
             if c == count:
                 woven[count - 1] = weave_y(count - 1)
-        store_scales(slice(0, T2))
+        store_scales()

@@ -21,9 +21,10 @@ PACK = 4
 BANK = 512
 TINY = 2.0 ** -63
 OVERLAID = {"w3_raw": 0, "v2_words": 0, "v_words0": 4096, "page2": 8192, "w2_raw1": 12288, "firsts1": 16384,
-            "firsts0": 28672, "y2": 16384, "gain_ahead": 32768, "w2_bf": 34816, "held": 32768,
+            "firsts0": 28672, "y2": 16384, "gain2_4": 32768, "w2_bf": 34816, "values5": 34304,
             "sizes0": 43008, "sizes1": 43008, "z_woven": 43008}
-LEAD = 256
+PIECES = ((0, 0, 256), (1, 0, 384), (0, 256, 768), (1, 384, 1024), (2, 0, 512),
+          (0, 768, 1024), (3, 0, 512), (2, 512, 1024), (3, 512, 1024))
 CHUNKS = (256, 512, 512, 512, 256)
 
 
@@ -71,24 +72,18 @@ def tile_list_woven_tile_denoise_kernel(
             return raw
 
         earlier = [tile("prev%d" % t, [P, S], F32) for t in range(PACK)]
-        gain2 = [tile("gain2_%d" % t, [P, S], F32) for t in range(PACK)]
         gain1 = [tile("gain1_%d" % t, [P, S], F32) for t in range(PACK)]
-        lead, rest = slice(0, LEAD), slice(LEAD, S)
-        most, last = slice(0, S - LEAD), slice(S - LEAD, S)
+        gain2 = {}
 
         def load_gain(held, rows):
             for q in (0, 2, 1, 3):
                 nc.sync.dma_start(held[32 * q : 32 * q + 32], rows)
 
-        def load_gain2(t, cols):
-            load_gain(gain2[t][:, cols], wg2.rearrange("(m t) j -> m t j", t=PACK)[:, t, cols])
-
-        def load_prev(t, cols):
-            nc.sync.dma_start(earlier[t][:, cols], prev.rearrange("(p t) j -> p t j", t=PACK)[:, t, cols])
-
-        def load_second(t, cols):
-            load_gain2(t, cols)
-            load_prev(t, cols)
+        def load_piece(n):
+            t, start, stop = PIECES[n]
+            nc.sync.dma_start(earlier[t][:, start:stop], prev.rearrange("(p t) j -> p t j", t=PACK)[:, t, start:stop])
+            gain2[n] = tile("gain2_%d" % n, [P, stop - start], F32)
+            load_gain(gain2[n][:], wg2.rearrange("(m t) j -> m t j", t=PACK)[:, t, start:stop])
 
         def gather(name, window, offsets, dtype, pieces=(whole,)):
             picked = tile(name, [P, S], dtype)
@@ -141,17 +136,11 @@ def tile_list_woven_tile_denoise_kernel(
                 w1_plane[32 * q : 32 * q + 4, :].rearrange("p (a c) -> p a c", a=2).bitcast(I32),
                 w1_scales[:, 4 * q : 4 * q + 4, :].rearrange("a r c -> r a c").bitcast(I32))
         tab_w = [load_words("tab_w0", tab_words[0])]
-        load_prev(0, lead)
-        load_gain2(0, lead)
+        load_piece(0)
         list4 = load_list("list4", offs4)
-        tab_w.append(tile("tab_w1", [P, T], I32))
-        tab_w1_source = tab_words[1].rearrange("p c i -> p (c i)").bitcast(I32)
-        nc.sync.dma_start(tab_w[1][:, : 3 * T // 4], tab_w1_source[:, : 3 * T // 4])
-        load_prev(0, rest)
-        load_gain2(0, rest)
-        nc.sync.dma_start(tab_w[1][:, 3 * T // 4 :], tab_w1_source[:, 3 * T // 4 :])
-        load_prev(1, whole)
-        load_gain2(1, whole)
+        tab_w.append(load_words("tab_w1", tab_words[1]))
+        load_piece(1)
+        load_piece(2)
         level_t = tile("level_t", [P, PACK], F32)
         nc.sync.dma_start(level_t[:], level.rearrange("(p t) -> p t", t=PACK))
 
@@ -177,22 +166,21 @@ def tile_list_woven_tile_denoise_kernel(
                                   v_rows[start : start + 4, :].bitcast(I32))
 
         w2_raw = [load_weight("w2_raw0", w2[0:512, :])]
-        seat_scales(0)
+        load_piece(3)
         w1_raw = tile("w1_raw", [P, 2, 2 * H], U8)
         nc.sync.dma_start(w1_raw[:].bitcast(I32), w1_words.rearrange("a p c -> p a c").bitcast(I32))
+        seat_scales(0)
         w2_raw.append(load_weight("w2_raw1", w2[512:1024, :]))
         seat_scales(1)
-        load_prev(2, halves[0])
-        gain_ahead = tile("gain_ahead", [P, BANK], F32)
-        load_gain(gain_ahead[:], wg2.rearrange("(m t) j -> m t j", t=PACK)[:, 2, halves[0]])
-        load_second(3, halves[0])
+        for n in (4, 5, 6):
+            load_piece(n)
         list3 = load_list("list3", offs3)
         w4_raw = load_words("w4_raw", w4_words[0])
         for q in range(4):
             nc.sync.dma_start(w4_plane[32 * q : 32 * q + 4, :].bitcast(I32),
                               w4_scales[0, 4 * q : 4 * q + 4, :].bitcast(I32))
-        load_second(2, halves[1])
-        load_second(3, halves[1])
+        load_piece(7)
+        load_piece(8)
         for t in range(PACK):
             load_gain(gain1[t][:], wg1.rearrange("(m t) j -> m t j", t=PACK)[:, t, :])
 
@@ -209,11 +197,12 @@ def tile_list_woven_tile_denoise_kernel(
                                 start=True, stop=True)
             return acc
 
-        def second_values(t, cols, values=None):
-            values = second[t][:, cols] if values is None else values
-            nc.gpsimd.tensor_tensor(values, second[t][:, cols], earlier[t][:, cols], ALU.add)
-            nc.gpsimd.tensor_tensor(values, values, gain2[t][:, cols], ALU.mult)
-            return values
+        def second_values(n):
+            t, start, stop = PIECES[n]
+            values = tile("values%d" % n, [P, stop - start], F32, "gain2_%d" % (n - 1) if n else None)
+            nc.gpsimd.tensor_tensor(values[:], second[t][:, start:stop], earlier[t][:, start:stop], ALU.add)
+            nc.gpsimd.tensor_tensor(values[:], values[:], gain2[n][:], ALU.mult)
+            return values[:]
 
         def place(t, offsets, cols, values):
             if t not in page:
@@ -221,35 +210,30 @@ def tile_list_woven_tile_denoise_kernel(
             nc.vector.tensor_copy(page[t][:].indirect(offsets[:, cols.start // 16 : cols.stop // 16]), values)
 
 
-        sums = {(t, u): second_product(t, u) for t in range(PACK) for u in range(2)}
-        nc.scalar.copy(second[0][:, lead], sums[0, 0][:, lead])
-        for t in range(PACK):
-            start = LEAD if t == 0 else 0
-            nc.scalar.copy(second[t][:, start:BANK], sums[t, 0][:, start:BANK])
-            nc.scalar.copy(second[t][:, halves[1]], sums[t, 1][:])
-        place(0, list4, lead, second_values(0, lead))
+        sums = {(t, u): second_product(t, u) for u in range(2) for t in range(PACK)}
+        def place_second(n, values):
+            t, start, stop = PIECES[n]
+            place(t, list4, slice(start, stop), values)
+
+        lead = PIECES[0][2]
+        nc.scalar.copy(second[0][:, :lead], sums[0, 0][:, :lead])
+        nc.scalar.copy(second[1][:, halves[0]], sums[1, 0][:])
+        nc.scalar.copy(second[0][:, lead:BANK], sums[0, 0][:, lead:])
+        for t, u in ((0, 1), (1, 1), (2, 0), (3, 0), (2, 1), (3, 1)):
+            nc.scalar.copy(second[t][:, halves[u]], sums[t, u][:])
+        place_second(0, second_values(0))
         v_words.append(gather("v_words1", tab_w[1][:].bitcast(U32), list1, U32))
-        place(0, list4, rest, second_values(0, rest))
-        nc.gpsimd.tensor_tensor(second[1][:], second[1][:], earlier[1][:], ALU.add)
-        nc.gpsimd.tensor_tensor(second[1][:, most], second[1][:, most], gain2[1][:, most], ALU.mult)
-        place(1, list4, most, second[1][:, most])
+        for n in (1, 2, 3):
+            place_second(n, second_values(n))
         w1_dealt = tile("w1_dealt", [P, 2, 2 * H], U8)
         nc.gpsimd.tensor_copy(
             w1_dealt[:].bitcast(U16).rearrange("p a (t m) -> p a t m", t=PACK),
             w1_raw[:].bitcast(U16).rearrange("p a (m t) -> p a t m", t=PACK))
-        ready = second[2][:, halves[0]]
-        nc.gpsimd.tensor_tensor(ready, ready, earlier[2][:, halves[0]], ALU.add)
-        nc.gpsimd.tensor_tensor(ready, ready, gain_ahead[:], ALU.mult)
         w2_codes, w2_scales = quantise_weight("w2", w2_raw)
         later_firsts = tile("firsts1", [P, 3 * S], F32)
         first = [tile("firsts0", [P, S], F32)[:]] + [later_firsts[:, S * t : S * (t + 1)] for t in range(3)]
-        place(2, list4, halves[0], ready)
-        held = tile("held", [P, LEAD + 3 * BANK], F32)
-        nc.gpsimd.tensor_tensor(held[:, :LEAD], second[1][:, last], gain2[1][:, last], ALU.mult)
-        place(1, list4, last, held[:, :LEAD])
-        for index, (t, cols) in enumerate(((3, halves[0]), (2, halves[1]), (3, halves[1]))):
-            start = LEAD + BANK * index
-            place(t, list4, cols, second_values(t, cols, held[:, start : start + BANK]))
+        for n in range(4, len(PIECES)):
+            place_second(n, second_values(n))
 
         def first_product(t):
             for u, cols in enumerate(halves):
@@ -285,7 +269,7 @@ def tile_list_woven_tile_denoise_kernel(
 
         def first_values(t):
             nc.scalar.activation(shrink[t], shrink[t], ACT.Sigmoid, bias=neg_log_level[:, t : t + 1], scale=2.0)
-            gained = tile("gained%d" % t, [P, S], F32, "gain2_3")
+            gained = tile("gained%d" % t, [P, S], F32, "gain2_8")
             nc.gpsimd.tensor_tensor(gained[:], first[t], gain1[t][:], ALU.mult)
             nc.gpsimd.tensor_tensor(first[t], gained[:], shrink[t], ALU.mult)
 
@@ -339,7 +323,7 @@ def tile_list_woven_tile_denoise_kernel(
         def multiply(c):
             width = CHUNKS[c]
             cols = slice(starts[c], starts[c] + width)
-            y = tile("y%d" % c, [P, PACK, width], F32, ("gain2_0", "w2_raw0", None, "tab_w0", "gain1_1")[c])
+            y = tile("y%d" % c, [P, PACK, width], F32, ("gain1_0", "w2_raw0", None, "tab_w0", "gain1_1")[c])
             for t in range(PACK):
                 rows = slice(P * t, P * (t + 1))
                 acc = bank("y_%d_%d" % (c, t), (4 * c + t) % 8)

@@ -22,6 +22,7 @@ BANK = 512
 TINY = 2.0 ** -63
 OVERLAID = {"w3_raw": 0, "v2_words": 0, "v_words0": 4096, "page2": 8192, "w2_raw1": 12288, "firsts1": 16384,
             "firsts0": 28672, "y2": 16384, "gain2_4": 32768, "w2_bf": 34816, "values5": 34304,
+            "values6": 35328, "values7": 37376, "values8": 39424,
             "sizes0": 43008, "sizes1": 43008, "z_woven": 43008}
 PIECES = ((0, 0, 256), (1, 0, 384), (0, 256, 768), (1, 384, 1024), (2, 0, 512),
           (0, 768, 1024), (3, 0, 512), (2, 512, 1024), (3, 512, 1024))
@@ -102,7 +103,7 @@ def tile_list_woven_tile_denoise_kernel(
             for a, raw in enumerate(passes):
                 dealt = woven[:, a, :].rearrange("p (t m i) -> p m t i", t=PACK, i=PACK)
                 given = raw[:].rearrange("p i (m t) -> p m t i", t=PACK)
-                if a == len(passes) - 1:
+                if len(passes) == 1:
                     nc.scalar.copy(dealt[:, :, 0:2], given[:, :, 0:2])
                     nc.gpsimd.tensor_scalar(dealt[:, :, 2:4], given[:, :, 2:4], 1.0, 0.0, ALU.mult, ALU.add)
                 else:
@@ -175,14 +176,14 @@ def tile_list_woven_tile_denoise_kernel(
         for n in (4, 5, 6):
             load_piece(n)
         list3 = load_list("list3", offs3)
-        w4_raw = load_words("w4_raw", w4_words[0])
-        for q in range(4):
-            nc.sync.dma_start(w4_plane[32 * q : 32 * q + 4, :].bitcast(I32),
-                              w4_scales[0, 4 * q : 4 * q + 4, :].bitcast(I32))
         load_piece(7)
         load_piece(8)
         for t in range(PACK):
             load_gain(gain1[t][:], wg1.rearrange("(m t) j -> m t j", t=PACK)[:, t, :])
+        w4_raw = load_words("w4_raw", w4_words[0])
+        for q in range(4):
+            nc.sync.dma_start(w4_plane[32 * q : 32 * q + 4, :].bitcast(I32),
+                              w4_scales[0, 4 * q : 4 * q + 4, :].bitcast(I32))
 
         page, second, shrink = {}, {}, {}
 
@@ -280,11 +281,11 @@ def tile_list_woven_tile_denoise_kernel(
             first_values(2 * pair)
             first_values(2 * pair + 1)
 
-        w4_dealt = tile("w4_dealt", [P, N], I32, "logs")
+        w4_dealt = tile("w4_dealt", [P, N], I32, "shrink3")
         nc.gpsimd.tensor_copy(
             w4_dealt[:].rearrange("p (t m) -> p t m", t=PACK),
             w4_raw[:].rearrange("p (m t) -> p t m", t=PACK))
-        w4_dealt_scales = tile("w4_dealt_scales", [P, N], U8, "shrink2")
+        w4_dealt_scales = tile("w4_dealt_scales", [P, N], U8, "gain2_8")
         nc.gpsimd.tensor_copy(
             w4_dealt_scales[:].rearrange("p (t m) -> p t m", t=PACK),
             w4_plane[:].rearrange("p (m t) -> p t m", t=PACK))

@@ -26,7 +26,8 @@ OVERLAID = {"w3_raw": 0, "v2_words": 0, "v_words0": 4096, "page2": 8192, "w2_raw
             "sizes0": 43008, "sizes1": 43008, "z_woven": 43008}
 PIECES = ((0, 0, 256), (1, 0, 384), (0, 256, 768), (1, 384, 1024), (2, 0, 512),
           (0, 768, 1024), (3, 0, 512), (2, 512, 1024), (3, 512, 1024))
-CHUNKS = (256, 512, 512, 512, 256)
+CHUNKS = (256, 256, 512, 512, 512)
+ROWS_A_STORE = (1, 2, 1, 1, 2)
 
 
 def tile_list_woven_tile_denoise_kernel(
@@ -306,15 +307,14 @@ def tile_list_woven_tile_denoise_kernel(
         y_scales = tile("y_scales", [P, BANK], U8)
         out_rows = out_0.rearrange("(p t) m -> p t m", t=PACK)
         out_words = out_1[0].rearrange("p m i -> p (m i)").bitcast(I32)
-        starts = (0, 512, 1024, 1536, 256)
-        y_tiles = {}
+        starts = [sum(CHUNKS[:c]) for c in range(len(CHUNKS))]
+        quarters = T2 // BANK
+        y_tiles = [tile("y%d" % q, [P, PACK, BANK], F32, ("tab2_w", "w2_raw0", None, "tab_w0")[q])
+                   for q in range(quarters)]
 
-        def make_z(start, width, on_scalar=False):
+        def make_z(start, width):
             cols = slice(start, start + width)
-            if on_scalar:
-                nc.scalar.activation(z_woven[:, cols, PACK - 1], page[PACK - 1][:, cols], ACT.Relu)
-            else:
-                nc.vector.tensor_scalar_max(z_woven[:, cols, PACK - 1], page[PACK - 1][:, cols], 0.0)
+            nc.vector.tensor_scalar_max(z_woven[:, cols, PACK - 1], page[PACK - 1][:, cols], 0.0)
 
         def quantise_z(c):
             cols = slice(starts[c], starts[c] + CHUNKS[c])
@@ -324,7 +324,7 @@ def tile_list_woven_tile_denoise_kernel(
         def multiply(c):
             width = CHUNKS[c]
             cols = slice(starts[c], starts[c] + width)
-            y = tile("y%d" % c, [P, PACK, width], F32, ("gain1_0", "w2_raw0", None, "tab_w0", "gain1_1")[c])
+            y = y_tiles[cols.start // BANK][:, :, cols.start % BANK : cols.start % BANK + width]
             for t in range(PACK):
                 rows = slice(P * t, P * (t + 1))
                 acc = bank("y_%d_%d" % (c, t), (4 * c + t) % 8)
@@ -332,52 +332,53 @@ def tile_list_woven_tile_denoise_kernel(
                                     rhs=z_codes[:, cols].bitcast(FP8X4), rhs_scale=z_scales[:, cols],
                                     start=True, stop=True)
                 nc.scalar.copy(y[:, t, :], acc[:, :width])
-                rows_a_store = (1, 1, 1, 2, 4)[c]
-                if (t + 1) % rows_a_store == 0:
-                    stored = slice(t + 1 - rows_a_store, t + 1)
+                if ROWS_A_STORE[c] == 1 or t % 2:
+                    stored = slice(t + 1 - ROWS_A_STORE[c], t + 1)
                     nc.sync.dma_start(out_rows[:, stored, cols], y[:, stored, :])
-            y_tiles[c] = y
 
-        def weave_y(c):
-            width = CHUNKS[c]
-            woven = tile("y_woven%d" % c, [P, width * PACK], BF16, "prev%d" % (c % 3))
-            copy = nc.scalar.copy if c == len(CHUNKS) - 1 else nc.vector.tensor_copy
+        def weave_y(quarter, within, on, copy):
+            woven = tile("y_woven%d_%d" % (quarter, within.start), [P, (within.stop - within.start) * PACK], BF16, on)
             copy(
                 woven[:].rearrange("p (m i t) -> p m t i", i=4, t=PACK),
-                y_tiles[c][:].rearrange("p t (m i) -> p m t i", i=4))
+                y_tiles[quarter][:, :, within].rearrange("p t (m i) -> p m t i", i=4))
             return woven
 
-        def quantise_y(c, woven):
-            cols = slice(starts[c], starts[c] + CHUNKS[c])
-            quarter = cols.start // BANK
-            within = slice(cols.start - BANK * quarter, cols.stop - BANK * quarter)
+        def quantise_y(quarter, within, woven):
+            cols = slice(BANK * quarter + within.start, BANK * quarter + within.stop)
             nc.vector.quantize_mx(out=y_codes[:, cols].bitcast(FP8X4), scales=y_scales[4 * quarter :, within], in_=woven[:])
-            if c == len(CHUNKS) - 2:
-                cols = slice(starts[c - 1], cols.stop)
-            if c != len(CHUNKS) - 3:
-                nc.sync.dma_start(out_words[:, cols], y_codes[:, cols])
+
+        def store_words(first, last):
+            cols = slice(BANK * first, BANK * (last + 1))
+            nc.sync.dma_start(out_words[:, cols], y_codes[:, cols])
 
         def store_scales():
             for q in range(4):
-                (nc.scalar, nc.sync)[q % 2].dma_start(
+                nc.scalar.dma_start(
                     out_2[0, 4 * q : 4 * q + 4, :].rearrange("r (j c) -> j r c", j=4).bitcast(I32),
                     y_scales[32 * q : 32 * q + 16, :].bitcast(I32))
 
+        full, lower, upper = slice(0, BANK), slice(0, BANK // 2), slice(BANK // 2, BANK)
         count = len(CHUNKS)
-        make_z(256, 256, True)
-        ahead = (((0, 256),), ((512, 128), (640, 384)), ((1024, 256), (1280, 256)), ((1536, 512),), ())
+        make_z(0, CHUNKS[0])
         woven = {}
-        for c in range(count + 2):
-            if c < count:
-                for piece in ahead[c]:
-                    make_z(*piece)
-            if 2 <= c <= count + 1 and c - 2 not in woven:
-                woven[c - 2] = weave_y(c - 2)
-            if c < count:
-                quantise_z(c)
-                multiply(c)
-            if c >= 2:
-                quantise_y(c - 2, woven[c - 2])
-            if c == count:
-                woven[count - 1] = weave_y(count - 1)
+        for c in range(count):
+            if c + 1 < count:
+                make_z(starts[c + 1], CHUNKS[c + 1] // 2)
+            else:
+                woven[0] = weave_y(0, full, "prev0", nc.vector.tensor_copy)
+            quantise_z(c)
+            multiply(c)
+            if c + 1 < count:
+                make_z(starts[c + 1] + CHUNKS[c + 1] // 2, CHUNKS[c + 1] // 2)
+        for q in (1, 2):
+            woven[q] = weave_y(q, full, "prev%d" % q, nc.vector.tensor_copy)
+            quantise_y(q - 1, full, woven[q - 1])
+        store_words(0, 1)
+        quantise_y(2, full, woven[2])
+        store_words(2, 2)
+        by_vector = weave_y(3, lower, "prev3", nc.vector.tensor_copy)
+        by_scalar = weave_y(3, upper, "gain1_0", nc.scalar.copy)
+        quantise_y(3, lower, by_vector)
+        quantise_y(3, upper, by_scalar)
+        store_words(3, 3)
         store_scales()

@@ -23,11 +23,14 @@ TINY = 2.0 ** -63
 OVERLAID = {"w3_raw": 0, "v2_words": 0, "v_words0": 4096, "page2": 8192, "w2_raw1": 12288, "firsts1": 16384,
             "firsts0": 28672, "y2": 16384, "gain2_4": 32768, "w2_bf": 34816, "values5": 34304,
             "values6": 35328, "values7": 37376, "values8": 39424,
-            "sizes0": 43008, "sizes1": 43008, "z_woven": 43008}
+            "sizes0": 43008, "sizes1": 43008, "z_direct": 38912, "pairs": 47104, "shrink3": 55296,
+            "shrink2": 59392, "z_paired": 55296, "gain2_8": 63488, "gained0": 63488, "gained1": 63488,
+            "gained2": 63488, "gained3": 63488, "w4_dealt": 63488, "w4_dealt_scales": 65536}
 PIECES = ((0, 0, 256), (1, 0, 384), (0, 256, 768), (1, 384, 1024), (2, 0, 512),
           (0, 768, 1024), (3, 0, 512), (2, 512, 1024), (3, 512, 1024))
-CHUNKS = (256, 256, 512, 512, 512)
-ROWS_A_STORE = (1, 2, 1, 1, 2)
+CHUNKS = (128, 128, 256, 512, 512, 512)
+ROWS_A_STORE = (2, 2, 2, 1, 1, 2)
+SHARED = 256
 
 
 def tile_list_woven_tile_denoise_kernel(
@@ -271,7 +274,7 @@ def tile_list_woven_tile_denoise_kernel(
 
         def first_values(t):
             nc.scalar.activation(shrink[t], shrink[t], ACT.Sigmoid, bias=neg_log_level[:, t : t + 1], scale=2.0)
-            gained = tile("gained%d" % t, [P, S], F32, "gain2_8")
+            gained = tile("gained%d" % t, [P, S], F32)
             nc.gpsimd.tensor_tensor(gained[:], first[t], gain1[t][:], ALU.mult)
             nc.gpsimd.tensor_tensor(first[t], gained[:], shrink[t], ALU.mult)
 
@@ -282,23 +285,35 @@ def tile_list_woven_tile_denoise_kernel(
             first_values(2 * pair)
             first_values(2 * pair + 1)
 
-        w4_dealt = tile("w4_dealt", [P, N], I32, "shrink3")
+        half = T2 // 2
+        z_direct = tile("z_direct", [P, half, PACK], BF16)
+        z_paired = tile("z_paired", [P, half, PACK], BF16)
+        pairs = tile("pairs", [P, 2, half, 2], BF16)
+
+        def z_woven(cols):
+            if cols.start < half:
+                return z_direct[:, cols, :]
+            return z_paired[:, cols.start - half : cols.stop - half, :]
+
+        for t in range(2):
+            place(t, list3, whole, first[t])
+            nc.scalar.activation(pairs[:, 0, :, t], page[t][:, half:], ACT.Relu)
+            nc.scalar.activation(z_direct[:, :, t], page[t][:, :half], ACT.Relu)
+        w4_dealt = tile("w4_dealt", [P, N], I32)
         nc.gpsimd.tensor_copy(
             w4_dealt[:].rearrange("p (t m) -> p t m", t=PACK),
             w4_raw[:].rearrange("p (m t) -> p t m", t=PACK))
-        w4_dealt_scales = tile("w4_dealt_scales", [P, N], U8, "gain2_8")
+        w4_dealt_scales = tile("w4_dealt_scales", [P, N], U8)
         nc.gpsimd.tensor_copy(
             w4_dealt_scales[:].rearrange("p (t m) -> p t m", t=PACK),
             w4_plane[:].rearrange("p (m t) -> p t m", t=PACK))
 
-        z_woven = tile("z_woven", [P, T2, PACK], BF16)
-        for t in range(2):
-            place(t, list3, whole, first[t])
-            nc.scalar.activation(z_woven[:, :, t], page[t][:], ACT.Relu)
         place(2, list3, whole, first[2])
-        for cols in (slice(0, 1280), slice(1280, T2)):
-            nc.scalar.activation(z_woven[:, cols, 2:4],
-                                 page[2][:, cols].unsqueeze(2).to_broadcast([P, cols.stop - cols.start, 2]), ACT.Relu)
+        nc.scalar.activation(pairs[:, 1, :, :], page[2][:, half:].unsqueeze(2).to_broadcast([P, half, 2]), ACT.Relu)
+        nc.gpsimd.tensor_copy(
+            z_paired[:].rearrange("p m t -> p (m t)").bitcast(I32).rearrange("p (m h) -> p m h", h=2),
+            pairs[:].rearrange("p h m t -> p (h m t)").bitcast(I32).rearrange("p (h m) -> p m h", h=2))
+        nc.scalar.activation(z_direct[:, :, 2:4], page[2][:, :half].unsqueeze(2).to_broadcast([P, half, 2]), ACT.Relu)
 
         place(3, list3, whole, first[3])
         z_codes = tile("z_codes", [P, T2], U32)
@@ -314,18 +329,21 @@ def tile_list_woven_tile_denoise_kernel(
 
         def make_z(start, width):
             cols = slice(start, start + width)
-            nc.vector.tensor_scalar_max(z_woven[:, cols, PACK - 1], page[PACK - 1][:, cols], 0.0)
+            if start == SHARED:
+                nc.scalar.activation(z_woven(cols)[:, :, PACK - 1], page[PACK - 1][:, cols], ACT.Relu)
+            else:
+                nc.vector.tensor_scalar_max(z_woven(cols)[:, :, PACK - 1], page[PACK - 1][:, cols], 0.0)
 
         def quantise_z(c):
             cols = slice(starts[c], starts[c] + CHUNKS[c])
             nc.vector.quantize_mx(out=z_codes[:, cols].bitcast(FP8X4), scales=z_scales[:, cols],
-                                  in_=z_woven[:, cols, :].rearrange("p m t -> p (m t)"))
+                                  in_=z_woven(cols).rearrange("p m t -> p (m t)"))
 
-        def multiply(c):
+        def multiply(c, row_tiles):
             width = CHUNKS[c]
             cols = slice(starts[c], starts[c] + width)
             y = y_tiles[cols.start // BANK][:, :, cols.start % BANK : cols.start % BANK + width]
-            for t in range(PACK):
+            for t in row_tiles:
                 rows = slice(P * t, P * (t + 1))
                 acc = bank("y_%d_%d" % (c, t), (4 * c + t) % 8)
                 nc.tensor.matmul_mx(out=acc[:, :width], lhsT=w4_dealt[:, rows].bitcast(FP8X4), lhsT_scale=w4_dealt_scales[:, rows],
@@ -347,38 +365,45 @@ def tile_list_woven_tile_denoise_kernel(
             cols = slice(BANK * quarter + within.start, BANK * quarter + within.stop)
             nc.vector.quantize_mx(out=y_codes[:, cols].bitcast(FP8X4), scales=y_scales[4 * quarter :, within], in_=woven[:])
 
-        def store_words(first, last):
-            cols = slice(BANK * first, BANK * (last + 1))
+        def store_words(start, stop):
+            cols = slice(start, stop)
             nc.sync.dma_start(out_words[:, cols], y_codes[:, cols])
 
         def store_scales():
             for q in range(4):
-                nc.scalar.dma_start(
+                (nc.scalar, nc.sync)[q % 2].dma_start(
                     out_2[0, 4 * q : 4 * q + 4, :].rearrange("r (j c) -> j r c", j=4).bitcast(I32),
                     y_scales[32 * q : 32 * q + 16, :].bitcast(I32))
 
         full, lower, upper = slice(0, BANK), slice(0, BANK // 2), slice(BANK // 2, BANK)
         count = len(CHUNKS)
-        make_z(0, CHUNKS[0])
+        make_z(SHARED, BANK - SHARED)
+        pieces = [(starts[c], CHUNKS[c]) for c in range(2)] + [(start, BANK // 2) for start in range(BANK, T2, BANK // 2)]
         woven = {}
-        for c in range(count):
-            if c + 1 < count:
-                make_z(starts[c + 1], CHUNKS[c + 1] // 2)
-            else:
-                woven[0] = weave_y(0, full, "prev0", nc.vector.tensor_copy)
+        for c in range(count - 1):
+            needed = [piece for piece in pieces if piece[0] < starts[c] + CHUNKS[c]]
+            for piece in pieces[: len(needed) + 1]:
+                make_z(*piece)
+            pieces = pieces[len(needed) + 1 :]
             quantise_z(c)
-            multiply(c)
-            if c + 1 < count:
-                make_z(starts[c + 1] + CHUNKS[c + 1] // 2, CHUNKS[c + 1] // 2)
+            multiply(c, range(PACK if c + 2 < count else 2))
+        make_z(*pieces[0])
+        woven[0] = weave_y(0, full, "prev0", nc.vector.tensor_copy)
+        quantise_z(count - 1)
+        quantise_y(0, full, woven[0])
+        store_words(0, BANK)
+        multiply(count - 2, (2, 3))
+        multiply(count - 1, (0, 1))
         for q in (1, 2):
             woven[q] = weave_y(q, full, "prev%d" % q, nc.vector.tensor_copy)
-            quantise_y(q - 1, full, woven[q - 1])
-        store_words(0, 1)
+        quantise_y(1, full, woven[1])
+        store_words(BANK, 2 * BANK)
+        multiply(count - 1, (2, 3))
         quantise_y(2, full, woven[2])
-        store_words(2, 2)
         by_vector = weave_y(3, lower, "prev3", nc.vector.tensor_copy)
         by_scalar = weave_y(3, upper, "gain1_0", nc.scalar.copy)
         quantise_y(3, lower, by_vector)
+        store_words(2 * BANK, T2 - BANK // 2)
         quantise_y(3, upper, by_scalar)
-        store_words(3, 3)
+        store_words(T2 - BANK // 2, T2)
         store_scales()

@@ -20,14 +20,14 @@ P = 128
 PACK = 4
 BANK = 512
 TINY = 2.0 ** -63
-OVERLAID = {"w3_raw": 0, "v2_words": 0, "v_words0": 4096, "page2": 8192, "w2_raw1": 12288, "firsts1": 16384,
-            "firsts0": 28672, "y2": 16384, "gain2_4": 32768, "w2_bf": 34816, "values5": 34304,
-            "values6": 35328, "values7": 37376, "values8": 39424,
+OVERLAID = {"w3_raw": 0, "v2_words": 0, "v_words0": 4096, "page2": 8192, "w2_raw1_0": 12288, "w2_raw1_1": 16384,
+            "first1": 16384, "factors": 20480, "first0": 28672, "y2": 16384, "gain2_5": 32768, "w2_bf": 34816,
+            "values6": 33792,
             "sizes0": 43008, "sizes1": 43008, "z_direct": 38912, "pairs": 47104, "shrink3": 55296,
             "shrink2": 59392, "z_paired": 55296, "gain2_8": 63488, "gained0": 63488, "gained1": 63488,
             "gained2": 63488, "gained3": 63488, "w4_dealt": 63488, "w4_dealt_scales": 65536}
-PIECES = ((0, 0, 256), (1, 0, 384), (0, 256, 768), (1, 384, 1024), (2, 0, 512),
-          (0, 768, 1024), (3, 0, 512), (2, 512, 1024), (3, 512, 1024))
+PIECES = ((0, 0, 256), (1, 0, 384), (0, 256, 768), (1, 384, 1024), (0, 768, 1024),
+          (2, 0, 512), (3, 0, 512), (2, 512, 1024), (3, 512, 1024))
 CHUNKS = (128, 128, 256, 512, 512, 512)
 ROWS_A_STORE = (2, 2, 2, 1, 1, 2)
 SHARED = 256
@@ -72,7 +72,7 @@ def tile_list_woven_tile_denoise_kernel(
             return plane
 
         def load_weight(name, rows):
-            raw = tile(name, [P, PACK, H], F32)
+            raw = tile(name, [P, PACK, rows.shape[1]], F32)
             nc.sync.dma_start(raw[:], rows.rearrange("(p i) c -> p i c", i=PACK))
             return raw
 
@@ -104,14 +104,16 @@ def tile_list_woven_tile_denoise_kernel(
 
         def round_weight(name, passes):
             woven = tile(name + "_bf", [P, len(passes), H * PACK], BF16)
-            for a, raw in enumerate(passes):
-                dealt = woven[:, a, :].rearrange("p (t m i) -> p m t i", t=PACK, i=PACK)
-                given = raw[:].rearrange("p i (m t) -> p m t i", t=PACK)
-                if len(passes) == 1:
-                    nc.scalar.copy(dealt[:, :, 0:2], given[:, :, 0:2])
-                    nc.gpsimd.tensor_scalar(dealt[:, :, 2:4], given[:, :, 2:4], 1.0, 0.0, ALU.mult, ALU.add)
-                else:
-                    nc.scalar.copy(dealt, given)
+            for a, parts in enumerate(passes):
+                span = P // len(parts)
+                for h, raw in enumerate(parts):
+                    dealt = woven[:, a, :].rearrange("p (t m i) -> p m t i", t=PACK, i=PACK)[:, span * h : span * (h + 1)]
+                    given = raw[:].rearrange("p i (m t) -> p m t i", t=PACK)
+                    if len(passes) == 1:
+                        nc.scalar.copy(dealt[:, :, 0:2], given[:, :, 0:2])
+                        nc.gpsimd.tensor_scalar(dealt[:, :, 2:4], given[:, :, 2:4], 1.0, 0.0, ALU.mult, ALU.add)
+                    else:
+                        nc.scalar.copy(dealt, given)
             return woven
 
         def quantise_weight(name, passes):
@@ -144,8 +146,8 @@ def tile_list_woven_tile_denoise_kernel(
         load_piece(0)
         list4 = load_list("list4", offs4)
         tab_w.append(load_words("tab_w1", tab_words[1]))
-        load_piece(1)
-        load_piece(2)
+        for n in (1, 2, 3, 4):
+            load_piece(n)
         level_t = tile("level_t", [P, PACK], F32)
         nc.sync.dma_start(level_t[:], level.rearrange("(p t) -> p t", t=PACK))
 
@@ -156,7 +158,7 @@ def tile_list_woven_tile_denoise_kernel(
 
         v_rows = gather("v_rows", tab_rows[:], list1, U8)
         v2_scales = gather("v2_scales", tab2_rows[:], list2, U8)
-        w3_codes, w3_scales = quantise_weight("w3", [w3_raw])
+        w3_codes, w3_scales = quantise_weight("w3", [[w3_raw]])
         w1_dealt_scales = tile("w1_dealt_scales", [P, 2 * H], U8, "w3_bf")
         nc.gpsimd.tensor_copy(
             w1_dealt_scales[:].rearrange("p (a t m) -> p a t m", a=2, t=PACK),
@@ -170,14 +172,13 @@ def tile_list_woven_tile_denoise_kernel(
                 nc.sync.dma_start(v_scales[32 * q : 32 * q + 4, S * a : S * (a + 1)].bitcast(I32),
                                   v_rows[start : start + 4, :].bitcast(I32))
 
-        w2_raw = [load_weight("w2_raw0", w2[0:512, :])]
-        load_piece(3)
+        w2_raw = [[load_weight("w2_raw0", w2[0:512, :])]]
         w1_raw = tile("w1_raw", [P, 2, 2 * H], U8)
         nc.sync.dma_start(w1_raw[:].bitcast(I32), w1_words.rearrange("a p c -> p a c").bitcast(I32))
         seat_scales(0)
-        w2_raw.append(load_weight("w2_raw1", w2[512:1024, :]))
+        w2_raw.append([load_weight("w2_raw1_%d" % h, w2[512:1024, H // 2 * h : H // 2 * (h + 1)]) for h in range(2)])
         seat_scales(1)
-        for n in (4, 5, 6):
+        for n in (5, 6):
             load_piece(n)
         list3 = load_list("list3", offs3)
         load_piece(7)
@@ -189,7 +190,7 @@ def tile_list_woven_tile_denoise_kernel(
             nc.sync.dma_start(w4_plane[32 * q : 32 * q + 4, :].bitcast(I32),
                               w4_scales[0, 4 * q : 4 * q + 4, :].bitcast(I32))
 
-        page, second, shrink = {}, {}, {}
+        page, second, logged, shrink = {}, {}, {}, {}
 
         def second_product(t, u):
             rows = slice(P * t, P * (t + 1))
@@ -228,16 +229,15 @@ def tile_list_woven_tile_denoise_kernel(
             nc.scalar.copy(second[t][:, halves[u]], sums[t, u][:])
         place_second(0, second_values(0))
         v_words.append(gather("v_words1", tab_w[1][:].bitcast(U32), list1, U32))
-        for n in (1, 2, 3):
+        for n in (1, 2, 3, 4):
             place_second(n, second_values(n))
         w1_dealt = tile("w1_dealt", [P, 2, 2 * H], U8)
         nc.gpsimd.tensor_copy(
             w1_dealt[:].bitcast(U16).rearrange("p a (t m) -> p a t m", t=PACK),
             w1_raw[:].bitcast(U16).rearrange("p a (m t) -> p a t m", t=PACK))
         w2_codes, w2_scales = quantise_weight("w2", w2_raw)
-        later_firsts = tile("firsts1", [P, 3 * S], F32)
-        first = [tile("firsts0", [P, S], F32)[:]] + [later_firsts[:, S * t : S * (t + 1)] for t in range(3)]
-        for n in range(4, len(PIECES)):
+        first = {t: tile("first%d" % t, [P, S], F32)[:] for t in range(2)}
+        for n in range(5, len(PIECES)):
             place_second(n, second_values(n))
 
         def first_product(t):
@@ -256,7 +256,7 @@ def tile_list_woven_tile_denoise_kernel(
             sizes = tile("sizes%d" % pair, [P, 2, S], F32, "sizes")
             for t in (2 * pair, 2 * pair + 1):
                 for u, cols in enumerate(halves):
-                    acc = bank("b_%d_%d" % (t, u), 2 * t + u)
+                    acc = bank("b_%d_%d" % (t, u), (2 * t + u + 4) % 8)
                     for a in range(2):
                         rows = slice(H * a + P * t, H * a + P * (t + 1))
                         nc.tensor.matmul_mx(out=acc[:], lhsT=w2_codes[:, rows].bitcast(FP8X4), lhsT_scale=w2_scales[:, rows],
@@ -266,21 +266,26 @@ def tile_list_woven_tile_denoise_kernel(
             if pair == 0:
                 logs = tile("logs", [P, 2, S], F32)
                 nc.scalar.activation(logs[:], sizes[:], ACT.Ln, bias=TINY)
-                shrink[0], shrink[1] = logs[:, 0, :], logs[:, 1, :]
+                factors = tile("factors", [P, 2, S], F32)
+                for t in (0, 1):
+                    logged[t], shrink[t] = logs[:, t, :], factors[:, t, :]
             else:
                 for t in (2, 3):
-                    shrink[t] = tile("shrink%d" % t, [P, S], F32)[:]
+                    logged[t] = shrink[t] = tile("shrink%d" % t, [P, S], F32)[:]
                     nc.scalar.activation(shrink[t], sizes[:, t % 2, :], ACT.Ln, bias=TINY)
 
         def first_values(t):
-            nc.scalar.activation(shrink[t], shrink[t], ACT.Sigmoid, bias=neg_log_level[:, t : t + 1], scale=2.0)
+            nc.scalar.activation(shrink[t], logged[t], ACT.Sigmoid, bias=neg_log_level[:, t : t + 1], scale=2.0)
             gained = tile("gained%d" % t, [P, S], F32)
             nc.gpsimd.tensor_tensor(gained[:], first[t], gain1[t][:], ALU.mult)
             nc.gpsimd.tensor_tensor(first[t], gained[:], shrink[t], ALU.mult)
 
-        for t in range(PACK):
-            first_product(t)
         for pair in range(2):
+            if pair:
+                later = tile("later_firsts", [P, 2, S], F32, "logs")
+                first[2], first[3] = later[:, 0, :], later[:, 1, :]
+            first_product(2 * pair)
+            first_product(2 * pair + 1)
             log_magnitudes(pair)
             first_values(2 * pair)
             first_values(2 * pair + 1)

@@ -21,13 +21,13 @@ PACK = 4
 BANK = 512
 TINY = 2.0 ** -63
 OVERLAID = {"w3_raw": 0, "v2_words": 0, "v_words0": 4096, "page2": 8192, "w2_raw1_0": 12288, "w2_raw1_1": 16384,
-            "first1": 16384, "factors": 20480, "first0": 28672, "y2": 16384, "gain2_5": 32768, "w2_bf": 34816,
-            "values6": 33792,
+            "first1": 16384, "factors": 20480, "first0": 28672, "y2": 16384, "gain2_4": 32768, "w2_bf": 34816,
+            "values5": 34304, "values6": 35328, "values7": 37376, "values8": 39424,
             "sizes0": 43008, "sizes1": 43008, "z_direct": 38912, "pairs": 47104, "shrink3": 55296,
-            "shrink2": 59392, "z_paired": 55296, "gain2_8": 63488, "gained0": 63488, "gained1": 63488,
-            "gained2": 63488, "gained3": 63488, "w4_dealt": 63488, "w4_dealt_scales": 65536}
-PIECES = ((0, 0, 256), (1, 0, 384), (0, 256, 768), (1, 384, 1024), (0, 768, 1024),
-          (2, 0, 512), (3, 0, 512), (2, 512, 1024), (3, 512, 1024))
+            "shrink2": 59392, "z_paired": 55296, "gain2_8": 63488, "gained": 63488,
+            "w4_dealt": 63488, "w4_dealt_scales": 65536}
+PIECES = ((0, 0, 256), (1, 0, 384), (0, 256, 768), (1, 384, 1024), (2, 0, 512),
+          (0, 768, 1024), (3, 0, 512), (2, 512, 1024), (3, 512, 1024))
 CHUNKS = (128, 128, 256, 512, 512, 512)
 ROWS_A_STORE = (2, 2, 2, 1, 1, 2)
 SHARED = 256
@@ -146,8 +146,8 @@ def tile_list_woven_tile_denoise_kernel(
         load_piece(0)
         list4 = load_list("list4", offs4)
         tab_w.append(load_words("tab_w1", tab_words[1]))
-        for n in (1, 2, 3, 4):
-            load_piece(n)
+        load_piece(1)
+        load_piece(2)
         level_t = tile("level_t", [P, PACK], F32)
         nc.sync.dma_start(level_t[:], level.rearrange("(p t) -> p t", t=PACK))
 
@@ -173,12 +173,13 @@ def tile_list_woven_tile_denoise_kernel(
                                   v_rows[start : start + 4, :].bitcast(I32))
 
         w2_raw = [[load_weight("w2_raw0", w2[0:512, :])]]
+        load_piece(3)
         w1_raw = tile("w1_raw", [P, 2, 2 * H], U8)
         nc.sync.dma_start(w1_raw[:].bitcast(I32), w1_words.rearrange("a p c -> p a c").bitcast(I32))
         seat_scales(0)
         w2_raw.append([load_weight("w2_raw1_%d" % h, w2[512:1024, H // 2 * h : H // 2 * (h + 1)]) for h in range(2)])
         seat_scales(1)
-        for n in (5, 6):
+        for n in (4, 5, 6):
             load_piece(n)
         list3 = load_list("list3", offs3)
         load_piece(7)
@@ -229,7 +230,7 @@ def tile_list_woven_tile_denoise_kernel(
             nc.scalar.copy(second[t][:, halves[u]], sums[t, u][:])
         place_second(0, second_values(0))
         v_words.append(gather("v_words1", tab_w[1][:].bitcast(U32), list1, U32))
-        for n in (1, 2, 3, 4):
+        for n in (1, 2, 3):
             place_second(n, second_values(n))
         w1_dealt = tile("w1_dealt", [P, 2, 2 * H], U8)
         nc.gpsimd.tensor_copy(
@@ -237,7 +238,7 @@ def tile_list_woven_tile_denoise_kernel(
             w1_raw[:].bitcast(U16).rearrange("p a (m t) -> p a t m", t=PACK))
         w2_codes, w2_scales = quantise_weight("w2", w2_raw)
         first = {t: tile("first%d" % t, [P, S], F32)[:] for t in range(2)}
-        for n in range(5, len(PIECES)):
+        for n in range(4, len(PIECES)):
             place_second(n, second_values(n))
 
         def first_product(t):
@@ -274,11 +275,13 @@ def tile_list_woven_tile_denoise_kernel(
                     logged[t] = shrink[t] = tile("shrink%d" % t, [P, S], F32)[:]
                     nc.scalar.activation(shrink[t], sizes[:, t % 2, :], ACT.Ln, bias=TINY)
 
-        def first_values(t):
+        def factor(t):
             nc.scalar.activation(shrink[t], logged[t], ACT.Sigmoid, bias=neg_log_level[:, t : t + 1], scale=2.0)
-            gained = tile("gained%d" % t, [P, S], F32)
-            nc.gpsimd.tensor_tensor(gained[:], first[t], gain1[t][:], ALU.mult)
-            nc.gpsimd.tensor_tensor(first[t], gained[:], shrink[t], ALU.mult)
+
+        def first_values(t, cols):
+            gained = tile("gained", [P, cols.stop - cols.start], F32)
+            nc.gpsimd.tensor_tensor(gained[:], first[t][:, cols], gain1[t][:, cols], ALU.mult)
+            nc.gpsimd.tensor_tensor(first[t][:, cols], gained[:], shrink[t][:, cols], ALU.mult)
 
         for pair in range(2):
             if pair:
@@ -287,8 +290,11 @@ def tile_list_woven_tile_denoise_kernel(
             first_product(2 * pair)
             first_product(2 * pair + 1)
             log_magnitudes(pair)
-            first_values(2 * pair)
-            first_values(2 * pair + 1)
+            factor(2 * pair)
+            factor(2 * pair + 1)
+            for cols in ([whole] if pair else halves):
+                first_values(2 * pair, cols)
+                first_values(2 * pair + 1, cols)
 
         half = T2 // 2
         z_direct = tile("z_direct", [P, half, PACK], BF16)
@@ -301,7 +307,9 @@ def tile_list_woven_tile_denoise_kernel(
             return z_paired[:, cols.start - half : cols.stop - half, :]
 
         for t in range(2):
-            place(t, list3, whole, first[t])
+            place(t, list3, halves[0], first[t][:, halves[0]])
+        for t in range(2):
+            place(t, list3, halves[1], first[t][:, halves[1]])
             nc.scalar.activation(pairs[:, 0, :, t], page[t][:, half:], ACT.Relu)
             nc.scalar.activation(z_direct[:, :, t], page[t][:, :half], ACT.Relu)
         w4_dealt = tile("w4_dealt", [P, N], I32)

@@ -18,19 +18,29 @@ ACT = mybir.ActivationFunctionType
 
 P = 128
 PACK = 4
+K_PASS = P * PACK
 BANK = 512
+QUADRANTS = (0, 2, 1, 3)
 TINY = 2.0 ** -63
-OVERLAID = {"w3_raw": 0, "v2_words": 0, "v_words0": 4096, "page2": 8192, "w2_raw1_0": 12288, "w2_raw1_1": 16384,
-            "first1": 16384, "factors": 20480, "first0": 28672, "y2": 16384, "gain2_4": 32768, "w2_bf": 34816,
-            "values5": 34304, "values6": 35328, "values7": 37376, "values8": 39424,
-            "sizes0": 43008, "sizes1": 43008, "z_direct": 38912, "pairs": 47104, "shrink3": 55296,
-            "shrink2": 59392, "z_paired": 55296, "gain2_8": 63488, "gained": 63488,
-            "w4_dealt": 63488, "w4_dealt_scales": 65536}
+
+OVERLAID = {
+    "w3_raw": 0, "v2_words": 0, "v_words0": 4096,
+    "page2": 8192, "w2_raw1": 12288, "first1": 16384, "factors": 20480, "first0": 28672,
+    "y2": 16384,
+    "gain2_4": 32768, "w2_bf": 34816, "values5": 34304, "values6": 35328, "values7": 37376, "values8": 39424,
+    "sizes0": 43008, "sizes1": 43008, "z_direct": 38912, "pairs": 47104,
+    "shrink3": 55296, "shrink2": 59392, "z_paired": 55296,
+    "gain2_8": 63488, "gained": 63488,
+    "w4_dealt": 63488, "w4_dealt_scales": 65536,
+}
+
 PIECES = ((0, 0, 256), (1, 0, 384), (0, 256, 768), (1, 384, 1024), (2, 0, 512),
           (0, 768, 1024), (3, 0, 512), (2, 512, 1024), (3, 512, 1024))
+AHEAD_OF_W2 = 4
+
 CHUNKS = (128, 128, 256, 512, 512, 512)
 ROWS_A_STORE = (2, 2, 2, 1, 1, 2)
-SHARED = 256
+SCALAR_CHUNK = 2
 
 
 def tile_list_woven_tile_denoise_kernel(
@@ -72,7 +82,7 @@ def tile_list_woven_tile_denoise_kernel(
             return plane
 
         def load_weight(name, rows):
-            raw = tile(name, [P, PACK, rows.shape[1]], F32)
+            raw = tile(name, [P, PACK, H], F32)
             nc.sync.dma_start(raw[:], rows.rearrange("(p i) c -> p i c", i=PACK))
             return raw
 
@@ -81,7 +91,7 @@ def tile_list_woven_tile_denoise_kernel(
         gain2 = {}
 
         def load_gain(held, rows):
-            for q in (0, 2, 1, 3):
+            for q in QUADRANTS:
                 nc.sync.dma_start(held[32 * q : 32 * q + 32], rows)
 
         def load_piece(n):
@@ -90,9 +100,9 @@ def tile_list_woven_tile_denoise_kernel(
             gain2[n] = tile("gain2_%d" % n, [P, stop - start], F32)
             load_gain(gain2[n][:], wg2.rearrange("(m t) j -> m t j", t=PACK)[:, t, start:stop])
 
-        def gather(name, window, offsets, dtype, pieces=(whole,)):
+        def gather(name, window, offsets, dtype, ranges=(whole,)):
             picked = tile(name, [P, S], dtype)
-            for cols in pieces:
+            for cols in ranges:
                 nc.vector.tensor_copy(picked[:, cols], window.indirect(offsets[:, cols.start // 16 : cols.stop // 16]))
             return picked
 
@@ -104,16 +114,14 @@ def tile_list_woven_tile_denoise_kernel(
 
         def round_weight(name, passes):
             woven = tile(name + "_bf", [P, len(passes), H * PACK], BF16)
-            for a, parts in enumerate(passes):
-                span = P // len(parts)
-                for h, raw in enumerate(parts):
-                    dealt = woven[:, a, :].rearrange("p (t m i) -> p m t i", t=PACK, i=PACK)[:, span * h : span * (h + 1)]
-                    given = raw[:].rearrange("p i (m t) -> p m t i", t=PACK)
-                    if len(passes) == 1:
-                        nc.scalar.copy(dealt[:, :, 0:2], given[:, :, 0:2])
-                        nc.gpsimd.tensor_scalar(dealt[:, :, 2:4], given[:, :, 2:4], 1.0, 0.0, ALU.mult, ALU.add)
-                    else:
-                        nc.scalar.copy(dealt, given)
+            for g, raw in enumerate(passes):
+                dealt = woven[:, g, :].rearrange("p (t m i) -> p m t i", t=PACK, i=PACK)
+                given = raw[:].rearrange("p i (m t) -> p m t i", t=PACK)
+                if name == "w3":
+                    nc.scalar.copy(dealt[:, :, 0:2], given[:, :, 0:2])
+                    nc.gpsimd.tensor_scalar(dealt[:, :, 2:4], given[:, :, 2:4], 1.0, 0.0, ALU.mult, ALU.add)
+                else:
+                    nc.scalar.copy(dealt, given)
             return woven
 
         def quantise_weight(name, passes):
@@ -121,7 +129,7 @@ def tile_list_woven_tile_denoise_kernel(
             codes = tile(name + "_codes", [P, len(passes) * H], U32)
             scales = tile(name + "_scales", [P, len(passes) * H], U8)
             nc.vector.quantize_mx(out=codes[:].bitcast(FP8X4), scales=scales[:],
-                                  in_=woven[:].rearrange("p a c -> p (a c)"))
+                                  in_=woven[:].rearrange("p g c -> p (g c)"))
             return codes, scales
 
         tab2_rows = zeroed_plane("tab2_rows", T)
@@ -131,17 +139,17 @@ def tile_list_woven_tile_denoise_kernel(
         w4_plane = zeroed_plane("w4_plane", N)
 
         list1 = load_list("list1", offs)
-        nc.sync.dma_start(tab_rows[0:32, :].bitcast(I32), tab_scales.rearrange("a q c -> (a q) c").bitcast(I32))
+        nc.sync.dma_start(tab_rows[0:32, :].bitcast(I32), tab_scales.rearrange("g q c -> (g q) c").bitcast(I32))
         list2 = load_list("list2", offs2)
-        for q in (0, 2, 1, 3):
+        for q in QUADRANTS:
             nc.sync.dma_start(tab2_rows[32 * q : 32 * q + 4, :].bitcast(I32),
                               tab2_scales[0, 4 * q : 4 * q + 4, :].bitcast(I32))
         w3_raw = load_weight("w3_raw", w3)
         tab2_w = load_words("tab2_w", tab2_words[0])
-        for q in (0, 2, 1, 3):
+        for q in QUADRANTS:
             nc.sync.dma_start(
-                w1_plane[32 * q : 32 * q + 4, :].rearrange("p (a c) -> p a c", a=2).bitcast(I32),
-                w1_scales[:, 4 * q : 4 * q + 4, :].rearrange("a r c -> r a c").bitcast(I32))
+                w1_plane[32 * q : 32 * q + 4, :].rearrange("p (g c) -> p g c", g=2).bitcast(I32),
+                w1_scales[:, 4 * q : 4 * q + 4, :].rearrange("g r c -> r g c").bitcast(I32))
         tab_w = [load_words("tab_w0", tab_words[0])]
         load_piece(0)
         list4 = load_list("list4", offs4)
@@ -158,26 +166,26 @@ def tile_list_woven_tile_denoise_kernel(
 
         v_rows = gather("v_rows", tab_rows[:], list1, U8)
         v2_scales = gather("v2_scales", tab2_rows[:], list2, U8)
-        w3_codes, w3_scales = quantise_weight("w3", [[w3_raw]])
+        w3_codes, w3_scales = quantise_weight("w3", [w3_raw])
         w1_dealt_scales = tile("w1_dealt_scales", [P, 2 * H], U8, "w3_bf")
         nc.gpsimd.tensor_copy(
-            w1_dealt_scales[:].rearrange("p (a t m) -> p a t m", a=2, t=PACK),
-            w1_plane[:].rearrange("p (a m t) -> p a t m", a=2, t=PACK))
+            w1_dealt_scales[:].rearrange("p (g t m) -> p g t m", g=2, t=PACK),
+            w1_plane[:].rearrange("p (g m t) -> p g t m", g=2, t=PACK))
         v2_words = gather("v2_words", tab2_w[:].bitcast(U32), list2, U32, halves)
         v_words = [gather("v_words0", tab_w[0][:].bitcast(U32), list1, U32)]
 
-        def seat_scales(a):
+        def seat_scales(g):
             for q in range(4):
-                start = 16 * a + 4 * q
-                nc.sync.dma_start(v_scales[32 * q : 32 * q + 4, S * a : S * (a + 1)].bitcast(I32),
+                start = 16 * g + 4 * q
+                nc.sync.dma_start(v_scales[32 * q : 32 * q + 4, S * g : S * (g + 1)].bitcast(I32),
                                   v_rows[start : start + 4, :].bitcast(I32))
 
-        w2_raw = [[load_weight("w2_raw0", w2[0:512, :])]]
+        w2_raw = [load_weight("w2_raw0", w2[:K_PASS, :])]
         load_piece(3)
         w1_raw = tile("w1_raw", [P, 2, 2 * H], U8)
-        nc.sync.dma_start(w1_raw[:].bitcast(I32), w1_words.rearrange("a p c -> p a c").bitcast(I32))
+        nc.sync.dma_start(w1_raw[:].bitcast(I32), w1_words.rearrange("g p c -> p g c").bitcast(I32))
         seat_scales(0)
-        w2_raw.append([load_weight("w2_raw1_%d" % h, w2[512:1024, H // 2 * h : H // 2 * (h + 1)]) for h in range(2)])
+        w2_raw.append(load_weight("w2_raw1", w2[K_PASS:, :]))
         seat_scales(1)
         for n in (4, 5, 6):
             load_piece(n)
@@ -213,15 +221,14 @@ def tile_list_woven_tile_denoise_kernel(
 
         def place(t, offsets, cols, values):
             if t not in page:
-                page[t] = tile("page%d" % t, [P, T2], F32, ("tab2_w", "tab_w0", "w2_raw0", "tab_w1")[t])
+                page[t] = tile("page%d" % t, [P, T2], F32, ("tab2_w", "tab_w0", None, "tab_w1")[t])
             nc.vector.tensor_copy(page[t][:].indirect(offsets[:, cols.start // 16 : cols.stop // 16]), values)
 
-
-        sums = {(t, u): second_product(t, u) for u in range(2) for t in range(PACK)}
         def place_second(n, values):
             t, start, stop = PIECES[n]
             place(t, list4, slice(start, stop), values)
 
+        sums = {(t, u): second_product(t, u) for u in range(2) for t in range(PACK)}
         lead = PIECES[0][2]
         nc.scalar.copy(second[0][:, :lead], sums[0, 0][:, :lead])
         nc.scalar.copy(second[1][:, halves[0]], sums[1, 0][:])
@@ -230,39 +237,41 @@ def tile_list_woven_tile_denoise_kernel(
             nc.scalar.copy(second[t][:, halves[u]], sums[t, u][:])
         place_second(0, second_values(0))
         v_words.append(gather("v_words1", tab_w[1][:].bitcast(U32), list1, U32))
-        for n in (1, 2, 3):
+        for n in range(1, AHEAD_OF_W2):
             place_second(n, second_values(n))
         w1_dealt = tile("w1_dealt", [P, 2, 2 * H], U8)
         nc.gpsimd.tensor_copy(
-            w1_dealt[:].bitcast(U16).rearrange("p a (t m) -> p a t m", t=PACK),
-            w1_raw[:].bitcast(U16).rearrange("p a (m t) -> p a t m", t=PACK))
+            w1_dealt[:].bitcast(U16).rearrange("p g (t m) -> p g t m", t=PACK),
+            w1_raw[:].bitcast(U16).rearrange("p g (m t) -> p g t m", t=PACK))
         w2_codes, w2_scales = quantise_weight("w2", w2_raw)
         first = {t: tile("first%d" % t, [P, S], F32)[:] for t in range(2)}
-        for n in range(4, len(PIECES)):
+        for n in range(AHEAD_OF_W2, len(PIECES)):
             place_second(n, second_values(n))
 
         def first_product(t):
             for u, cols in enumerate(halves):
                 acc = bank("a_%d_%d" % (t, u), 2 * t + u)
-                for a in range(2):
+                for g in range(2):
                     nc.tensor.matmul_mx(
-                        out=acc[:], lhsT=w1_dealt[:, a, 2 * P * t : 2 * P * (t + 1)].bitcast(FP4X4),
-                        lhsT_scale=w1_dealt_scales[:, H * a + P * t : H * a + P * (t + 1)],
-                        rhs=v_words[a][:, cols].bitcast(FP8X4),
-                        rhs_scale=v_scales[:, S * a + cols.start : S * a + cols.stop],
-                        start=(a == 0), stop=(a == 1))
+                        out=acc[:], lhsT=w1_dealt[:, g, 2 * P * t : 2 * P * (t + 1)].bitcast(FP4X4),
+                        lhsT_scale=w1_dealt_scales[:, H * g + P * t : H * g + P * (t + 1)],
+                        rhs=v_words[g][:, cols].bitcast(FP8X4),
+                        rhs_scale=v_scales[:, S * g + cols.start : S * g + cols.stop],
+                        start=(g == 0), stop=(g == 1))
                 nc.scalar.copy(first[t][:, cols], acc[:])
 
         def log_magnitudes(pair):
-            sizes = tile("sizes%d" % pair, [P, 2, S], F32, "sizes")
+            sizes = tile("sizes%d" % pair, [P, 2, S], F32)
             for t in (2 * pair, 2 * pair + 1):
                 for u, cols in enumerate(halves):
                     acc = bank("b_%d_%d" % (t, u), (2 * t + u + 4) % 8)
-                    for a in range(2):
-                        rows = slice(H * a + P * t, H * a + P * (t + 1))
-                        nc.tensor.matmul_mx(out=acc[:], lhsT=w2_codes[:, rows].bitcast(FP8X4), lhsT_scale=w2_scales[:, rows],
-                                            rhs=v_words[a][:, cols].bitcast(FP8X4), rhs_scale=v_scales[:, S * a + cols.start : S * a + cols.stop],
-                                            start=(a == 0), stop=(a == 1))
+                    for g in range(2):
+                        rows = slice(H * g + P * t, H * g + P * (t + 1))
+                        nc.tensor.matmul_mx(
+                            out=acc[:], lhsT=w2_codes[:, rows].bitcast(FP8X4), lhsT_scale=w2_scales[:, rows],
+                            rhs=v_words[g][:, cols].bitcast(FP8X4),
+                            rhs_scale=v_scales[:, S * g + cols.start : S * g + cols.stop],
+                            start=(g == 0), stop=(g == 1))
                     nc.scalar.activation(sizes[:, t % 2, cols], acc[:], ACT.Abs)
             if pair == 0:
                 logs = tile("logs", [P, 2, S], F32)
@@ -329,6 +338,7 @@ def tile_list_woven_tile_denoise_kernel(
         nc.scalar.activation(z_direct[:, :, 2:4], page[2][:, :half].unsqueeze(2).to_broadcast([P, half, 2]), ACT.Relu)
 
         place(3, list3, whole, first[3])
+
         z_codes = tile("z_codes", [P, T2], U32)
         z_scales = tile("z_scales", [P, T2], U8)
         y_codes = tile("y_codes", [P, T2], I32)
@@ -336,13 +346,12 @@ def tile_list_woven_tile_denoise_kernel(
         out_rows = out_0.rearrange("(p t) m -> p t m", t=PACK)
         out_words = out_1[0].rearrange("p m i -> p (m i)").bitcast(I32)
         starts = [sum(CHUNKS[:c]) for c in range(len(CHUNKS))]
-        quarters = T2 // BANK
-        y_tiles = [tile("y%d" % q, [P, PACK, BANK], F32, ("tab2_w", "w2_raw0", None, "tab_w0")[q])
-                   for q in range(quarters)]
+        y_tiles = [tile("y%d" % quarter, [P, PACK, BANK], F32, on)
+                   for quarter, on in enumerate(("tab2_w", "w2_raw0", None, "tab_w0"))]
 
-        def make_z(start, width):
+        def weave_last_row_tile(start, width):
             cols = slice(start, start + width)
-            if start == SHARED:
+            if start == starts[SCALAR_CHUNK]:
                 nc.scalar.activation(z_woven(cols)[:, :, PACK - 1], page[PACK - 1][:, cols], ACT.Relu)
             else:
                 nc.vector.tensor_scalar_max(z_woven(cols)[:, :, PACK - 1], page[PACK - 1][:, cols], 0.0)
@@ -358,7 +367,7 @@ def tile_list_woven_tile_denoise_kernel(
             y = y_tiles[cols.start // BANK][:, :, cols.start % BANK : cols.start % BANK + width]
             for t in row_tiles:
                 rows = slice(P * t, P * (t + 1))
-                acc = bank("y_%d_%d" % (c, t), (4 * c + t) % 8)
+                acc = bank("y_%d_%d" % (c, t), (PACK * c + t) % 8)
                 nc.tensor.matmul_mx(out=acc[:, :width], lhsT=w4_dealt[:, rows].bitcast(FP8X4), lhsT_scale=w4_dealt_scales[:, rows],
                                     rhs=z_codes[:, cols].bitcast(FP8X4), rhs_scale=z_scales[:, cols],
                                     start=True, stop=True)
@@ -390,25 +399,26 @@ def tile_list_woven_tile_denoise_kernel(
 
         full, lower, upper = slice(0, BANK), slice(0, BANK // 2), slice(BANK // 2, BANK)
         count = len(CHUNKS)
-        make_z(SHARED, BANK - SHARED)
-        pieces = [(starts[c], CHUNKS[c]) for c in range(2)] + [(start, BANK // 2) for start in range(BANK, T2, BANK // 2)]
+        weave_last_row_tile(starts[SCALAR_CHUNK], CHUNKS[SCALAR_CHUNK])
+        runs = [(starts[c], CHUNKS[c]) for c in range(SCALAR_CHUNK)]
+        runs = runs + [(start, BANK // 2) for start in range(BANK, T2, BANK // 2)]
         woven = {}
         for c in range(count - 1):
-            needed = [piece for piece in pieces if piece[0] < starts[c] + CHUNKS[c]]
-            for piece in pieces[: len(needed) + 1]:
-                make_z(*piece)
-            pieces = pieces[len(needed) + 1 :]
+            needed = [run for run in runs if run[0] < starts[c] + CHUNKS[c]]
+            for run in runs[: len(needed) + 1]:
+                weave_last_row_tile(*run)
+            runs = runs[len(needed) + 1 :]
             quantise_z(c)
             multiply(c, range(PACK if c + 2 < count else 2))
-        make_z(*pieces[0])
+        weave_last_row_tile(*runs[0])
         woven[0] = weave_y(0, full, "prev0", nc.vector.tensor_copy)
         quantise_z(count - 1)
         quantise_y(0, full, woven[0])
         store_words(0, BANK)
         multiply(count - 2, (2, 3))
         multiply(count - 1, (0, 1))
-        for q in (1, 2):
-            woven[q] = weave_y(q, full, "prev%d" % q, nc.vector.tensor_copy)
+        for quarter in (1, 2):
+            woven[quarter] = weave_y(quarter, full, "prev%d" % quarter, nc.vector.tensor_copy)
         quantise_y(1, full, woven[1])
         store_words(BANK, 2 * BANK)
         multiply(count - 1, (2, 3))

@@ -32,6 +32,8 @@ OVERLAID = {
     "shrink3": 55296, "shrink2": 59392, "z_paired": 55296,
     "gain2_8": 63488, "gained": 63488,
     "w4_dealt": 63488, "w4_dealt_scales": 65536,
+    "logs": 69120, "first2": 69120, "first3": 73216, "w4_first": 69120,
+    "gain2_3": 66560, "values4": 66560, "w1_later_scales": 68608,
 }
 
 PIECES = ((0, 0, 256), (1, 0, 384), (0, 256, 768), (1, 384, 1024), (2, 0, 512),
@@ -108,8 +110,8 @@ def tile_list_woven_tile_denoise_kernel(
 
         def scale_window(name):
             window = tile(name, [P, T], U8)
-            nc.gpsimd.memset(window[32:64, :].bitcast(I32), 0)
-            nc.gpsimd.memset(window[64:128, :].bitcast(I32), 0)
+            nc.vector.memset(window[32:64, :].bitcast(I32), 0)
+            nc.vector.memset(window[64:128, :].bitcast(I32), 0)
             return window
 
         def round_weight(name, passes):
@@ -167,10 +169,13 @@ def tile_list_woven_tile_denoise_kernel(
         v_rows = gather("v_rows", tab_rows[:], list1, U8)
         v2_scales = gather("v2_scales", tab2_rows[:], list2, U8)
         w3_codes, w3_scales = quantise_weight("w3", [w3_raw])
-        w1_dealt_scales = tile("w1_dealt_scales", [P, 2 * H], U8, "w3_bf")
-        nc.gpsimd.tensor_copy(
-            w1_dealt_scales[:].rearrange("p (g t m) -> p g t m", g=2, t=PACK),
-            w1_plane[:].rearrange("p (g m t) -> p g t m", g=2, t=PACK))
+        w1_dealt_scales = tile("w1_dealt_scales", [P, H], U8, "w3_bf")
+
+        def deal_w1_scales(held, g):
+            nc.gpsimd.tensor_copy(held.rearrange("p (t m) -> p t m", t=PACK),
+                                  w1_plane[:, H * g : H * (g + 1)].rearrange("p (m t) -> p t m", t=PACK))
+
+        deal_w1_scales(w1_dealt_scales[:], 0)
         v2_words = gather("v2_words", tab2_w[:].bitcast(U32), list2, U32, halves)
         v_words = [gather("v_words0", tab_w[0][:].bitcast(U32), list1, U32)]
 
@@ -180,8 +185,8 @@ def tile_list_woven_tile_denoise_kernel(
                 nc.sync.dma_start(v_scales[32 * q : 32 * q + 4, S * g : S * (g + 1)].bitcast(I32),
                                   v_rows[start : start + 4, :].bitcast(I32))
 
-        w2_raw = [load_weight("w2_raw0", w2[:K_PASS, :])]
         load_piece(3)
+        w2_raw = [load_weight("w2_raw0", w2[:K_PASS, :])]
         w1_raw = tile("w1_raw", [P, 2, 2 * H], U8)
         nc.sync.dma_start(w1_raw[:].bitcast(I32), w1_words.rearrange("g p c -> p g c").bitcast(I32))
         seat_scales(0)
@@ -194,10 +199,11 @@ def tile_list_woven_tile_denoise_kernel(
         load_piece(8)
         for t in range(PACK):
             load_gain(gain1[t][:], wg1.rearrange("(m t) j -> m t j", t=PACK)[:, t, :])
-        w4_raw = load_words("w4_raw", w4_words[0])
-        for q in range(4):
-            nc.sync.dma_start(w4_plane[32 * q : 32 * q + 4, :].bitcast(I32),
-                              w4_scales[0, 4 * q : 4 * q + 4, :].bitcast(I32))
+            if t == 1:
+                w4_raw = load_words("w4_raw", w4_words[0])
+                for q in range(4):
+                    nc.sync.dma_start(w4_plane[32 * q : 32 * q + 4, :].bitcast(I32),
+                                      w4_scales[0, 4 * q : 4 * q + 4, :].bitcast(I32))
 
         page, second, logged, shrink = {}, {}, {}, {}
 
@@ -240,7 +246,9 @@ def tile_list_woven_tile_denoise_kernel(
         for n in range(1, AHEAD_OF_W2):
             place_second(n, second_values(n))
         w1_dealt = tile("w1_dealt", [P, 2, 2 * H], U8)
-        nc.gpsimd.tensor_copy(
+        later_scales = tile("w1_later_scales", [P, H], U8)
+        deal_w1_scales(later_scales[:], 1)
+        nc.scalar.copy(
             w1_dealt[:].bitcast(U16).rearrange("p g (t m) -> p g t m", t=PACK),
             w1_raw[:].bitcast(U16).rearrange("p g (m t) -> p g t m", t=PACK))
         w2_codes, w2_scales = quantise_weight("w2", w2_raw)
@@ -254,7 +262,7 @@ def tile_list_woven_tile_denoise_kernel(
                 for g in range(2):
                     nc.tensor.matmul_mx(
                         out=acc[:], lhsT=w1_dealt[:, g, 2 * P * t : 2 * P * (t + 1)].bitcast(FP4X4),
-                        lhsT_scale=w1_dealt_scales[:, H * g + P * t : H * g + P * (t + 1)],
+                        lhsT_scale=(w1_dealt_scales, later_scales)[g][:, P * t : P * (t + 1)],
                         rhs=v_words[g][:, cols].bitcast(FP8X4),
                         rhs_scale=v_scales[:, S * g + cols.start : S * g + cols.stop],
                         start=(g == 0), stop=(g == 1))
@@ -294,8 +302,8 @@ def tile_list_woven_tile_denoise_kernel(
 
         for pair in range(2):
             if pair:
-                later = tile("later_firsts", [P, 2, S], F32, "logs")
-                first[2], first[3] = later[:, 0, :], later[:, 1, :]
+                for t in (2, 3):
+                    first[t] = tile("first%d" % t, [P, S], F32)[:]
             first_product(2 * pair)
             first_product(2 * pair + 1)
             log_magnitudes(pair)
@@ -321,10 +329,8 @@ def tile_list_woven_tile_denoise_kernel(
             place(t, list3, halves[1], first[t][:, halves[1]])
             nc.scalar.activation(pairs[:, 0, :, t], page[t][:, half:], ACT.Relu)
             nc.scalar.activation(z_direct[:, :, t], page[t][:, :half], ACT.Relu)
-        w4_dealt = tile("w4_dealt", [P, N], I32)
-        nc.gpsimd.tensor_copy(
-            w4_dealt[:].rearrange("p (t m) -> p t m", t=PACK),
-            w4_raw[:].rearrange("p (m t) -> p t m", t=PACK))
+        w4_dealt = tile("w4_dealt", [P, PACK - 1, P], I32)
+        nc.gpsimd.tensor_copy(w4_dealt[:], w4_raw[:].rearrange("p (m t) -> p t m", t=PACK)[:, 1:, :])
         w4_dealt_scales = tile("w4_dealt_scales", [P, N], U8)
         nc.gpsimd.tensor_copy(
             w4_dealt_scales[:].rearrange("p (t m) -> p t m", t=PACK),
@@ -335,7 +341,16 @@ def tile_list_woven_tile_denoise_kernel(
         nc.gpsimd.tensor_copy(
             z_paired[:].rearrange("p m t -> p (m t)").bitcast(I32).rearrange("p (m h) -> p m h", h=2),
             pairs[:].rearrange("p h m t -> p (h m t)").bitcast(I32).rearrange("p (h m) -> p m h", h=2))
-        nc.scalar.activation(z_direct[:, :, 2:4], page[2][:, :half].unsqueeze(2).to_broadcast([P, half, 2]), ACT.Relu)
+        w4_first = tile("w4_first", [P, P], U32)
+        for cols in halves:
+            nc.scalar.activation(z_direct[:, cols, 2:4], page[2][:, cols].unsqueeze(2).to_broadcast([P, BANK, 2]), ACT.Relu)
+            if cols.start == 0:
+                nc.scalar.copy(w4_first[:], w4_raw[:].bitcast(U32).rearrange("p (m t) -> p t m", t=PACK)[:, 0, :])
+        w4_stationary = [w4_first[:]] + [w4_dealt[:, t, :] for t in range(PACK - 1)]
+        for n in range(5):
+            idle = bank("warm%d" % n, 3 + n)
+            nc.tensor.matmul_mx(out=idle[:], lhsT=w4_first[:].bitcast(FP8X4), lhsT_scale=w4_dealt_scales[:, :P],
+                                rhs=w3_codes[:].bitcast(FP8X4), rhs_scale=w3_scales[:], start=True, stop=True)
 
         place(3, list3, whole, first[3])
 
@@ -368,7 +383,7 @@ def tile_list_woven_tile_denoise_kernel(
             for t in row_tiles:
                 rows = slice(P * t, P * (t + 1))
                 acc = bank("y_%d_%d" % (c, t), (PACK * c + t) % 8)
-                nc.tensor.matmul_mx(out=acc[:, :width], lhsT=w4_dealt[:, rows].bitcast(FP8X4), lhsT_scale=w4_dealt_scales[:, rows],
+                nc.tensor.matmul_mx(out=acc[:, :width], lhsT=w4_stationary[t].bitcast(FP8X4), lhsT_scale=w4_dealt_scales[:, rows],
                                     rhs=z_codes[:, cols].bitcast(FP8X4), rhs_scale=z_scales[:, cols],
                                     start=True, stop=True)
                 nc.scalar.copy(y[:, t, :], acc[:, :width])

@@ -41,7 +41,7 @@ PIECES = ((0, 0, 256), (1, 0, 384), (0, 256, 768), (1, 384, 1024), (2, 0, 512),
 AHEAD_OF_W2 = 4
 
 CHUNKS = (128, 128, 256, 512, 512, 512)
-ROWS_A_STORE = (2, 2, 2, 1, 1, 2)
+STORES = (((0, 2), (2, 4)),) * 3 + (((0, 1), (1, 2), (2, 4)),) + (((0, 2), (2, 4)),) * 2
 SCALAR_CHUNK = 2
 
 
@@ -376,7 +376,7 @@ def tile_list_woven_tile_denoise_kernel(
             nc.vector.quantize_mx(out=z_codes[:, cols].bitcast(FP8X4), scales=z_scales[:, cols],
                                   in_=z_woven(cols).rearrange("p m t -> p (m t)"))
 
-        def multiply(c, row_tiles):
+        def multiply(c, row_tiles, copy=nc.scalar.copy):
             width = CHUNKS[c]
             cols = slice(starts[c], starts[c] + width)
             y = y_tiles[cols.start // BANK][:, :, cols.start % BANK : cols.start % BANK + width]
@@ -386,10 +386,10 @@ def tile_list_woven_tile_denoise_kernel(
                 nc.tensor.matmul_mx(out=acc[:, :width], lhsT=w4_stationary[t].bitcast(FP8X4), lhsT_scale=w4_dealt_scales[:, rows],
                                     rhs=z_codes[:, cols].bitcast(FP8X4), rhs_scale=z_scales[:, cols],
                                     start=True, stop=True)
-                nc.scalar.copy(y[:, t, :], acc[:, :width])
-                if ROWS_A_STORE[c] == 1 or t % 2:
-                    stored = slice(t + 1 - ROWS_A_STORE[c], t + 1)
-                    nc.sync.dma_start(out_rows[:, stored, cols], y[:, stored, :])
+                copy(y[:, t, :], acc[:, :width])
+                for first_row, end in STORES[c]:
+                    if t + 1 == end:
+                        nc.sync.dma_start(out_rows[:, first_row:end, cols], y[:, first_row:end, :])
 
         def weave_y(quarter, within, on, copy):
             woven = tile("y_woven%d_%d" % (quarter, within.start), [P, (within.stop - within.start) * PACK], BF16, on)
@@ -408,40 +408,48 @@ def tile_list_woven_tile_denoise_kernel(
 
         def store_scales():
             for q in range(4):
-                (nc.scalar, nc.sync)[q % 2].dma_start(
+                nc.scalar.dma_start(
                     out_2[0, 4 * q : 4 * q + 4, :].rearrange("r (j c) -> j r c", j=4).bitcast(I32),
                     y_scales[32 * q : 32 * q + 16, :].bitcast(I32))
 
         full, lower, upper = slice(0, BANK), slice(0, BANK // 2), slice(BANK // 2, BANK)
-        count = len(CHUNKS)
+        run = BANK // 2
         weave_last_row_tile(starts[SCALAR_CHUNK], CHUNKS[SCALAR_CHUNK])
-        runs = [(starts[c], CHUNKS[c]) for c in range(SCALAR_CHUNK)]
-        runs = runs + [(start, BANK // 2) for start in range(BANK, T2, BANK // 2)]
-        woven = {}
-        for c in range(count - 1):
-            needed = [run for run in runs if run[0] < starts[c] + CHUNKS[c]]
-            for run in runs[: len(needed) + 1]:
-                weave_last_row_tile(*run)
-            runs = runs[len(needed) + 1 :]
-            quantise_z(c)
-            multiply(c, range(PACK if c + 2 < count else 2))
-        weave_last_row_tile(*runs[0])
-        woven[0] = weave_y(0, full, "prev0", nc.vector.tensor_copy)
-        quantise_z(count - 1)
+        weave_last_row_tile(starts[0], CHUNKS[0])
+        weave_last_row_tile(starts[1], CHUNKS[1])
+        quantise_z(0)
+        multiply(0, range(PACK))
+        weave_last_row_tile(2 * run, run)
+        quantise_z(1)
+        multiply(1, range(PACK))
+        weave_last_row_tile(3 * run, run)
+        quantise_z(2)
+        multiply(2, range(PACK))
+        weave_last_row_tile(4 * run, run)
+        quantise_z(3)
+        multiply(3, range(PACK - 1))
+        weave_last_row_tile(5 * run, run)
+        weave_last_row_tile(6 * run, run)
+        quantise_z(4)
+        weave_last_row_tile(7 * run, run)
+        multiply(3, (PACK - 1,), nc.vector.tensor_copy)
+        multiply(4, range(PACK))
+        quantise_z(5)
+        woven = {quarter: weave_y(quarter, full, "prev%d" % quarter, nc.vector.tensor_copy) for quarter in (0, 1)}
         quantise_y(0, full, woven[0])
         store_words(0, BANK)
-        multiply(count - 2, (2, 3))
-        multiply(count - 1, (0, 1))
-        for quarter in (1, 2):
-            woven[quarter] = weave_y(quarter, full, "prev%d" % quarter, nc.vector.tensor_copy)
+        multiply(5, range(PACK))
+        woven[2] = weave_y(2, full, "prev2", nc.vector.tensor_copy)
         quantise_y(1, full, woven[1])
-        store_words(BANK, 2 * BANK)
-        multiply(count - 1, (2, 3))
         quantise_y(2, full, woven[2])
-        by_vector = weave_y(3, lower, "prev3", nc.vector.tensor_copy)
-        by_scalar = weave_y(3, upper, "gain1_0", nc.scalar.copy)
-        quantise_y(3, lower, by_vector)
-        store_words(2 * BANK, T2 - BANK // 2)
-        quantise_y(3, upper, by_scalar)
+        store_words(BANK, 3 * BANK)
+        by_scalar = weave_y(3, lower, "prev3", nc.scalar.copy)
+        shared = tile("y_woven_last", [P, BANK // 2 * PACK], BF16, "gain1_0")
+        for within, copy in ((slice(0, P), nc.scalar.copy), (slice(P, 2 * P), nc.vector.tensor_copy)):
+            copy(shared[:, PACK * within.start : PACK * within.stop].rearrange("p (m i t) -> p m t i", i=4, t=PACK),
+                 y_tiles[3][:, :, upper.start + within.start : upper.start + within.stop].rearrange("p t (m i) -> p m t i", i=4))
+        quantise_y(3, lower, by_scalar)
+        store_words(3 * BANK, T2 - BANK // 2)
+        quantise_y(3, upper, shared)
         store_words(T2 - BANK // 2, T2)
         store_scales()

@@ -41,8 +41,8 @@ PIECES = ((0, 0, 256), (1, 0, 384), (0, 256, 768), (1, 384, 1024), (2, 0, 512),
 AHEAD_OF_W2 = 4
 
 CHUNKS = (128, 128, 256, 512, 512, 512)
-STORES = (((0, 2), (2, 4)),) * 3 + (((0, 1), (1, 2), (2, 4)),) + (((0, 2), (2, 4)),) * 2
-SCALAR_CHUNK = 2
+STORES = (((0, 2), (2, 4)),) * 3 + (((0, 1), (1, 2), (2, 3), (3, 4)),) * 2 + (((0, 2), (2, 4)),)
+SCALAR_RUN = slice(256, 640)
 
 
 def tile_list_woven_tile_denoise_kernel(
@@ -366,7 +366,7 @@ def tile_list_woven_tile_denoise_kernel(
 
         def weave_last_row_tile(start, width):
             cols = slice(start, start + width)
-            if start == starts[SCALAR_CHUNK]:
+            if SCALAR_RUN.start <= start < SCALAR_RUN.stop:
                 nc.scalar.activation(z_woven(cols)[:, :, PACK - 1], page[PACK - 1][:, cols], ACT.Relu)
             else:
                 nc.vector.tensor_scalar_max(z_woven(cols)[:, :, PACK - 1], page[PACK - 1][:, cols], 0.0)
@@ -376,19 +376,26 @@ def tile_list_woven_tile_denoise_kernel(
             nc.vector.quantize_mx(out=z_codes[:, cols].bitcast(FP8X4), scales=z_scales[:, cols],
                                   in_=z_woven(cols).rearrange("p m t -> p (m t)"))
 
-        def multiply(c, row_tiles, copy=nc.scalar.copy):
+        banks_used = []
+
+        def multiply(c, row_tiles, together=1, copy=nc.scalar.copy):
             width = CHUNKS[c]
             cols = slice(starts[c], starts[c] + width)
             y = y_tiles[cols.start // BANK][:, :, cols.start % BANK : cols.start % BANK + width]
-            for t in row_tiles:
-                rows = slice(P * t, P * (t + 1))
-                acc = bank("y_%d_%d" % (c, t), (PACK * c + t) % 8)
-                nc.tensor.matmul_mx(out=acc[:, :width], lhsT=w4_stationary[t].bitcast(FP8X4), lhsT_scale=w4_dealt_scales[:, rows],
-                                    rhs=z_codes[:, cols].bitcast(FP8X4), rhs_scale=z_scales[:, cols],
-                                    start=True, stop=True)
-                copy(y[:, t, :], acc[:, :width])
+            for first_tile in row_tiles[::together]:
+                acc = bank("y_%d_%d" % (c, first_tile), len(banks_used) % 8)
+                banks_used.append(acc)
+                for t in range(first_tile, first_tile + together):
+                    rows = slice(P * t, P * (t + 1))
+                    place_in_bank = slice(width * (t - first_tile), width * (t - first_tile + 1))
+                    nc.tensor.matmul_mx(out=acc[:, place_in_bank], lhsT=w4_stationary[t].bitcast(FP8X4),
+                                        lhsT_scale=w4_dealt_scales[:, rows],
+                                        rhs=z_codes[:, cols].bitcast(FP8X4), rhs_scale=z_scales[:, cols],
+                                        start=True, stop=True)
+                copy(y[:, first_tile : first_tile + together, :],
+                     acc[:, : together * width].rearrange("p (t c) -> p t c", t=together))
                 for first_row, end in STORES[c]:
-                    if t + 1 == end:
+                    if first_tile + together == end:
                         nc.sync.dma_start(out_rows[:, first_row:end, cols], y[:, first_row:end, :])
 
         def weave_y(quarter, within, on, copy):
@@ -408,40 +415,40 @@ def tile_list_woven_tile_denoise_kernel(
 
         def store_scales():
             for q in range(4):
-                nc.scalar.dma_start(
+                (nc.scalar, nc.sync)[q % 2].dma_start(
                     out_2[0, 4 * q : 4 * q + 4, :].rearrange("r (j c) -> j r c", j=4).bitcast(I32),
                     y_scales[32 * q : 32 * q + 16, :].bitcast(I32))
 
         full, lower, upper = slice(0, BANK), slice(0, BANK // 2), slice(BANK // 2, BANK)
         run = BANK // 2
-        weave_last_row_tile(starts[SCALAR_CHUNK], CHUNKS[SCALAR_CHUNK])
+        weave_last_row_tile(starts[2], CHUNKS[2])
+        weave_last_row_tile(starts[3], SCALAR_RUN.stop - starts[3])
         weave_last_row_tile(starts[0], CHUNKS[0])
         weave_last_row_tile(starts[1], CHUNKS[1])
         quantise_z(0)
-        multiply(0, range(PACK))
-        weave_last_row_tile(2 * run, run)
+        multiply(0, range(PACK), 2)
+        weave_last_row_tile(640, 256)
         quantise_z(1)
-        multiply(1, range(PACK))
-        weave_last_row_tile(3 * run, run)
+        multiply(1, range(PACK), 2)
+        weave_last_row_tile(896, 128)
         quantise_z(2)
-        multiply(2, range(PACK))
-        weave_last_row_tile(4 * run, run)
+        multiply(2, range(PACK), 2)
         quantise_z(3)
         multiply(3, range(PACK - 1))
-        weave_last_row_tile(5 * run, run)
-        weave_last_row_tile(6 * run, run)
+        weave_last_row_tile(starts[4], BANK)
+        weave_last_row_tile(starts[5], BANK)
         quantise_z(4)
-        weave_last_row_tile(7 * run, run)
-        multiply(3, (PACK - 1,), nc.vector.tensor_copy)
+        multiply(3, range(PACK - 1, PACK), 1, nc.vector.tensor_copy)
         multiply(4, range(PACK))
+        woven = {0: weave_y(0, full, "prev0", nc.vector.tensor_copy)}
         quantise_z(5)
-        woven = {quarter: weave_y(quarter, full, "prev%d" % quarter, nc.vector.tensor_copy) for quarter in (0, 1)}
         quantise_y(0, full, woven[0])
         store_words(0, BANK)
         multiply(5, range(PACK))
-        woven[2] = weave_y(2, full, "prev2", nc.vector.tensor_copy)
-        quantise_y(1, full, woven[1])
-        quantise_y(2, full, woven[2])
+        for quarter in (1, 2):
+            woven[quarter] = weave_y(quarter, full, "prev%d" % quarter, nc.vector.tensor_copy)
+        for quarter in (1, 2):
+            quantise_y(quarter, full, woven[quarter])
         store_words(BANK, 3 * BANK)
         by_scalar = weave_y(3, lower, "prev3", nc.scalar.copy)
         shared = tile("y_woven_last", [P, BANK // 2 * PACK], BF16, "gain1_0")

@@ -26,7 +26,7 @@ TINY = 2.0 ** -63
 OVERLAID = {
     "w3_raw": 0, "v2_words": 0, "v_words0": 4096,
     "page2": 8192, "w2_raw1": 12288, "first1": 16384, "factors": 20480, "first0": 28672,
-    "y2": 16384,
+    "y2": 0,
     "gain2_4": 32768, "w2_bf": 34816, "values5": 34304, "values6": 35328, "values7": 37376, "values8": 39424,
     "sizes0": 43008, "sizes1": 43008, "z_direct": 38912, "pairs": 47104,
     "shrink3": 55296, "shrink2": 59392, "z_paired": 55296,
@@ -41,7 +41,7 @@ PIECES = ((0, 0, 256), (1, 0, 384), (0, 256, 768), (1, 384, 1024), (2, 0, 512),
 AHEAD_OF_W2 = 4
 
 CHUNKS = (128, 128, 256, 512, 512, 512)
-STORES = (((0, 2), (2, 4)),) * 3 + (((0, 1), (1, 2), (2, 3), (3, 4)),) * 2 + (((0, 2), (2, 4)),)
+STORES = (((0, 2), (2, 4)),) * 3 + (((0, 1), (1, 2), (2, 3), (3, 4)),) + ((), ())
 SCALAR_RUN = slice(256, 640)
 
 
@@ -361,8 +361,9 @@ def tile_list_woven_tile_denoise_kernel(
         out_rows = out_0.rearrange("(p t) m -> p t m", t=PACK)
         out_words = out_1[0].rearrange("p m i -> p (m i)").bitcast(I32)
         starts = [sum(CHUNKS[:c]) for c in range(len(CHUNKS))]
-        y_tiles = [tile("y%d" % quarter, [P, PACK, BANK], F32, on)
-                   for quarter, on in enumerate(("tab2_w", "w2_raw0", None, "tab_w0"))]
+        y_tiles = [tile("y%d" % quarter, [P, PACK, BANK], F32, on)[:] for quarter, on in enumerate(("tab2_w", "w2_raw0"))]
+        upper_half = tile("y2", [P, PACK, 2 * BANK], F32)
+        y_tiles = y_tiles + [upper_half[:, :, cols] for cols in halves]
 
         def weave_last_row_tile(start, width):
             cols = slice(start, start + width)
@@ -438,25 +439,29 @@ def tile_list_woven_tile_denoise_kernel(
         weave_last_row_tile(starts[4], BANK)
         weave_last_row_tile(starts[5], BANK)
         quantise_z(4)
-        multiply(3, range(PACK - 1, PACK), 1, nc.vector.tensor_copy)
-        multiply(4, range(PACK))
-        woven = {0: weave_y(0, full, "prev0", nc.vector.tensor_copy)}
         quantise_z(5)
-        quantise_y(0, full, woven[0])
-        store_words(0, BANK)
-        multiply(5, range(PACK))
-        for quarter in (1, 2):
-            woven[quarter] = weave_y(quarter, full, "prev%d" % quarter, nc.vector.tensor_copy)
-        for quarter in (1, 2):
+        multiply(3, range(PACK - 1, PACK), 1, nc.vector.tensor_copy)
+
+        def upper_row_tile(t, copy):
+            multiply(4, range(t, t + 1))
+            multiply(5, range(t, t + 1), 1, copy)
+            nc.sync.dma_start(out_rows[:, t, 2 * BANK :], upper_half[:, t, :])
+
+        upper_row_tile(0, nc.scalar.copy)
+        upper_row_tile(1, nc.scalar.copy)
+        woven = {quarter: weave_y(quarter, full, "prev%d" % quarter, nc.vector.tensor_copy) for quarter in (0, 1)}
+        for quarter in (0, 1):
             quantise_y(quarter, full, woven[quarter])
-        store_words(BANK, 3 * BANK)
-        by_scalar = weave_y(3, lower, "prev3", nc.scalar.copy)
-        shared = tile("y_woven_last", [P, BANK // 2 * PACK], BF16, "gain1_0")
-        for within, copy in ((slice(0, P), nc.scalar.copy), (slice(P, 2 * P), nc.vector.tensor_copy)):
+        upper_row_tile(2, nc.scalar.copy)
+        store_words(0, 2 * BANK)
+        upper_row_tile(3, nc.vector.tensor_copy)
+        woven[2] = weave_y(2, full, "prev2", nc.vector.tensor_copy)
+        shared = tile("y_woven_last", [P, BANK * PACK], BF16, "prev3")
+        for within, copy in ((slice(0, 384), nc.scalar.copy), (slice(384, BANK), nc.vector.tensor_copy)):
             copy(shared[:, PACK * within.start : PACK * within.stop].rearrange("p (m i t) -> p m t i", i=4, t=PACK),
-                 y_tiles[3][:, :, upper.start + within.start : upper.start + within.stop].rearrange("p t (m i) -> p m t i", i=4))
-        quantise_y(3, lower, by_scalar)
-        store_words(3 * BANK, T2 - BANK // 2)
-        quantise_y(3, upper, shared)
-        store_words(T2 - BANK // 2, T2)
+                 y_tiles[3][:, :, within].rearrange("p t (m i) -> p m t i", i=4))
+        quantise_y(2, full, woven[2])
+        store_words(2 * BANK, 3 * BANK)
+        quantise_y(3, full, shared)
+        store_words(3 * BANK, T2)
         store_scales()

@@ -28,10 +28,10 @@ OVERLAID = {
     "page2": 8192, "w2_raw1": 12288, "first1": 16384, "factors": 20480, "first0": 28672,
     "y2": 0,
     "gain2_4": 32768, "w2_bf": 34816, "values5": 34304, "values6": 35328, "values7": 37376, "values8": 39424,
-    "sizes0": 43008, "sizes1": 43008, "z_direct": 38912, "pairs": 47104,
-    "shrink3": 55296, "shrink2": 59392, "z_paired": 55296,
+    "sizes0": 43008, "sizes1": 43008, "pairs": 36864, "z_direct": 49152,
+    "shrink3": 55296, "shrink2": 59392, "z_paired": 53248,
     "gain2_8": 63488, "gained": 63488,
-    "w4_dealt": 63488, "w4_dealt_scales": 65536,
+    "w4_dealt": 66048, "w4_dealt_scales": 65536,
     "logs": 69120, "first2": 69120, "first3": 73216, "w4_first": 69120,
     "gain2_3": 66560, "values4": 66560, "w1_later_scales": 68608,
 }
@@ -42,6 +42,8 @@ AHEAD_OF_W2 = 4
 
 CHUNKS = (128, 128, 256, 512, 512, 512)
 STORES = (((0, 2), (2, 4)),) * 3 + (((0, 1), (1, 2), (2, 3), (3, 4)),) + ((), ())
+DIRECT = 512
+PARTS, GROUP = 3, 64
 SCALAR_RUN = slice(256, 640)
 
 
@@ -313,22 +315,25 @@ def tile_list_woven_tile_denoise_kernel(
                 first_values(2 * pair, cols)
                 first_values(2 * pair + 1, cols)
 
-        half = T2 // 2
-        z_direct = tile("z_direct", [P, half, PACK], BF16)
-        z_paired = tile("z_paired", [P, half, PACK], BF16)
-        pairs = tile("pairs", [P, 2, half, 2], BF16)
+        z_direct = tile("z_direct", [P, DIRECT, PACK], BF16)
+        z_paired = tile("z_paired", [P, T2 - DIRECT, PACK], BF16)
+        part = (T2 - DIRECT) // PARTS
+        pairs = tile("pairs", [P, 2, PARTS, part, 2], BF16)
 
         def z_woven(cols):
-            if cols.start < half:
+            if cols.start < DIRECT:
                 return z_direct[:, cols, :]
-            return z_paired[:, cols.start - half : cols.stop - half, :]
+            return z_paired[:, cols.start - DIRECT : cols.stop - DIRECT, :]
+
+        def by_parts(t):
+            return page[t][:, DIRECT:].rearrange("p (g k i) -> p k g i", k=PARTS, i=GROUP)
 
         for t in range(2):
             place(t, list3, halves[0], first[t][:, halves[0]])
         for t in range(2):
             place(t, list3, halves[1], first[t][:, halves[1]])
-            nc.scalar.activation(pairs[:, 0, :, t], page[t][:, half:], ACT.Relu)
-            nc.scalar.activation(z_direct[:, :, t], page[t][:, :half], ACT.Relu)
+            nc.scalar.activation(pairs[:, 0, :, :, t].rearrange("p k (g i) -> p k g i", i=GROUP), by_parts(t), ACT.Relu)
+            nc.scalar.activation(z_direct[:, :, t], page[t][:, :DIRECT], ACT.Relu)
         w4_dealt = tile("w4_dealt", [P, PACK - 1, P], I32)
         nc.gpsimd.tensor_copy(w4_dealt[:], w4_raw[:].rearrange("p (m t) -> p t m", t=PACK)[:, 1:, :])
         w4_dealt_scales = tile("w4_dealt_scales", [P, N], U8)
@@ -337,15 +342,17 @@ def tile_list_woven_tile_denoise_kernel(
             w4_plane[:].rearrange("p (m t) -> p t m", t=PACK))
 
         place(2, list3, whole, first[2])
-        nc.scalar.activation(pairs[:, 1, :, :], page[2][:, half:].unsqueeze(2).to_broadcast([P, half, 2]), ACT.Relu)
-        nc.gpsimd.tensor_copy(
-            z_paired[:].rearrange("p m t -> p (m t)").bitcast(I32).rearrange("p (m h) -> p m h", h=2),
-            pairs[:].rearrange("p h m t -> p (h m t)").bitcast(I32).rearrange("p (h m) -> p m h", h=2))
+        woven_words = z_paired[:].rearrange("p m t -> p (m t)").bitcast(I32).rearrange(
+            "p (g k i h) -> p k g i h", k=PARTS, i=GROUP, h=2)
+        pair_words = pairs[:].rearrange("p h k m t -> p (h k m t)").bitcast(I32).rearrange(
+            "p (h k g i) -> p k g i h", h=2, k=PARTS, i=GROUP)
+        for k in range(PARTS):
+            nc.scalar.activation(pairs[:, 1, k].rearrange("p (g i) t -> p g i t", i=GROUP),
+                                 by_parts(2)[:, k].unsqueeze(3).to_broadcast([P, part // GROUP, GROUP, 2]), ACT.Relu)
+            nc.gpsimd.tensor_copy(woven_words[:, k], pair_words[:, k])
         w4_first = tile("w4_first", [P, P], U32)
-        for cols in halves:
-            nc.scalar.activation(z_direct[:, cols, 2:4], page[2][:, cols].unsqueeze(2).to_broadcast([P, BANK, 2]), ACT.Relu)
-            if cols.start == 0:
-                nc.scalar.copy(w4_first[:], w4_raw[:].bitcast(U32).rearrange("p (m t) -> p t m", t=PACK)[:, 0, :])
+        nc.scalar.copy(w4_first[:], w4_raw[:].bitcast(U32).rearrange("p (m t) -> p t m", t=PACK)[:, 0, :])
+        nc.scalar.activation(z_direct[:, :, 2:4], page[2][:, :DIRECT].unsqueeze(2).to_broadcast([P, DIRECT, 2]), ACT.Relu)
         w4_stationary = [w4_first[:]] + [w4_dealt[:, t, :] for t in range(PACK - 1)]
         for n in range(5):
             idle = bank("warm%d" % n, 3 + n)
@@ -408,7 +415,7 @@ def tile_list_woven_tile_denoise_kernel(
 
         def quantise_y(quarter, within, woven):
             cols = slice(BANK * quarter + within.start, BANK * quarter + within.stop)
-            nc.vector.quantize_mx(out=y_codes[:, cols].bitcast(FP8X4), scales=y_scales[4 * quarter :, within], in_=woven[:])
+            nc.vector.quantize_mx(out=y_codes[:, cols].bitcast(FP8X4), scales=y_scales[4 * quarter :, within], in_=woven[:, :])
 
         def store_words(start, stop):
             cols = slice(start, stop)
@@ -442,26 +449,34 @@ def tile_list_woven_tile_denoise_kernel(
         quantise_z(5)
         multiply(3, range(PACK - 1, PACK), 1, nc.vector.tensor_copy)
 
-        def upper_row_tile(t, copy):
-            multiply(4, range(t, t + 1))
-            multiply(5, range(t, t + 1), 1, copy)
+        def store_upper(t):
             nc.sync.dma_start(out_rows[:, t, 2 * BANK :], upper_half[:, t, :])
 
-        upper_row_tile(0, nc.scalar.copy)
-        upper_row_tile(1, nc.scalar.copy)
+        def upper_row_tile(t):
+            multiply(4, range(t, t + 1))
+            multiply(5, range(t, t + 1))
+            store_upper(t)
+
+        upper_row_tile(0)
+        upper_row_tile(1)
         woven = {quarter: weave_y(quarter, full, "prev%d" % quarter, nc.vector.tensor_copy) for quarter in (0, 1)}
-        for quarter in (0, 1):
-            quantise_y(quarter, full, woven[quarter])
-        upper_row_tile(2, nc.scalar.copy)
+        quantise_y(0, full, woven[0])
+        multiply(5, range(PACK - 1, PACK), 1, nc.vector.tensor_copy)
+        quantise_y(1, full, woven[1])
+        upper_row_tile(2)
         store_words(0, 2 * BANK)
-        upper_row_tile(3, nc.vector.tensor_copy)
+        multiply(4, range(PACK - 1, PACK))
+        store_upper(PACK - 1)
         woven[2] = weave_y(2, full, "prev2", nc.vector.tensor_copy)
-        shared = tile("y_woven_last", [P, BANK * PACK], BF16, "prev3")
-        for within, copy in ((slice(0, 384), nc.scalar.copy), (slice(384, BANK), nc.vector.tensor_copy)):
+        by_scalar = weave_y(3, lower, "prev3", nc.scalar.copy)
+        shared = tile("y_woven_last", [P, BANK // 2 * PACK], BF16, "gain1_0")
+        for within, copy in ((slice(0, P), nc.scalar.copy), (slice(P, 2 * P), nc.vector.tensor_copy)):
             copy(shared[:, PACK * within.start : PACK * within.stop].rearrange("p (m i t) -> p m t i", i=4, t=PACK),
-                 y_tiles[3][:, :, within].rearrange("p t (m i) -> p m t i", i=4))
-        quantise_y(2, full, woven[2])
+                 y_tiles[3][:, :, upper.start + within.start : upper.start + within.stop].rearrange("p t (m i) -> p m t i", i=4))
+        for within in (lower, upper):
+            quantise_y(2, within, woven[2][:, PACK * within.start : PACK * within.stop])
         store_words(2 * BANK, 3 * BANK)
-        quantise_y(3, full, shared)
+        quantise_y(3, lower, by_scalar)
+        quantise_y(3, upper, shared)
         store_words(3 * BANK, T2)
         store_scales()

@@ -41,7 +41,7 @@ PIECES = ((0, 0, 256), (1, 0, 384), (0, 256, 768), (1, 384, 1024), (2, 0, 512),
 AHEAD_OF_W2 = 4
 
 CHUNKS = (128, 128, 256, 512, 512, 512)
-STORES = (((0, 2), (2, 4)),) * 3 + (((0, 1), (1, 2), (2, 3), (3, 4)),) + ((), ())
+STORES = (((0, 1), (1, 2), (2, 4)),) + (((0, 2), (2, 4)),) * 2 + (((0, 1), (1, 2), (2, 3), (3, 4)),) + ((), ())
 DIRECT = 512
 PARTS, GROUP = 3, 64
 SCALAR_RUN = slice(256, 640)
@@ -143,7 +143,7 @@ def tile_list_woven_tile_denoise_kernel(
         w4_plane = zeroed_plane("w4_plane", N)
 
         list1 = load_list("list1", offs)
-        nc.sync.dma_start(tab_rows[0:32, :].bitcast(I32), tab_scales.rearrange("g q c -> (g q) c").bitcast(I32))
+        nc.scalar.dma_start(tab_rows[0:32, :].bitcast(I32), tab_scales.rearrange("g q c -> (g q) c").bitcast(I32))
         list2 = load_list("list2", offs2)
         for q in QUADRANTS:
             nc.sync.dma_start(tab2_rows[32 * q : 32 * q + 4, :].bitcast(I32),
@@ -434,7 +434,8 @@ def tile_list_woven_tile_denoise_kernel(
         weave_last_row_tile(starts[0], CHUNKS[0])
         weave_last_row_tile(starts[1], CHUNKS[1])
         quantise_z(0)
-        multiply(0, range(PACK), 2)
+        multiply(0, range(2))
+        multiply(0, range(2, PACK), 2)
         weave_last_row_tile(640, 256)
         quantise_z(1)
         multiply(1, range(PACK), 2)

from contextlib import ExitStack

import concourse.mybir as mybir

K, K2, T, S, T2, H, N = 1024, 512, 2048, 1024, 2048, 512, 512
FLOPS = 2 * S * H * (2 * K + K2) + 2 * T2 * H * N

F32 = mybir.dt.float32
BF16 = mybir.dt.bfloat16
I32 = mybir.dt.int32
U32 = mybir.dt.uint32
U16 = mybir.dt.uint16
U8 = mybir.dt.uint8
FP8X4 = mybir.dt.float8_e4m3fn_x4
FP4X4 = mybir.dt.float4_e2m1fn_x4
ALU = mybir.AluOpType
ACT = mybir.ActivationFunctionType

P = 128
PACK = 4
K_PASS = P * PACK
BANK = 512
QUADRANTS = (0, 2, 1, 3)
TINY = 2.0 ** -63

OVERLAID = {
    "w3_raw": 0, "v2_words": 0, "v_words0": 4096,
    "page2": 8192, "w2_raw1": 12288, "first1": 16384, "factors": 20480, "first0": 28672,
    "y2": 0,
    "gain2_4": 32768, "w2_bf": 34816, "values5": 34304, "values6": 35328, "values7": 37376, "values8": 39424,
    "sizes0": 43008, "sizes1": 43008, "pairs": 36864, "z_direct": 49152,
    "shrink3": 55296, "shrink2": 59392, "z_paired": 53248,
    "gain2_8": 63488, "gained": 63488,
    "w4_dealt": 66048, "w4_dealt_scales": 65536,
    "logs": 69120, "first2": 69120, "first3": 73216, "w4_first": 69120,
    "gain2_3": 66560, "values4": 66560, "w1_later_scales": 68608,
}

PIECES = ((0, 0, 256), (1, 0, 384), (0, 256, 768), (1, 384, 1024), (2, 0, 512),
          (0, 768, 1024), (3, 0, 512), (2, 512, 1024), (3, 512, 1024))
AHEAD_OF_W2 = 4

CHUNKS = (128, 128, 256, 512, 512, 512)
STORES = (((0, 1), (1, 2), (2, 4)),) + (((0, 2), (2, 4)),) * 2 + (((0, 1), (1, 2), (2, 3), (3, 4)),) + ((), ())
DIRECT = 512
PARTS, GROUP = 3, 64
SCALAR_RUN = slice(256, 640)


def tile_list_woven_tile_denoise_kernel(
    tc, tab_words, tab_scales, tab2_words, tab2_scales, offs, offs2, offs3, offs4,
    w1_words, w1_scales, w2, w3, w4_words, w4_scales, level, prev, wg1, wg2,
    out_0, out_1, out_2,
):
    nc = tc.nc
    with ExitStack() as ctx:
        lists = ctx.enter_context(tc.tile_pool(name="lists", bufs=1))
        keep = ctx.enter_context(tc.tile_pool(name="keep", bufs=1))
        overlay = ctx.enter_context(tc.tile_pool(name="overlay", bufs=1))
        psum = ctx.enter_context(tc.psum_pool(name="psum", bufs=1))

        halves = [slice(BANK * u, BANK * (u + 1)) for u in range(S // BANK)]
        whole = slice(0, S)

        def tile(name, shape, dtype, on=None):
            if name in OVERLAID:
                return overlay.tile(shape, dtype, name=name, align_bytes=64, offset=OVERLAID[name])
            return keep.tile(shape, dtype, name=name, tag=on or name, align_bytes=64)

        def bank(name, index):
            return psum.tile([P, BANK], F32, name=name, tag="bank%d" % index)

        def load_list(name, source):
            held = lists.tile([P, S // 16], U16, name=name)
            nc.sync.dma_start(held[:], source)
            return held

        def load_words(name, source):
            held = tile(name, [P, source.shape[1]], I32)
            nc.sync.dma_start(held[:], source.rearrange("p c i -> p (c i)").bitcast(I32))
            return held

        def zeroed_plane(name, width):
            plane = tile(name, [P, width], U8)
            nc.gpsimd.memset(plane[:].bitcast(I32), 0)
            return plane

        def load_weight(name, rows):
            raw = tile(name, [P, PACK, H], F32)
            nc.sync.dma_start(raw[:], rows.rearrange("(p i) c -> p i c", i=PACK))
            return raw

        earlier = [tile("prev%d" % t, [P, S], F32) for t in range(PACK)]
        gain1 = [tile("gain1_%d" % t, [P, S], F32) for t in range(PACK)]
        gain2 = {}

        def load_gain(held, rows):
            for q in QUADRANTS:
                nc.sync.dma_start(held[32 * q : 32 * q + 32], rows)

        def load_piece(n):
            t, start, stop = PIECES[n]
            nc.sync.dma_start(earlier[t][:, start:stop], prev.rearrange("(p t) j -> p t j", t=PACK)[:, t, start:stop])
            gain2[n] = tile("gain2_%d" % n, [P, stop - start], F32)
            load_gain(gain2[n][:], wg2.rearrange("(m t) j -> m t j", t=PACK)[:, t, start:stop])

        def gather(name, window, offsets, dtype, ranges=(whole,)):
            picked = tile(name, [P, S], dtype)
            for cols in ranges:
                nc.vector.tensor_copy(picked[:, cols], window.indirect(offsets[:, cols.start // 16 : cols.stop // 16]))
            return picked

        def scale_window(name):
            window = tile(name, [P, T], U8)
            nc.vector.memset(window[32:64, :].bitcast(I32), 0)
            nc.vector.memset(window[64:128, :].bitcast(I32), 0)
            return window

        def round_weight(name, passes):
            woven = tile(name + "_bf", [P, len(passes), H * PACK], BF16)
            for g, raw in enumerate(passes):
                dealt = woven[:, g, :].rearrange("p (t m i) -> p m t i", t=PACK, i=PACK)
                given = raw[:].rearrange("p i (m t) -> p m t i", t=PACK)
                if name == "w3":
                    nc.scalar.copy(dealt[:, :, 0:2], given[:, :, 0:2])
                    nc.gpsimd.tensor_scalar(dealt[:, :, 2:4], given[:, :, 2:4], 1.0, 0.0, ALU.mult, ALU.add)
                else:
                    nc.scalar.copy(dealt, given)
            return woven

        def quantise_weight(name, passes):
            woven = round_weight(name, passes)
            codes = tile(name + "_codes", [P, len(passes) * H], U32)
            scales = tile(name + "_scales", [P, len(passes) * H], U8)
            nc.vector.quantize_mx(out=codes[:].bitcast(FP8X4), scales=scales[:],
                                  in_=woven[:].rearrange("p g c -> p (g c)"))
            return codes, scales

        tab2_rows = zeroed_plane("tab2_rows", T)
        tab_rows = scale_window("tab_rows")
        w1_plane = zeroed_plane("w1_plane", 2 * H)
        v_scales = zeroed_plane("v_scales", 2 * S)
        w4_plane = zeroed_plane("w4_plane", N)

        list1 = load_list("list1", offs)
        nc.scalar.dma_start(tab_rows[0:32, :].bitcast(I32), tab_scales.rearrange("g q c -> (g q) c").bitcast(I32))
        list2 = load_list("list2", offs2)
        for q in QUADRANTS:
            nc.sync.dma_start(tab2_rows[32 * q : 32 * q + 4, :].bitcast(I32),
                              tab2_scales[0, 4 * q : 4 * q + 4, :].bitcast(I32))
        w3_raw = load_weight("w3_raw", w3)
        tab2_w = load_words("tab2_w", tab2_words[0])
        for q in QUADRANTS:
            nc.sync.dma_start(
                w1_plane[32 * q : 32 * q + 4, :].rearrange("p (g c) -> p g c", g=2).bitcast(I32),
                w1_scales[:, 4 * q : 4 * q + 4, :].rearrange("g r c -> r g c").bitcast(I32))
        tab_w = [load_words("tab_w0", tab_words[0])]
        load_piece(0)
        list4 = load_list("list4", offs4)
        tab_w.append(load_words("tab_w1", tab_words[1]))
        load_piece(1)
        load_piece(2)
        level_t = tile("level_t", [P, PACK], F32)
        nc.sync.dma_start(level_t[:], level.rearrange("(p t) -> p t", t=PACK))

        log_level = tile("log_level", [P, PACK], F32)
        nc.scalar.activation(log_level[:], level_t[:], ACT.Ln)
        neg_log_level = tile("neg_log_level", [P, PACK], F32)
        nc.scalar.mul(neg_log_level[:], log_level[:], -1.0)

        v_rows = gather("v_rows", tab_rows[:], list1, U8)
        v2_scales = gather("v2_scales", tab2_rows[:], list2, U8)
        w3_codes, w3_scales = quantise_weight("w3", [w3_raw])
        w1_dealt_scales = tile("w1_dealt_scales", [P, H], U8, "w3_bf")

        def deal_w1_scales(held, g):
            nc.gpsimd.tensor_copy(held.rearrange("p (t m) -> p t m", t=PACK),
                                  w1_plane[:, H * g : H * (g + 1)].rearrange("p (m t) -> p t m", t=PACK))

        deal_w1_scales(w1_dealt_scales[:], 0)
        v2_words = gather("v2_words", tab2_w[:].bitcast(U32), list2, U32, halves)
        v_words = [gather("v_words0", tab_w[0][:].bitcast(U32), list1, U32)]

        def seat_scales(g):
            for q in range(4):
                start = 16 * g + 4 * q
                nc.sync.dma_start(v_scales[32 * q : 32 * q + 4, S * g : S * (g + 1)].bitcast(I32),
                                  v_rows[start : start + 4, :].bitcast(I32))

        load_piece(3)
        w2_raw = [load_weight("w2_raw0", w2[:K_PASS, :])]
        w1_raw = tile("w1_raw", [P, 2, 2 * H], U8)
        nc.sync.dma_start(w1_raw[:].bitcast(I32), w1_words.rearrange("g p c -> p g c").bitcast(I32))
        seat_scales(0)
        w2_raw.append(load_weight("w2_raw1", w2[K_PASS:, :]))
        seat_scales(1)
        for n in (4, 5, 6):
            load_piece(n)
        list3 = load_list("list3", offs3)
        load_piece(7)
        load_piece(8)
        for t in range(PACK):
            load_gain(gain1[t][:], wg1.rearrange("(m t) j -> m t j", t=PACK)[:, t, :])
            if t == 1:
                w4_raw = load_words("w4_raw", w4_words[0])
                for q in range(4):
                    nc.sync.dma_start(w4_plane[32 * q : 32 * q + 4, :].bitcast(I32),
                                      w4_scales[0, 4 * q : 4 * q + 4, :].bitcast(I32))

        page, second, logged, shrink = {}, {}, {}, {}

        def second_product(t, u):
            rows = slice(P * t, P * (t + 1))
            if t not in second:
                second[t] = tile("second%d" % t, [P, S], F32)
            acc = bank("c_%d_%d" % (t, u), 2 * t + u)
            cols = halves[u]
            nc.tensor.matmul_mx(out=acc[:], lhsT=w3_codes[:, rows].bitcast(FP8X4), lhsT_scale=w3_scales[:, rows],
                                rhs=v2_words[:, cols].bitcast(FP8X4), rhs_scale=v2_scales[:, cols],
                                start=True, stop=True)
            return acc

        def second_values(n):
            t, start, stop = PIECES[n]
            values = tile("values%d" % n, [P, stop - start], F32, "gain2_%d" % (n - 1) if n else None)
            nc.gpsimd.tensor_tensor(values[:], second[t][:, start:stop], earlier[t][:, start:stop], ALU.add)
            nc.gpsimd.tensor_tensor(values[:], values[:], gain2[n][:], ALU.mult)
            return values[:]

        def place(t, offsets, cols, values):
            if t not in page:
                page[t] = tile("page%d" % t, [P, T2], F32, ("tab2_w", "tab_w0", None, "tab_w1")[t])
            nc.vector.tensor_copy(page[t][:].indirect(offsets[:, cols.start // 16 : cols.stop // 16]), values)

        def place_second(n, values):
            t, start, stop = PIECES[n]
            place(t, list4, slice(start, stop), values)

        sums = {(t, u): second_product(t, u) for u in range(2) for t in range(PACK)}
        lead = PIECES[0][2]
        nc.scalar.copy(second[0][:, :lead], sums[0, 0][:, :lead])
        nc.scalar.copy(second[1][:, halves[0]], sums[1, 0][:])
        nc.scalar.copy(second[0][:, lead:BANK], sums[0, 0][:, lead:])
        for t, u in ((0, 1), (1, 1), (2, 0), (3, 0), (2, 1), (3, 1)):
            nc.scalar.copy(second[t][:, halves[u]], sums[t, u][:])
        place_second(0, second_values(0))
        v_words.append(gather("v_words1", tab_w[1][:].bitcast(U32), list1, U32))
        for n in range(1, AHEAD_OF_W2):
            place_second(n, second_values(n))
        w1_dealt = tile("w1_dealt", [P, 2, 2 * H], U8)
        later_scales = tile("w1_later_scales", [P, H], U8)
        deal_w1_scales(later_scales[:], 1)
        nc.scalar.copy(
            w1_dealt[:].bitcast(U16).rearrange("p g (t m) -> p g t m", t=PACK),
            w1_raw[:].bitcast(U16).rearrange("p g (m t) -> p g t m", t=PACK))
        w2_codes, w2_scales = quantise_weight("w2", w2_raw)
        first = {t: tile("first%d" % t, [P, S], F32)[:] for t in range(2)}
        for n in range(AHEAD_OF_W2, len(PIECES)):
            place_second(n, second_values(n))

        def first_product(t):
            for u, cols in enumerate(halves):
                acc = bank("a_%d_%d" % (t, u), 2 * t + u)
                for g in range(2):
                    nc.tensor.matmul_mx(
                        out=acc[:], lhsT=w1_dealt[:, g, 2 * P * t : 2 * P * (t + 1)].bitcast(FP4X4),
                        lhsT_scale=(w1_dealt_scales, later_scales)[g][:, P * t : P * (t + 1)],
                        rhs=v_words[g][:, cols].bitcast(FP8X4),
                        rhs_scale=v_scales[:, S * g + cols.start : S * g + cols.stop],
                        start=(g == 0), stop=(g == 1))
                nc.scalar.copy(first[t][:, cols], acc[:])

        def log_magnitudes(pair):
            sizes = tile("sizes%d" % pair, [P, 2, S], F32)
            for t in (2 * pair, 2 * pair + 1):
                for u, cols in enumerate(halves):
                    acc = bank("b_%d_%d" % (t, u), (2 * t + u + 4) % 8)
                    for g in range(2):
                        rows = slice(H * g + P * t, H * g + P * (t + 1))
                        nc.tensor.matmul_mx(
                            out=acc[:], lhsT=w2_codes[:, rows].bitcast(FP8X4), lhsT_scale=w2_scales[:, rows],
                            rhs=v_words[g][:, cols].bitcast(FP8X4),
                            rhs_scale=v_scales[:, S * g + cols.start : S * g + cols.stop],
                            start=(g == 0), stop=(g == 1))
                    nc.scalar.activation(sizes[:, t % 2, cols], acc[:], ACT.Abs)
            if pair == 0:
                logs = tile("logs", [P, 2, S], F32)
                nc.scalar.activation(logs[:], sizes[:], ACT.Ln, bias=TINY)
                factors = tile("factors", [P, 2, S], F32)
                for t in (0, 1):
                    logged[t], shrink[t] = logs[:, t, :], factors[:, t, :]
            else:
                for t in (2, 3):
                    logged[t] = shrink[t] = tile("shrink%d" % t, [P, S], F32)[:]
                    nc.scalar.activation(shrink[t], sizes[:, t % 2, :], ACT.Ln, bias=TINY)

        def factor(t):
            nc.scalar.activation(shrink[t], logged[t], ACT.Sigmoid, bias=neg_log_level[:, t : t + 1], scale=2.0)

        def first_values(t, cols):
            gained = tile("gained", [P, cols.stop - cols.start], F32)
            nc.gpsimd.tensor_tensor(gained[:], first[t][:, cols], gain1[t][:, cols], ALU.mult)
            nc.gpsimd.tensor_tensor(first[t][:, cols], gained[:], shrink[t][:, cols], ALU.mult)

        for pair in range(2):
            if pair:
                for t in (2, 3):
                    first[t] = tile("first%d" % t, [P, S], F32)[:]
            first_product(2 * pair)
            first_product(2 * pair + 1)
            log_magnitudes(pair)
            factor(2 * pair)
            factor(2 * pair + 1)
            for cols in ([whole] if pair else halves):
                first_values(2 * pair, cols)
                first_values(2 * pair + 1, cols)

        z_direct = tile("z_direct", [P, DIRECT, PACK], BF16)
        z_paired = tile("z_paired", [P, T2 - DIRECT, PACK], BF16)
        part = (T2 - DIRECT) // PARTS
        pairs = tile("pairs", [P, 2, PARTS, part, 2], BF16)

        def z_woven(cols):
            if cols.start < DIRECT:
                return z_direct[:, cols, :]
            return z_paired[:, cols.start - DIRECT : cols.stop - DIRECT, :]

        def by_parts(t):
            return page[t][:, DIRECT:].rearrange("p (g k i) -> p k g i", k=PARTS, i=GROUP)

        for t in range(2):
            place(t, list3, halves[0], first[t][:, halves[0]])
        for t in range(2):
            place(t, list3, halves[1], first[t][:, halves[1]])
            nc.scalar.activation(pairs[:, 0, :, :, t].rearrange("p k (g i) -> p k g i", i=GROUP), by_parts(t), ACT.Relu)
            nc.scalar.activation(z_direct[:, :, t], page[t][:, :DIRECT], ACT.Relu)
        w4_dealt = tile("w4_dealt", [P, PACK - 1, P], I32)
        nc.gpsimd.tensor_copy(w4_dealt[:], w4_raw[:].rearrange("p (m t) -> p t m", t=PACK)[:, 1:, :])
        w4_dealt_scales = tile("w4_dealt_scales", [P, N], U8)
        nc.gpsimd.tensor_copy(
            w4_dealt_scales[:].rearrange("p (t m) -> p t m", t=PACK),
            w4_plane[:].rearrange("p (m t) -> p t m", t=PACK))

        place(2, list3, whole, first[2])
        woven_words = z_paired[:].rearrange("p m t -> p (m t)").bitcast(I32).rearrange(
            "p (g k i h) -> p k g i h", k=PARTS, i=GROUP, h=2)
        pair_words = pairs[:].rearrange("p h k m t -> p (h k m t)").bitcast(I32).rearrange(
            "p (h k g i) -> p k g i h", h=2, k=PARTS, i=GROUP)
        for k in range(PARTS):
            nc.scalar.activation(pairs[:, 1, k].rearrange("p (g i) t -> p g i t", i=GROUP),
                                 by_parts(2)[:, k].unsqueeze(3).to_broadcast([P, part // GROUP, GROUP, 2]), ACT.Relu)
            nc.gpsimd.tensor_copy(woven_words[:, k], pair_words[:, k])
        w4_first = tile("w4_first", [P, P], U32)
        nc.scalar.copy(w4_first[:], w4_raw[:].bitcast(U32).rearrange("p (m t) -> p t m", t=PACK)[:, 0, :])
        nc.scalar.activation(z_direct[:, :, 2:4], page[2][:, :DIRECT].unsqueeze(2).to_broadcast([P, DIRECT, 2]), ACT.Relu)
        w4_stationary = [w4_first[:]] + [w4_dealt[:, t, :] for t in range(PACK - 1)]
        for n in range(5):
            idle = bank("warm%d" % n, 3 + n)
            nc.tensor.matmul_mx(out=idle[:], lhsT=w4_first[:].bitcast(FP8X4), lhsT_scale=w4_dealt_scales[:, :P],
                                rhs=w3_codes[:].bitcast(FP8X4), rhs_scale=w3_scales[:], start=True, stop=True)

        place(3, list3, whole, first[3])

        z_codes = tile("z_codes", [P, T2], U32)
        z_scales = tile("z_scales", [P, T2], U8)
        y_codes = tile("y_codes", [P, T2], I32)
        y_scales = tile("y_scales", [P, BANK], U8)
        out_rows = out_0.rearrange("(p t) m -> p t m", t=PACK)
        out_words = out_1[0].rearrange("p m i -> p (m i)").bitcast(I32)
        starts = [sum(CHUNKS[:c]) for c in range(len(CHUNKS))]
        y_tiles = [tile("y%d" % quarter, [P, PACK, BANK], F32, on)[:] for quarter, on in enumerate(("tab2_w", "w2_raw0"))]
        upper_half = tile("y2", [P, PACK, 2 * BANK], F32)
        y_tiles = y_tiles + [upper_half[:, :, cols] for cols in halves]

        def weave_last_row_tile(start, width):
            cols = slice(start, start + width)
            if SCALAR_RUN.start <= start < SCALAR_RUN.stop:
                nc.scalar.activation(z_woven(cols)[:, :, PACK - 1], page[PACK - 1][:, cols], ACT.Relu)
            else:
                nc.vector.tensor_scalar_max(z_woven(cols)[:, :, PACK - 1], page[PACK - 1][:, cols], 0.0)

        def quantise_z(c):
            cols = slice(starts[c], starts[c] + CHUNKS[c])
            nc.vector.quantize_mx(out=z_codes[:, cols].bitcast(FP8X4), scales=z_scales[:, cols],
                                  in_=z_woven(cols).rearrange("p m t -> p (m t)"))

        banks_used = []

        def multiply(c, row_tiles, together=1, copy=nc.scalar.copy):
            width = CHUNKS[c]
            cols = slice(starts[c], starts[c] + width)
            y = y_tiles[cols.start // BANK][:, :, cols.start % BANK : cols.start % BANK + width]
            for first_tile in row_tiles[::together]:
                acc = bank("y_%d_%d" % (c, first_tile), len(banks_used) % 8)
                banks_used.append(acc)
                for t in range(first_tile, first_tile + together):
                    rows = slice(P * t, P * (t + 1))
                    place_in_bank = slice(width * (t - first_tile), width * (t - first_tile + 1))
                    nc.tensor.matmul_mx(out=acc[:, place_in_bank], lhsT=w4_stationary[t].bitcast(FP8X4),
                                        lhsT_scale=w4_dealt_scales[:, rows],
                                        rhs=z_codes[:, cols].bitcast(FP8X4), rhs_scale=z_scales[:, cols],
                                        start=True, stop=True)
                copy(y[:, first_tile : first_tile + together, :],
                     acc[:, : together * width].rearrange("p (t c) -> p t c", t=together))
                for first_row, end in STORES[c]:
                    if first_tile + together == end:
                        nc.sync.dma_start(out_rows[:, first_row:end, cols], y[:, first_row:end, :])

        def weave_y(quarter, within, on, copy):
            woven = tile("y_woven%d_%d" % (quarter, within.start), [P, (within.stop - within.start) * PACK], BF16, on)
            copy(
                woven[:].rearrange("p (m i t) -> p m t i", i=4, t=PACK),
                y_tiles[quarter][:, :, within].rearrange("p t (m i) -> p m t i", i=4))
            return woven

        def quantise_y(quarter, within, woven):
            cols = slice(BANK * quarter + within.start, BANK * quarter + within.stop)
            nc.vector.quantize_mx(out=y_codes[:, cols].bitcast(FP8X4), scales=y_scales[4 * quarter :, within], in_=woven[:, :])

        def store_words(start, stop):
            cols = slice(start, stop)
            nc.sync.dma_start(out_words[:, cols], y_codes[:, cols])

        def store_scales():
            for q in range(4):
                (nc.scalar, nc.sync)[q % 2].dma_start(
                    out_2[0, 4 * q : 4 * q + 4, :].rearrange("r (j c) -> j r c", j=4).bitcast(I32),
                    y_scales[32 * q : 32 * q + 16, :].bitcast(I32))

        full, lower, upper = slice(0, BANK), slice(0, BANK // 2), slice(BANK // 2, BANK)
        run = BANK // 2
        weave_last_row_tile(starts[2], CHUNKS[2])
        weave_last_row_tile(starts[3], SCALAR_RUN.stop - starts[3])
        weave_last_row_tile(starts[0], CHUNKS[0])
        weave_last_row_tile(starts[1], CHUNKS[1])
        quantise_z(0)
        multiply(0, range(2))
        multiply(0, range(2, PACK), 2)
        weave_last_row_tile(640, 256)
        quantise_z(1)
        multiply(1, range(PACK), 2)
        weave_last_row_tile(896, 128)
        quantise_z(2)
        multiply(2, range(PACK), 2)
        quantise_z(3)
        multiply(3, range(PACK - 1))
        weave_last_row_tile(starts[4], BANK)
        weave_last_row_tile(starts[5], BANK)
        quantise_z(4)
        quantise_z(5)
        multiply(3, range(PACK - 1, PACK), 1, nc.vector.tensor_copy)

        def store_upper(t):
            nc.sync.dma_start(out_rows[:, t, 2 * BANK :], upper_half[:, t, :])

        def upper_row_tile(t):
            multiply(4, range(t, t + 1))
            multiply(5, range(t, t + 1))
            store_upper(t)

        upper_row_tile(0)
        upper_row_tile(1)
        woven = {quarter: weave_y(quarter, full, "prev%d" % quarter, nc.vector.tensor_copy) for quarter in (0, 1)}
        quantise_y(0, full, woven[0])
        multiply(5, range(PACK - 1, PACK), 1, nc.vector.tensor_copy)
        quantise_y(1, full, woven[1])
        upper_row_tile(2)
        store_words(0, 2 * BANK)
        multiply(4, range(PACK - 1, PACK))
        store_upper(PACK - 1)
        woven[2] = weave_y(2, full, "prev2", nc.vector.tensor_copy)
        by_scalar = weave_y(3, lower, "prev3", nc.scalar.copy)
        shared = tile("y_woven_last", [P, BANK // 2 * PACK], BF16, "gain1_0")
        for within, copy in ((slice(0, P), nc.scalar.copy), (slice(P, 2 * P), nc.vector.tensor_copy)):
            copy(shared[:, PACK * within.start : PACK * within.stop].rearrange("p (m i t) -> p m t i", i=4, t=PACK),
                 y_tiles[3][:, :, upper.start + within.start : upper.start + within.stop].rearrange("p t (m i) -> p m t i", i=4))
        for within in (lower, upper):
            quantise_y(2, within, woven[2][:, PACK * within.start : PACK * within.stop])
        store_words(2 * BANK, 3 * BANK)
        quantise_y(3, lower, by_scalar)
        quantise_y(3, upper, shared)
        store_words(3 * BANK, T2)
        store_scales()
